import numpy as np, ml_dtypes
CORES = [36,164,52,180,100,228,116,244]
N = 8
BF = ml_dtypes.bfloat16
W, C, B, VI, S = 3072, 2048, 128, 3, 5
def parts(rng):
    rt = rng.integers(0, 16, (N, 8, 16, W)); pf = rng.integers(0, W, (N, 8, 16, C))
    jc = np.argsort(rng.random((N, 8, C)), axis=-1)[..., :16 * B].reshape(N, 8, 16, B)
    return rt, pf, jc, rng.integers(0, 16, (N, 8, 16, B)), rng.integers(0, 16, (N, 8, B))
def pack(rt, pf, jc, fx, sr):
    return {"rt": np.ascontiguousarray(rt.reshape(N, 128, W)).astype(np.float32).astype(BF),
            "pk": np.ascontiguousarray((pf[..., :C // 2] + 4096 * pf[..., C // 2:]).reshape(N, 128, C // 2)).astype(np.int32),
            "jc": np.ascontiguousarray(jc.reshape(N, 128, B)).astype(np.int32),
            "fx": np.ascontiguousarray(fx.reshape(N, 128, B)).astype(np.float32).astype(BF), "sr": np.ascontiguousarray(sr).astype(np.int32)}
def setup_inputs(rng):
    return pack(*parts(rng))
def setup_inputs_ties(rng):
    rt, pf, jc, fx, sr = parts(rng)
    pool = rng.integers(0, 16, (N, 8, 16, 8)); pool[:, 1::2] = rng.integers(0, 2, (N, 4, 16, 8))
    rt = np.take_along_axis(pool, rng.integers(0, 8, (N, 8, 1, W)), 3)
    fx = np.where(rng.random((N, 8, 1, B)) < 0.5, np.take_along_axis(pool, rng.integers(0, 8, (N, 8, 1, B)), 3), fx)
    q = rng.permutation(C)[:C // 8]; pf[..., q] = pf[:, :, :1, q]
    return pack(rt, pf, jc, fx, sr)
def setup_inputs_rounds(rng):
    rt, pf, jc, fx, sr = parts(rng); h = W // 2
    o = np.argsort(rng.random((N, 8, W)), axis=-1); light = np.zeros((N, 8, W), bool); np.put_along_axis(light, o[..., :h], True, 2)
    rt = np.where(light[:, :, None, :], rng.integers(0, 2, (N, 8, 16, W)), rng.integers(8, 16, (N, 8, 16, W)))
    ln = rng.integers(1, S + 2, (8, B)); back = (rng.random((8, B)) * ln).astype(np.int64)
    ln[0] = S; back[0] = 0; ln[1] = S + 1; ln[2] = 1; back[2] = 0
    if np.count_nonzero(ln <= S) % 2 == 0:
        ln[3, 0] = S + 1 if ln[3, 0] <= S else S; back[3, 0] = 0
    s0 = rng.integers(0, 16, (8, B)); a = (np.arange(16)[None, :, None] - s0[:, None, :]) % 16
    nxt = (np.where(a == ln[:, None, :] - 1, back[:, None, :], a + 1) + s0[:, None, :]) % 16
    pc = np.argsort(rng.random((8, C)), axis=-1)[:, :16 * B]
    kap = rng.integers(0, 16, (8, C)); np.put_along_axis(kap, pc, nxt.reshape(8, 16 * B), 1)
    one = kap[None, :, None, :] == np.arange(16)[None, None, :, None]
    pf = np.take_along_axis(o[:, :, None, :], rng.integers(0, h, (N, 8, 16, C)) + np.where(one, 0, h), 3)
    e = np.argsort(rng.random((N, 8, B)), axis=-1)
    jc = np.take_along_axis(np.broadcast_to(pc.reshape(1, 8, 16, B), (N, 8, 16, B)), np.broadcast_to(e[:, :, None, :], (N, 8, 16, B)), 3)
    sr = np.take_along_axis(np.broadcast_to(s0[None], (N, 8, B)), e, 2)
    return pack(rt, pf, jc, rng.integers(0, 2, (N, 8, 16, B)), sr)
def setup_inputs_full(rng):
    h = W // 2; u = h // 2; rows = np.arange(16)
    side = (np.arange(N)[:, None] + np.arange(8)[None, :]) % 2 * h
    o = np.argsort(rng.random((N, 8, h)), axis=-1) + side[:, :, None]; light = np.zeros((N, 8, W), bool); np.put_along_axis(light, o[..., :u], True, 2)
    rt = np.where(light[:, :, None, :], rng.integers(0, 2, (N, 8, 16, W)), rng.integers(8, 16, (N, 8, 16, W)))
    s0 = 2 * rng.permutation(8) + rng.integers(0, 2, 8); a = (rows[None, :] - s0[:, None]) % 16
    nxt = (np.where(a == S - 1, 0, a + 1) + s0[:, None]) % 16
    lower = np.argsort(rng.random((8, C // 2)), axis=-1)[:, :8 * B]; upper = np.argsort(rng.random((8, C // 2)), axis=-1)[:, :8 * B] + C // 2
    pc = np.concatenate([lower, upper], axis=1).reshape(8, 16, B)
    kap = rng.integers(0, 16, (N, 8, C))
    np.put_along_axis(kap, np.broadcast_to(pc.reshape(1, 8, 16 * B), (N, 8, 16 * B)), np.broadcast_to(np.repeat(nxt, B, axis=1)[None], (N, 8, 16 * B)), 2)
    whole = int(rng.integers(0, 8))
    for g in range(8):
        if g != whole: kap[1::2, g, int(pc[g, (s0[g] + S - 1) % 16, 0])] = (s0[g] + S) % 16
    one = kap[:, :, None, :] == rows[None, None, :, None]
    pf = np.take_along_axis(o[:, :, None, :], rng.integers(0, u, (N, 8, 16, C)) + np.where(one, 0, u), 3)
    e = np.argsort(rng.random((N, 8, 16, B)), axis=-1)
    jc = np.take_along_axis(np.broadcast_to(pc[None], (N, 8, 16, B)), e, 3)
    return pack(rt, pf, jc, rng.integers(0, 2, (N, 8, 16, B)), np.broadcast_to(s0[None, :, None], (N, 8, B)))
def setup_inputs_ends(rng):
    rt, pf, jc, fx, sr = parts(rng)
    pf[:, ::2] = rng.choice(np.array([0, 1, W // 2, W - 1]), (N, 4, 16, C)); pf[:, 1::2, :, C // 2 - 1] = W - 1; pf[:, 1::2, :, C - 1] = W - 1
    jc[:, ::2] = np.concatenate([np.arange(8 * B), np.arange(C - 8 * B, C)]).reshape(16, B)
    rt[:, 1::2] = 15 * rng.integers(0, 2, (N, 4, 16, W)); fx = 15 * rng.integers(0, 2, (N, 8, 16, B)); sr = 15 * rng.integers(0, 2, (N, 8, B))
    o = rng.permutation(W); n = B // 2; hi = o[:W // 4]; mid = o[W // 4:W // 2]; lo = o[W // 2:3 * W // 4]
    rt[:, 1][:, :, hi] = 15; rt[:, 1][:, :, mid] = 14; rt[:, 1][:, :, lo] = 0
    for q in range(N):
        x = rng.permutation(B)[:n]; p = np.argsort(rng.random((16, n)), axis=0)[:3]; c = jc[q, 1, p, x]
        for i, k, a, b in ((0, p[1], mid, hi), (1, p[2], hi, lo), (2, p[1], lo, hi)):
            pf[q, 1][:, c[i]] = rng.choice(b, (16, n)); pf[q, 1][k, c[i]] = rng.choice(a, n)
        fx[q, 1][:, x] = 0; sr[q, 1][x] = p[0]
    return pack(rt, pf, jc, fx, sr)
def setup_inputs_spread(rng):
    rt, pf, jc, fx, sr = parts(rng)
    rt = np.minimum((16 * rng.random((N, 8, 16, W)) ** np.exp2(rng.integers(-2, 4, (N, 8, 1, W)))).astype(np.int64), 15)
    pf = np.minimum((W * rng.random((N, 8, 16, C)) ** np.exp2(rng.integers(-2, 4, (N, 8, 1, C)))).astype(np.int64), W - 1)
    fx = np.minimum((16 * rng.random((N, 8, 16, B)) ** np.exp2(rng.integers(-2, 4, (N, 8, 1, B)))).astype(np.int64), 15)
    sr = np.minimum((16 * rng.random((N, 8, B)) ** np.exp2(rng.integers(-1, 3, (N, 8, 1)))).astype(np.int64), 15)
    return pack(rt, pf, jc, fx, sr)
def check_inputs(d):
    bad = []
    for k in ("rt", "fx"):
        a = np.asarray(d[k]).astype(np.float32)
        if not np.all((a >= 0) & (a <= 15) & (a == np.floor(a))): bad.append("whole numbers of " + k)
    a = np.asarray(d["pk"]).astype(np.int64)
    if np.min(a) < 0 or np.max(a & 4095) >= W or np.max(a >> 12) >= W: bad.append("range of pk")
    for k, hi in (("jc", C - 1), ("sr", 15)):
        if np.min(d[k]) < 0 or np.max(d[k]) > hi: bad.append("range of " + k)
    s = np.sort(np.asarray(d["jc"]).reshape(N, 8, 16 * B), axis=-1)
    if np.any(s[..., 1:] == s[..., :-1]): bad.append("courts of a group differ")
    return bad
def reference(rt, pk, jc, fx, sr):
    R = rt.astype(np.float32).astype(np.int32).reshape(N, 8, 16, W); f = fx.astype(np.float32).astype(np.int32).reshape(N, 8, 16, B)
    two = pk.astype(np.int32).reshape(N, 8, 16, C // 2); pf = np.concatenate([two & 4095, two >> 12], axis=3)
    J = jc.astype(np.int32).reshape(N, 8, 16, B); start = sr.astype(np.int32); Z = np.zeros(N, np.int32); rows = np.arange(16, dtype=np.int32)
    for t in range(VI):
        if t > 0:
            f = np.roll(f, 1, axis=0); J = np.roll(J, 1, axis=0); start = np.roll(start, 1, axis=0)
        m = np.zeros((N, 8, 16, B), np.int32); v = np.zeros((N, 8, 16, B), np.int32); num = np.zeros((N, 8, 16, B), np.int32)
        p = start; go = np.ones((N, 8, B), bool); first = np.zeros((N, 8, B), np.int32); new = np.zeros((N, 8, B), np.int32)
        for s in range(1, S + 1):
            c = np.take_along_axis(J, p[:, :, None, :], 2)
            n = np.take_along_axis(pf, np.broadcast_to(c, (N, 8, 16, B)), 3)
            x = np.take_along_axis(R, np.broadcast_to(n.reshape(N, 8, 1, 16 * B), (N, 8, 16, 16 * B)), 3).reshape(N, 8, 16, 16, B)
            dist = np.add.reduce(np.abs(x - f[:, :, :, None, :]), axis=2)
            k = np.argmin(dist, axis=2).astype(np.int32)
            kk = k[:, :, None, :]; nk = np.take_along_axis(n, kk, 2)
            rule = np.take_along_axis(R, np.broadcast_to(nk, (N, 8, 16, B)), 3)
            here = (rows[None, None, :, None] == p[:, :, None, :]) & go[:, :, None, :]
            v = np.where(here, kk, v); num = np.where(here, nk, num); m = np.where(here, np.int32(s), m)
            f = np.where(go[:, :, None, :], np.abs(f - rule), f)
            mk = np.take_along_axis(m, kk, 2)[:, :, 0]; nr = np.take_along_axis(num, kk, 2)
            shut = go & (mk > 0)
            tot = np.add.reduce(np.take_along_axis(R, np.broadcast_to(nr, (N, 8, 16, B)), 3), axis=2)
            odd = ((tot + Z[:, None, None]) & 1) == 1
            new = np.where(shut, np.where(odd, nk[:, :, 0], nr[:, :, 0]), new); first = np.where(shut, mk, first)
            go = go & ~shut; p = np.where(go, k, p)
        closed = first > 0
        loop = closed[:, :, None, :] & (m >= first[:, :, None, :])
        at = np.broadcast_to(J.reshape(N, 8, 1, 16 * B), (N, 8, 16, 16 * B))
        old = np.take_along_axis(pf, at, 3).reshape(N, 8, 16, 16, B)
        hit = loop[:, :, None] & (v[:, :, None] == rows[None, None, :, None, None])
        np.put_along_axis(pf, at, np.where(hit, new[:, :, None, None, :], old).reshape(N, 8, 16, 16 * B), 3)
        Z = Z + np.add.reduce(closed.astype(np.int32), axis=(1, 2))
    return {"yp": (pf[..., :C // 2] + 4096 * pf[..., C // 2:]).reshape(N, 128, C // 2).astype(np.float32), "yf": f.reshape(N, 128, B).astype(np.float32).astype(BF)}

@@ -1,0 +1,444 @@
+from concourse.mybir import AluOpType, AxisListType, ActivationFunctionType
+
+A = AluOpType
+AF = ActivationFunctionType
+VI, S = 3, 5
+NDUM = 640
+SCRATCH = {}
+for _n, _s, _d in (
+        ("pkt tmpi", [128, 1024], "int32"), ("rtt", [128, 3072], "bfloat16"), ("tab", [128, 2048 + NDUM], "float32"),
+        ("jci jh jl", [128, 128], "int32"), ("sri", [8, 128], "int32"), ("srb bo8", [8, 128], "bfloat16"),
+        ("fin0 fin1 fin2 fout oneb idb idn jhb jlb oh", [128, 128], "bfloat16"), ("fw0 fw1 fw2", [128, 272], "bfloat16"),
+        ("pi yli", [128, 1], "int32"), ("ylf y16 q2k zr zc", [128, 1], "float32"),
+        ("io32", [128, 32], "int32"), ("w1 w1c la lb lc", [128, 32], "float32"), ("lists", [128, 32], "uint16"),
+        ("onef bof bon edec", [128, 128], "float32"), ("sel", [128, 16, 128], "bfloat16"),
+        ("sk", [128, 8], "int32"), ("fbi fb fs", [128, 8], "float32"),
+        ("jji q6 q8", [128, 4], "int32"), ("jj q6f q8f", [128, 4], "float32"),
+        ("km", [128, 64], "float32"), ("fmask fsp0 fsp1", [128, 1024], "bfloat16"),
+        ("d6 pri", [128, 48], "int32"), ("ad", [128, 40], "int32"),
+        ("segm eoi dui eoc dum c48 cf cc cs cl prf kr ctf cd so cpr cl2 bv eqv ss cod cle scb sc2 fv tot", [128, 48], "float32"),
+        ("jx0 jx1", [128, 8, 256], "bfloat16"), ("ms", [128, 256], "bfloat16"),
+        ("hx", [128, 2, 48], "int32"), ("sch", [128, 5, 128], "int32"),
+        ("eq", [128, 200], "float32"), ("m1", [128, 80], "float32"),
+        ("soff cdl", [128, 48], "uint16"), ("fl dec lf0 lf1", [128, 8], "uint16"),
+        ("eall aa hit bb", [128, NDUM], "float32"), ("ypt", [128, 1024], "float32"),
+        ("lst0 lst1", [128, 4], "uint16"), ("eu0 eu1", [128, 64], "uint16"),
+        ("fr0 fr1", [128, 6 * 1024], "bfloat16"), ("dr0 dr1", [128, 768], "bfloat16"),
+        ("ab0 ab1", [128, 4, 256], "bfloat16"), ("rg0 rg1", [128, 256], "bfloat16")):
+    for _m in _n.split():
+        SCRATCH[_m] = ("sbuf", _s, _d)
+for _m in "kp0 kp1 pd0 pd1 pnew pmis".split():
+    SCRATCH[_m] = ("psum", [128, 512], "float32")
+SEMAPHORES = ("cv cs ct cg lpk0 lpk1 lrt ljc lsr lfx rw1 rw2 rf1 rf2 lsend oyf oyp0 oyp1 oyp2 oyp3").split()
+LNAMES = ("FWD", "FWD8", "REV", "ROUT", "PRR", "TRL", "TRS")
+LISTS = ((8, -47, 0, "q6"), (8, -47, -8, "q6"), (-1, 12, 5, "q6"), (-8, 49, 40, "q6"), (-8, 49, 32, "q6"),
+         (6, -47, 0, "q8"), (6, -49, 5, "q8"))
+
+
+def make_flow(g, T):
+    queues = {"v": g.vector, "s": g.scalar, "t": g.tensor, "g": g, "y": g.sync}
+    know = {q: {} for q in queues}
+    total, clocks, writer, readers = {}, {}, {}, {}
+    batch, collect = [], [False]
+
+    def need(q, toks):
+        worst = {}
+        for sem, val in toks:
+            if know[q].get(sem, 0) < val:
+                worst[sem] = max(worst.get(sem, 0), val)
+        for sem, val in sorted(worst.items()):
+            if know[q].get(sem, 0) < val:
+                queues[q].wait_ge(T.sem[sem], val)
+                for k, n in clocks[(sem, val)].items():
+                    know[q][k] = max(know[q].get(k, 0), n)
+
+    def deps(reads, writes):
+        toks = [writer[r] for r in reads if r in writer]
+        for w in writes:
+            if w in writer:
+                toks.append(writer[w])
+            toks += readers.get(w, [])
+        return toks
+
+    def done(tok, reads, writes):
+        for r in reads:
+            readers.setdefault(r, []).append(tok)
+        for w in writes:
+            writer[w] = tok
+            readers[w] = []
+
+    def schedule():
+        lag = 0.12
+        w, rd, pred = {}, {}, []
+        for i, it in enumerate(batch):
+            p = {w[r] for r in it[2] if r in w}
+            for x in it[3]:
+                p |= ({w[x]} if x in w else set()) | rd.get(x, set())
+            for r in it[2]:
+                rd.setdefault(r, set()).add(i)
+            for x in it[3]:
+                w[x] = i
+                rd[x] = set()
+            pred.append(p - {i})
+        prio = [it[6] for it in batch]
+        for i in range(len(batch) - 1, -1, -1):
+            for p in pred[i]:
+                prio[p] = max(prio[p], batch[p][6] + lag + prio[i])
+        free, endt, left = {}, {}, list(range(len(batch)))
+        while left:
+            best = None
+            for i in left:
+                if all(p in endt for p in pred[i]):
+                    st = max([free.get(batch[i][0], 0.0)] + [endt[p] + lag for p in pred[i]])
+                    k = (round(st, 3), -prio[i], i)
+                    best = k if best is None or k < best else best
+            i = best[2]
+            left.remove(i)
+            endt[i] = best[0] + batch[i][6]
+            free[batch[i][0]] = endt[i]
+            issue(*batch[i][:6])
+        batch.clear()
+
+    def op(q, calls, reads, writes, sem=None, inc=1, dur=0.06):
+        if collect[0]:
+            batch.append((q, calls, reads, writes, sem, inc, dur))
+        else:
+            issue(q, calls, reads, writes, sem, inc)
+
+    def issue(q, calls, reads, writes, sem, inc):
+        remote = q == "r"
+        q = "g" if remote else q
+        need(q, deps(reads, writes))
+        name = sem or "c" + q
+        for c in (calls if isinstance(calls, list) else [calls]):
+            if remote:
+                c(queues[q])
+            else:
+                c(queues[q]).then_inc(T.sem[name], inc)
+            total[name] = total.get(name, 0) + inc
+            clocks[(name, total[name])] = {**know[q], name: total[name]}
+        done((name, total[name]), reads, writes)
+
+    def send(call, reads, lsem, n):
+        op("r", call, reads, [], lsem, n, 1.0)
+
+    def lands(names, sem, n):
+        total[sem] = n
+        clocks[(sem, n)] = {sem: n}
+        done((sem, n), [], list(names))
+
+    def finish():
+        for sem, n in sorted(total.items()):
+            if know["g"].get(sem, 0) < n:
+                g.wait_ge(T.sem[sem], n)
+    return op, send, lands, finish, collect, schedule
+
+
+def rank_program(g, core, T, topo):
+    rank = T.rank_of(core)
+    if rank is None:
+        return
+    N = len(T.cores)
+    op, send, lands, finish, collect, schedule = make_flow(g, T)
+
+    def V(fn, r, w, dur=0.06):
+        op("v", fn, r, w, dur=dur)
+
+    def G(fn, r, w):
+        op("g", fn, r, w)
+
+    def Sc(fn, r, w, dur=0.12):
+        op("s", fn, r, w, dur=dur)
+
+    op("y", lambda e: e.dma_start(T.jci[:], T.jc[:]), [], ["jci"], "ljc", 16)
+    op("s", lambda e: e.dma_start(T.sri[:], T.sr[:]), [], ["sri"], "lsr", 16)
+    op("y", lambda e: e.dma_start(T.pkt[:, 0:512], T.pk[:, 0:512]), [], ["pkt0"], "lpk0", 16)
+    op("s", lambda e: e.dma_start(T.fin0[:], T.fx[:]), [], ["fin0"], "lfx", 16)
+    op("y", lambda e: e.dma_start(T.pkt[:, 512:1024], T.pk[:, 512:1024]), [], ["pkt1"], "lpk1", 16)
+    op("s", lambda e: e.dma_start(T.rtt[:], T.rt[:]), [], ["rtt"], "lrt", 16)
+    for t in (1, 2):
+        lands(("fw%d" % t, "fws%d" % t), "rw%d" % t, len(topo.engines(T.cores[(rank - t) % N], core)))
+        lands(("fin%d" % t,), "rf%d" % t, len(topo.engines(T.cores[(rank - 1) % N], core)))
+
+    flag = {"allow_small_or_imprecise_dtypes": True}
+    G(lambda e: e.iota(T.pi[:], [[1, 1]], 0, 1), [], ["pi"])
+    G(lambda e: e.iota(T.io32[:], [[1, 32]], 0, 0), [], ["io32"])
+    V(lambda e: e.memset(T.onef[:], 1.0), [], ["onef"])
+    V(lambda e: e.memset(T.oneb[:], 1.0), [], ["oneb"])
+    G(lambda e: e.affine_select(T.bon[:], T.onef[:], [[-16, 8], [0, 16]], A.is_ge, 0.0, 0, 1), ["onef"], ["bon"])
+    G(lambda e: e.affine_select(T.bof[:], T.bon[:], [[16, 8], [0, 16]], A.is_ge, 0.0, 15, -1), ["bon"], ["bof"])
+    G(lambda e: e.affine_select(T.bo8[:], T.oneb[0:8, :], [[1, 128]], A.is_ge, 0.0, 0, -16), ["oneb"], ["bo8"])
+    G(lambda e: e.affine_select(T.bo8[:], T.bo8[:], [[-1, 128]], A.is_ge, 0.0, 15, 16), ["bo8"], ["bo8"])
+    G(lambda e: e.affine_select(T.idb[:], T.oneb[:], [[-1, 128]], A.is_equal, 0.0, 0, 1), ["oneb"], ["idb"])
+    G(lambda e: e.iota(T.jji[:], [[16, 4]], 0, 0), [], ["jji"])
+    G(lambda e: e.iota(T.eoi[:], [[16, 8], [128, 6]], 0, 0, **flag), [], ["eoi"])
+    G(lambda e: e.iota(T.dui[:], [[16, 8], [-128, 6]], 2048 + 640, 0, **flag), [], ["dui"])
+    G(lambda e: e.iota(T.fbi[:], [[0, 2], [256, 4]], 5 * 1024, 0, **flag), [], ["fbi"])
+    for h in "01":
+        G(lambda e: e.iota(T["fsp" + h][:], [[0, 1024]], 0, 0, **flag), [], ["fsp%s_%d" % (h, b) for b in range(4)])
+    V(lambda e: e.memset(T.sel[:], 0.0), [], ["sel"])
+    V(lambda e: e.tensor_scalar(T.yli[:], T.pi[:], 15, None, A.bitwise_and), ["pi"], ["yli"])
+    V(lambda e: e.memset(T.fmask[:], 1.0), [], ["fmask"])
+    V(lambda e: e.tensor_copy(T.ylf[:], T.yli[:]), ["yli"], ["ylf"])
+    V(lambda e: e.tensor_scalar(T.q2k[:], T.yli[:], 2048.0, None, A.mult), ["yli"], ["q2k"])
+    V(lambda e: e.tensor_scalar(T.y16[:], T.yli[:], 16.0, None, A.mult), ["yli"], ["y16"])
+    V(lambda e: e.tensor_scalar(T.w1[:], T.io32[:], T.ylf[:, 0:1], None, A.is_equal), ["io32", "ylf"], ["w1"])
+    V(lambda e: e.memset(T.fmask[:, 0::16], 0.0), ["fmask"], ["fmask"])
+    V(lambda e: e.memset(T.tab[:, 2048:], 0.0), [], ["tab"])
+    V(lambda e: e.memset(T.km[:], 0.0), [], ["km"])
+    SELK = ["sel%d" % y for y in range(16)]
+    for y in range(16):
+        Sc(lambda e: e.activation(T.sel[:, y, y::16], T.bof[:, 0::16], AF.Copy, scale=32768.0), ["bof", "sel"], ["sel%d" % y])
+    V(lambda e: e.tensor_scalar(T.jh[:], T.jci[:], 8, None, A.arith_shift_right), ["jci"], ["jh"])
+    V(lambda e: e.tensor_scalar(T.jl[:], T.jci[:], 255, None, A.bitwise_and), ["jci"], ["jl"])
+    V(lambda e: e.memset(T.km[:, 0::16], 1.0e9), ["km"], ["km"])
+    V(lambda e: e.tensor_copy(T.jlb[:], T.jl[:]), ["jl"], ["jlb"])
+    V(lambda e: e.tensor_scalar(T.jhb[:], T.jh[:], 256.0, T.q2k[:, 0:1], A.mult, A.add), ["jh", "q2k"], ["jhb"])
+    V(lambda e: e.tensor_copy(T.srb[:], T.sri[:]), ["sri"], ["srb"])
+    op("t", lambda e: e.matmul(T.pnew[:, 0:128], T.bo8[:], T.srb[:], True, True), ["bo8", "srb"], ["pnew"])
+    for q in range(16):
+        V(lambda e: e.tensor_scalar(T.jx0[:, :, q::16], T.jhb[:], T.w1[:, q:q + 1], None, A.mult), ["jhb", "w1"], ["jx0_%d" % q])
+        Sc(lambda e: e.activation(T.jx1[:, :, q::16], T.jlb[:], AF.Copy, scale=T.w1[:, q:q + 1]), ["jlb", "w1"], ["jx1_%d" % q])
+    V(lambda e: e.tensor_scalar(T.oh[:], T.pnew[:, 0:128], T.ylf[:, 0:1], None, A.is_equal), ["pnew", "ylf"], ["oh"])
+    V(lambda e: e.tensor_tensor(T.ms[:, 0:128], T.oh[:], T.jhb[:], A.mult), ["oh", "jhb"], ["ms0"])
+    V(lambda e: e.tensor_tensor(T.ms[:, 128:256], T.oh[:], T.jlb[:], A.mult), ["oh", "jlb"], ["ms1"])
+    op("t", [lambda e, y=y: e.matmul(T.pd1[:, 0:16], T.sel[:, y, :], T.ms[:, y::16], y == 0, y == 15)
+             for y in range(16)], SELK + ["ms0", "ms1"], ["pd1"])
+    Sc(lambda e: e.activation(T.fw0[:, 256:272], T.pd1[:, 0:16], AF.Copy, scale=1.0 / 32768.0), ["pd1"], ["fws0"])
+    for i, b in enumerate(("jx0", "jx1")):
+        op("t", [lambda e, y=y: e.matmul(T.pd0[:, i * 128:(i + 1) * 128], T.sel[:, y, :], T[b][:, :, y * 16:y * 16 + 16], y == 0, y == 15)
+                 for y in range(16)], SELK + ["%s_%d" % (b, q) for q in range(16)], ["pd0"])
+    V(lambda e: e.memset(T.segm[:], 1.0), [], ["segm"])
+    V(lambda e: e.tensor_scalar(T.jj[:], T.jji[:], T.ylf[:, 0:1], None, A.add), ["jji", "ylf"], ["jj"])
+    V(lambda e: e.tensor_scalar(T.fb[:], T.fbi[:], T.y16[:, 0:1], 1.0 / 1024.0, A.add, A.mult), ["fbi", "y16"], ["fb"])
+    V(lambda e: e.tensor_scalar(T.q6[:], T.jj[:], 1.0 / 6.0, -2.5 / 6.0, A.mult, A.add), ["jj"], ["q6"])
+    V(lambda e: e.tensor_scalar(T.q8[:], T.jj[:], 0.125, -3.5 / 8.0, A.mult, A.add), ["jj"], ["q8"])
+    V(lambda e: e.memset(T.segm[:, 0::6], 0.0), ["segm"], ["segm"])
+    V(lambda e: e.tensor_copy(T.q6f[:], T.q6[:]), ["q6"], ["q6f"])
+    V(lambda e: e.tensor_copy(T.q8f[:], T.q8[:]), ["q8"], ["q8f"])
+    for i, (a, b, c, q) in enumerate(LISTS):
+        Sc(lambda e: e.activation(T.la[:, 4 * i:4 * i + 4], T.jj[:], AF.Copy, scale=float(a), bias=float(c)), ["jj"], ["la%d" % i])
+        Sc(lambda e: e.activation(T.lb[:, 4 * i:4 * i + 4], T[q + "f"][:], AF.Copy, scale=float(b)), [q + "f"], ["lb%d" % i])
+    Sc(lambda e: e.activation(T.fw0[:, 0:256], T.pd0[:, 0:256], AF.Copy, scale=1.0 / 32768.0), ["pd0"], ["fw0"])
+    Sc(lambda e: e.activation(T.idn[:], T.idb[:], AF.Copy, scale=-1.0), ["idb"], ["idn"])
+    for t in (1, 2):
+        dst = T.cores[(rank + t) % N]
+        rid, pid = topo.addr(dst, core)
+        send(lambda e: e.remote_dma(T["fw%d" % t][:], T.fw0[:], T.sem["rw%d" % t], T.sem.lsend, pid, rid, topo.mask(core, dst)),
+             ["fw0", "fws0"], "lsend", len(topo.engines(core, dst)))
+    for n in ("eq", "c48", "cl", "cd", "fv"):
+        G(lambda e: e.iota(T[n][:], [[0, T[n].shape[1]]], 0, 0, **flag), [], [n])
+    G(lambda e: e.iota(T.pri[:], [[0, 48]], 0, 0), [], ["pri"])
+    G(lambda e: e.iota(T.hx[:, 0, 40:48], [[0, 8]], 0, 0), [], ["hx5"])
+    for h in "01":
+        G(lambda e: e.iota(T["fr" + h][:, 5120:6144], [[0, 1024]], 0, 0, **flag), [], ["fr%s_5_%d" % (h, b) for b in range(4)])
+    TABK = ["tab"] + ["tab%d%d" % (i, j) for i in range(2) for j in range(2)]
+    for i in range(2):
+        a, b = 512 * i, 512 * i + 512
+        V(lambda e: e.tensor_scalar(T.tmpi[:, a:b], T.pkt[:, a:b], 4095, None, A.bitwise_and), ["pkt%d" % i], ["tmpi%d" % i])
+        V(lambda e: e.tensor_scalar(T.pkt[:, a:b], T.pkt[:, a:b], 12, None, A.arith_shift_right), ["pkt%d" % i], ["pkt%d" % i])
+        V(lambda e: e.tensor_copy(T.tab[:, a:b], T.tmpi[:, a:b]), ["tmpi%d" % i], ["tab%d0" % i])
+        V(lambda e: e.tensor_copy(T.tab[:, 1024 + a:1024 + b], T.pkt[:, a:b]), ["pkt%d" % i], ["tab%d1" % i])
+
+    HXA = ["hxa0", "hxa1"]
+    HXB = ["hxb0", "hxb1"]
+
+    def start_keys(t):
+        fw = "fw%d" % t
+        V(lambda e: e.tensor_tensor(T.sk[:], T[fw][:, 256:264], T[fw][:, 264:272], A.add), ["fws%d" % t], ["sk"])
+        V(lambda e: e.tensor_scalar(T.hx[:, 0, 0:8], T.sk[:], 2047, None, A.bitwise_and), ["sk"], HXA)
+        V(lambda e: e.tensor_scalar(T.hx[:, 1, 0:8], T.sk[:], 11, 15, A.arith_shift_right, A.bitwise_and), ["sk"], HXB)
+        for h in "01":
+            lo = 4 * int(h)
+            V(lambda e, h=h, lo=lo: e.tensor_copy(T["lst" + h][:], T.hx[:, 0, lo:lo + 4]), ["hxa" + h], ["lst" + h])
+
+    def start_facts(h, t):
+        fin = "fin%d" % t
+        lo = 64 * int(h)
+        Sc(lambda e: e.activation(T["fsp" + h][:, 0::16], T[fin][:, lo:lo + 64], AF.Copy), [fin], ["fsp%s_%d" % (h, b) for b in range(4)])
+
+    def entries(h):
+        V(lambda e: e.tensor_copy(T["eu" + h][:], T.tab[:].indirect(T["lst" + h][:])), TABK + ["lst" + h], ["eu" + h])
+
+    def spread(h, s):
+        for x, a, b in (("a", 0, 256), ("b", 256, 1024)):
+            V(lambda e: e.tensor_tensor_scan(T["fr" + h][:, 1024 * s + a:1024 * s + b], T.fmask[:, a:b], T["fsp" + h][:, a:b], 0.0, A.mult, A.add),
+              ["fmask"] + ["fsp%s_%d" % (h, i) for i in range(4)], ["fr%s_%d%s" % (h, s, x)])
+
+    def post(h, s):
+        lo = 64 * int(h)
+        c = s * 8 + 4 * int(h)
+        key = T.sch[:, s - 1, lo + 15:lo + 64:16]
+        sch, lst, lf = "sch%d%s" % (s, h), "lst" + h, "lf" + h
+        V(lambda e: e.tensor_tensor_scan(T.sch[:, s - 1, lo:lo + 64], T.km[:], T["kp" + h][:, 0:64], 0.0, A.max, A.min),
+          ["km", "kp" + h], [sch])
+        V(lambda e: e.tensor_scalar(T.hx[:, 1, c:c + 4], key, 11, 15, A.arith_shift_right, A.bitwise_and), [sch], ["hxb" + h])
+        if s < S:
+            V(lambda e: e.tensor_scalar(T.hx[:, 0, c:c + 4], key, 2047, None, A.bitwise_and), [sch], ["hxa" + h])
+        V(lambda e: e.tensor_scalar(T[lf][:, 0::2], T.hx[:, 1, c:c + 4], T.y16[:, 0:1], None, A.add), ["hxb" + h, "y16"], [lf])
+        if s < S:
+            V(lambda e: e.tensor_copy(T[lst][:], T.hx[:, 0, c:c + 4]), ["hxa" + h], [lst])
+            dst, o, fk = T["fsp" + h], 0, "fsp%s_" % h
+        else:
+            dst, o, fk = T["fr" + h], 5120, "fr%s_5_" % h
+        for b in range(4):
+            win = T["dr" + h][:, 256 * b:256 * b + 256] if b < 3 else T["ab" + h][:, 3, :]
+            Sc(lambda e, b=b, win=win: e.activation(dst[:, o + 256 * b:o + 256 * b + 256:16], win.indirect(T[lf][:, 2 * b:2 * b + 1]), AF.Abs),
+               [("dr%sc0", "dr%sc1", "dr%sc2", "ab%s3")[b] % h, lf], [fk + str(b)])
+
+    def gather(h, s, i):
+        eu, fr, dr = "eu" + h, "fr" + h, "dr" + h
+        f0 = 1024 * (s - 1)
+        V(lambda e: e.tensor_tensor(T[dr][:, 256 * i:256 * i + 256], T.rtt[:].indirect(T[eu][:, 16 * i:16 * i + 16]),
+                                    T[fr][:, f0 + 256 * i:f0 + 256 * i + 256], A.subtract),
+          ["rtt", eu, "fr%s_%d%s" % (h, s - 1, "abb"[i])], [dr + "c%d" % i], 0.37)
+
+    def begin(h, s, t):
+        eu, fr, dr, ab, rg, pd, kp = (n + h for n in ("eu", "fr", "dr", "ab", "rg", "pd", "kp"))
+        f0 = 1024 * (s - 1)
+        Sc(lambda e: e.activation(T[rg][:], T.rtt[:].indirect(T[eu][:, 48:64]), AF.Copy), ["rtt", eu], [rg])
+        gather(h, s, 0)
+        gather(h, s, 1)
+        op("t", [lambda e: e.matmul(T[pd][:, 0:256], T.idb[:], T[rg][:], True, False),
+                 lambda e: e.matmul(T[pd][:, 0:256], T.idn[:], T[fr][:, f0 + 768:f0 + 1024], False, True)],
+           ["idb", "idn", rg, "fr%s_%db" % (h, s - 1)], [pd])
+        fw = "fw%d" % t
+        lo = 64 * int(h)
+        op("t", [lambda e: e.matmul(T[kp][:, 0:64], T.idb[:], T[fw][:, lo:lo + 64], True, False),
+                 lambda e: e.matmul(T[kp][:, 0:64], T.idb[:], T[fw][:, 128 + lo:128 + lo + 64], False, False)], ["idb", fw], [kp])
+        for b in (0, 1):
+            Sc(lambda e, b=b: e.activation(T[ab][:, b, :], T[dr][:, 256 * b:256 * b + 256], AF.Abs), [dr + "c%d" % b], [ab + str(b)], 0.3)
+
+    def end(h, s):
+        dr, ab, kp, pd = "dr" + h, "ab" + h, "kp" + h, "pd" + h
+        gather(h, s, 2)
+        Sc(lambda e: e.activation(T[ab][:, 3, :], T[pd][:, 0:256], AF.Abs), [pd], [ab + "3"], 0.3)
+        Sc(lambda e: e.activation(T[ab][:, 2, :], T[dr][:, 512:768], AF.Abs), [dr + "c2"], [ab + "2"], 0.3)
+        op("t", [lambda e, y=y: e.matmul(T[kp][:, 0:64], T.sel[:, y, :], T[ab][:, :, y * 16:y * 16 + 16], False, y == 15)
+                 for y in range(16)], SELK + [ab + "0", ab + "1", ab + "2", ab + "3"], [kp], dur=0.75)
+
+    def L(name):
+        i = LNAMES.index(name)
+        return T.lists[:, 4 * i:4 * i + 3]
+
+    def close(t):
+        EQK = ["eq"] + ["eq%d" % d for d in range(1, 6)]
+        for d in range(1, 6):
+            V(lambda e, d=d: e.tensor_tensor(T.eq[:, 48 * (d - 1):40 * d], T.hx[:, 1, 8 * d:48], T.hx[:, 1, 0:48 - 8 * d], A.is_equal),
+              HXB + ["eq"], ["eq%d" % d])
+        V(lambda e: e.tensor_scalar(T.prf[:], T.hx[:, 1, :].indirect(L("ROUT")), 1.0, None, A.add), HXB + ["lists"], ["prf"], 0.11)
+        V(lambda e: e.tensor_tensor(T.m1[:], T.eq[:, 0:80], T.eq[:, 80:160], A.max), EQK, ["m1"])
+        V(lambda e: e.tensor_tensor(T.m1[:, 0:40], T.m1[:, 0:40], T.m1[:, 40:80], A.max), ["m1"], ["m1"])
+        V(lambda e: e.tensor_copy(T.ctf[:], T.hx[:, 0, :].indirect(L("FWD8"))), HXA + ["hx5", "lists"], ["ctf"], 0.11)
+        V(lambda e: e.tensor_tensor(T.c48[:, 8:48], T.m1[:, 0:40], T.eq[:, 160:200], A.max), ["m1", "c48"] + EQK, ["c48"])
+        V(lambda e: e.tensor_scalar(T.kr[:], T.hx[:, 1, :].indirect(L("ROUT")), -31.0, None, A.add), HXB + ["lists"], ["kr"], 0.11)
+        V(lambda e: e.tensor_copy(T.cf[:], T.c48[:].indirect(L("FWD"))), ["c48", "lists"], ["cf"], 0.11)
+        V(lambda e: e.tensor_scalar(T.d6[:, 8:48], T.sch[:, :, 15::16], 15, None, A.arith_shift_right),
+          ["sch%d%s" % (s, h) for s in range(1, 6) for h in "01"], ["d6"])
+        V(lambda e: e.tensor_tensor_scan(T.cc[:], T.segm[:], T.cf[:], 0.0, A.mult, A.max), ["segm", "cf"], ["cc"])
+        V(lambda e: e.tensor_tensor(T.ad[:], T.d6[:, 8:48], T.d6[:, 0:40], A.add), ["d6", "d60"], ["ad"])
+        V(lambda e: e.tensor_tensor(T.cl[:, 1:48], T.cc[:, 1:48], T.cc[:, 0:47], A.is_gt), ["cc", "cl"], ["cl"])
+        V(lambda e: e.tensor_tensor(T.cd[:, 1:48], T.cc[:, 0:47], T.dum[:, 1:48], A.mult), ["cc", "dum", "cd"], ["cd"])
+        V(lambda e: e.tensor_tensor_scan(T.cs[:], T.segm[:], T.cc[:], 0.0, A.mult, A.add), ["segm", "cc"], ["cs"])
+        V(lambda e: e.tensor_tensor(T.cpr[:], T.cl[:].indirect(L("REV")), T.prf[:], A.mult), ["cl", "prf", "lists"], ["cpr"], 0.11)
+        V(lambda e: e.tensor_tensor(T.so[:], T.cd[:], T.ctf[:], A.max), ["cd", "ctf"], ["so"])
+        V(lambda e: e.tensor_tensor(T.fs[:], T.fb[:], T.cs[:, 4::6], A.subtract), ["fb", "cs"], ["fs"])
+        V(lambda e: e.tensor_tensor_scan(T.bv[:], T.segm[:], T.cpr[:], 0.0, A.mult, A.add), ["segm", "cpr"], ["bv"])
+        V(lambda e: e.tensor_copy(T.soff[:], T.so[:].indirect(L("TRS"))), ["so", "lists"], ["soff"], 0.11)
+        V(lambda e: e.tensor_scalar(T.fl[:], T.fs[:], 1024.0, None, A.mult), ["fs"], ["fl"])
+        for h in "01":
+            lo = 64 * int(h)
+            Sc(lambda e, h=h, lo=lo: e.activation(T.fout[:, lo:lo + 64], T["fr" + h][:].indirect(T.fl[:, 4 * int(h):4 * int(h) + 4]), AF.Copy),
+               ["fl"] + ["fr%s_%d%s" % (h, s, x) for s in range(5) for x in "ab"] + ["fr%s_5_%d" % (h, b) for b in range(4)], ["fout" + h])
+        if t < VI - 1:
+            dst = T.cores[(rank + 1) % N]
+            rid, pid = topo.addr(dst, core)
+            send(lambda e: e.remote_dma(T["fin%d" % (t + 1)][:], T.fout[:], T.sem["rf%d" % (t + 1)], T.sem.lsend, pid, rid,
+                                        topo.mask(core, dst)), ["fout0", "fout1"], "lsend", len(topo.engines(core, dst)))
+        else:
+            op("y", lambda e: e.dma_start(T.yf[:], T.fout[:]), ["fout0", "fout1"], ["yf"], "oyf", 16)
+        Sc(lambda e: e.activation(T.eall[:], T.tab[:].indirect(T.soff[:, 0:40]), AF.Copy), TABK + ["soff"], ["eall"], dur=0.86)
+        V(lambda e: e.tensor_scalar(T.cl2[:], T.cl[:].indirect(L("REV")), 2.0, None, A.mult), ["cl", "lists"], ["cl2"], 0.11)
+        V(lambda e: e.tensor_tensor(T.eqv[:], T.bv[:], T.prf[:], A.is_equal), ["bv", "prf"], ["eqv"])
+        V(lambda e: e.tensor_tensor(T.cle[:], T.cl[:].indirect(L("REV")), T.eoc[:], A.mult), ["cl", "eoc", "lists"], ["cle"], 0.11)
+        V(lambda e: e.tensor_tensor_scan(T.ss[:], T.cl2[:], T.eqv[:], 0.0, A.add, A.subtract), ["cl2", "eqv"], ["ss"])
+        if t > 0:
+            V(lambda e: e.tensor_scalar(T.ad[:], T.ad[:], T.zc[:, 0:1], None, A.add), ["ad", "zc"], ["ad"])
+        V(lambda e: e.tensor_tensor(T.cod[:], T.ss[:], T.kr[:], A.mult), ["ss", "kr"], ["cod"])
+        V(lambda e: e.tensor_tensor_scan(T.scb[:], T.segm[:], T.cle[:], 0.0, A.mult, A.add), ["segm", "cle"], ["scb"])
+        V(lambda e: e.tensor_scalar(T.cdl[:], T.cod[:].indirect(L("TRL")), 31.0, None, A.add), ["cod", "lists"], ["cdl"], 0.11)
+        Sc(lambda e: e.activation(T.hit[:], T.w1[:].indirect(T.cdl[:, 0:40]), AF.Copy), ["w1", "cdl"], ["hit"], dur=0.86)
+        V(lambda e: e.tensor_scalar(T.pri[:, 0:40], T.ad[:], 1, None, A.bitwise_and), ["ad", "pri"], ["pri"])
+        V(lambda e: e.tensor_tensor(T.sc2[:], T.scb[:], T.eoc[:], A.subtract), ["scb", "eoc"], ["sc2"])
+        V(lambda e: e.tensor_tensor(T.fv[:, 0:47], T.ss[:, 0:47], T.ss[:, 1:48], A.is_gt), ["ss", "fv"], ["fv"])
+        V(lambda e: e.tensor_tensor(T.sc2[:], T.pri[:].indirect(L("PRR")), T.sc2[:], A.mult), ["pri", "sc2", "lists"], ["sc2"], 0.11)
+        V(lambda e: e.tensor_tensor(T.sc2[:], T.sc2[:], T.eoc[:], A.add), ["sc2", "eoc"], ["sc2"])
+        V(lambda e: e.tensor_tensor(T.sc2[:], T.sc2[:], T.fv[:], A.mult), ["sc2", "fv"], ["sc2"])
+        V(lambda e: e.tensor_tensor_scan(T.tot[:], T.segm[:], T.sc2[:], 0.0, A.mult, A.add), ["segm", "sc2"], ["tot"])
+        V(lambda e: e.tensor_copy(T.dec[:], T.tot[:, 5::6]), ["tot"], ["dec"])
+        Sc(lambda e: e.activation(T.edec[:], T.eall[:].indirect(T.dec[:]), AF.Copy), ["eall", "dec"], ["edec"], dur=0.22)
+        V(lambda e: e.tensor_tensor(T.aa[:], T.w1c[:].indirect(T.cdl[:, 0:40]), T.eall[:], A.mult), ["w1c", "cdl", "eall"], ["aa"], dur=0.85)
+        V(lambda e: e.tensor_tensor(T.edec[:], T.aa[:].indirect(T.dec[:]), T.edec[:], A.subtract), ["aa", "dec", "edec"], ["edec"], dur=0.21)
+        op("t", lambda e: e.matmul(T.pnew[:, 0:128], T.bon[:], T.edec[:], True, True), ["bon", "edec"], ["pnew"], dur=0.4)
+        if t < VI - 1:
+            V(lambda e: e.tensor_reduce(T.zr[:], T.cc[:, 5::6], AxisListType.X, A.add), ["cc"], ["zr"])
+            op("t", lambda e: e.matmul(T.pmis[:, 0:1], T.onef[:], T.zr[:], True, True), ["onef", "zr"], ["pmis"])
+            start_keys(t + 1)
+        for r in range(5):
+            V(lambda e, r=r: e.tensor_tensor(T.bb[:, 128 * r:128 * r + 128], T.pnew[:, 0:128], T.hit[:, 128 * r:128 * r + 128], A.mult),
+              ["pnew", "hit"], ["bb%d" % r], dur=0.11)
+        V(lambda e: e.tensor_tensor(T.tab[:].indirect(T.soff[:, 0:40]), T.aa[:], T.bb[:], A.add),
+          ["aa", "soff"] + TABK + ["bb%d" % r for r in range(5)], ["tab"], dur=2.0)
+
+    start_keys(0)
+    for t in range(VI):
+        fin = "fin%d" % t
+        start_facts("0", t)
+        start_facts("1", t)
+        op("t", [lambda e, y=y: e.matmul(T.pmis[:, 8:16], T.sel[:, y, :], T[fin][:, y::16], y == 0, y == 15) for y in range(16)],
+           SELK + [fin], ["pmis"])
+        spread("0", 0)
+        entries("0")
+        begin("0", 1, t)
+        entries("1")
+        end("0", 1)
+        spread("1", 0)
+        begin("1", 1, t)
+        V(lambda e: e.tensor_scalar(T.d6[:, 0:8], T.pmis[:, 8:16], 1.0 / 32768.0, None, A.mult), ["pmis"], ["d60"])
+        if t == 1:
+            V(lambda e: e.tensor_copy(T.zc[:], T.pmis[:, 0:1]), ["pmis"], ["zc"])
+        elif t == 2:
+            V(lambda e: e.tensor_tensor(T.zc[:], T.pmis[:, 0:1], T.zc[:], A.add), ["pmis", "zc"], ["zc"])
+        if t == 0:
+            n = 4 * len(LISTS)
+            V(lambda e: e.tensor_tensor(T.lc[:, 0:n], T.la[:, 0:n], T.lb[:, 0:n], A.add),
+              [x % i for x in ("la%d", "lb%d") for i in range(len(LISTS))], ["lc"])
+            Sc(lambda e: e.activation(T.eoc[:], T.eoi[:], AF.Identity, bias=T.ylf[:, 0:1]), ["eoi", "ylf"], ["eoc"])
+            Sc(lambda e: e.activation(T.dum[:], T.dui[:], AF.Identity, bias=T.ylf[:, 0:1]), ["dui", "ylf"], ["dum"])
+            Sc(lambda e: e.activation(T.w1c[:], T.w1[:], AF.Copy, scale=-1.0, bias=1.0), ["w1"], ["w1c"])
+            Sc(lambda e: e.activation(T.bon[:], T.bof[:], AF.Copy, scale=-1.0), ["bof"], ["bon"])
+            V(lambda e: e.tensor_copy(T.lists[:, 0:n], T.lc[:, 0:n]), ["lc"], ["lists"])
+        for s in range(1, S + 1):
+            collect[0] = s == S
+            post("0", s)
+            end("1", s)
+            if s < S:
+                entries("0")
+                spread("0", s)
+                begin("0", s + 1, t)
+            post("1", s)
+            if s < S:
+                end("0", s + 1)
+                entries("1")
+                spread("1", s)
+                begin("1", s + 1, t)
+        close(t)
+        collect[0] = False
+        schedule()
+
+    for i in range(4):
+        pd, o = "pd%d" % (i % 2), 256 * i
+        Sc(lambda e: e.activation(T[pd][:, 0:256], T.tab[:, 1024 + o:1280 + o], AF.Copy, scale=4096.0), TABK, [pd])
+        V(lambda e: e.tensor_tensor(T.ypt[:, o:o + 256], T[pd][:, 0:256], T.tab[:, o:o + 256], A.add), [pd] + TABK, ["ypt%d" % i])
+        op("y", lambda e: e.dma_start(T.yp[:, o:o + 256], T.ypt[:, o:o + 256]), ["ypt%d" % i], ["yp%d" % i], "oyp%d" % i, 16)
+    finish()

@@ -7,39 +7,109 @@ NDUM = 640
 SCRATCH = {}
 for _n, _s, _d in (
         ("pkt tmpi", [128, 1024], "int32"), ("rtt", [128, 3072], "bfloat16"), ("tab", [128, 2048 + NDUM], "float32"),
-        ("jci jh jl", [128, 128], "int32"), ("sri", [8, 128], "int32"), ("srb bo8", [8, 128], "bfloat16"),
-        ("fin0 fin1 fin2 fout oneb idb idn jhb jlb oh", [128, 128], "bfloat16"), ("fw0 fw1 fw2", [128, 272], "bfloat16"),
-        ("pi yli", [128, 1], "int32"), ("ylf y16 q2k zr zc", [128, 1], "float32"),
-        ("io32", [128, 32], "int32"), ("w1 w1c la lb lc", [128, 32], "float32"), ("lists", [128, 32], "uint16"),
-        ("onef bof bon edec", [128, 128], "float32"), ("sel", [128, 16, 128], "bfloat16"),
-        ("sk", [128, 8], "int32"), ("fbi fb fs", [128, 8], "float32"),
-        ("jji q6 q8", [128, 4], "int32"), ("jj q6f q8f", [128, 4], "float32"),
-        ("km", [128, 64], "float32"), ("fmask fsp0 fsp1", [128, 1024], "bfloat16"),
-        ("d6 pri", [128, 48], "int32"), ("ad", [128, 40], "int32"),
-        ("segm eoi dui eoc dum c48 cf cc cs cl prf kr ctf cd so cpr cl2 bv eqv ss cod cle scb sc2 fv tot", [128, 48], "float32"),
-        ("jx0 jx1", [128, 8, 256], "bfloat16"), ("ms", [128, 256], "bfloat16"),
-        ("hx", [128, 2, 48], "int32"), ("sch", [128, 5, 128], "int32"),
-        ("eq", [128, 200], "float32"), ("m1", [128, 80], "float32"),
-        ("soff cdl", [128, 48], "uint16"), ("fl dec lf0 lf1", [128, 8], "uint16"),
-        ("eall aa hit bb", [128, NDUM], "float32"), ("ypt", [128, 1024], "float32"),
-        ("lst0 lst1", [128, 4], "uint16"), ("eu0 eu1", [128, 64], "uint16"),
-        ("fr0 fr1", [128, 6 * 1024], "bfloat16"), ("dr0 dr1", [128, 768], "bfloat16"),
-        ("ab0 ab1", [128, 4, 256], "bfloat16"), ("rg0 rg1", [128, 256], "bfloat16")):
+        ("jci jh jl i144", [128, 144], "int32"), ("jhb jlb selb", [128, 144], "bfloat16"),
+        ("tra trb", [128, 2, 4, 32], "bfloat16"),
+        ("sri", [8, 128], "int32"), ("srb bo8", [8, 128], "bfloat16"),
+        ("fout", [128, 128 * VI], "bfloat16"), ("fin0 fin1 fin2 oneb idb ide ido oh", [128, 128], "bfloat16"), ("fw0 fw1 fw2", [128, 17, 16], "bfloat16"),
+        ("pi yli", [128, 1], "int32"), ("ylf y64 q2k g15 zr zc", [128, 1], "float32"),
+        ("i80", [128, 80], "int32"), ("w1 w1c", [128, 80], "float32"),
+        ("negf bon edec", [128, 128], "float32"), ("ms", [128, 256], "bfloat16"),
+        ("nd ndi", [64, 1024], "bfloat16"), ("cst", [64, 64], "bfloat16"), ("c64 ft0 ft1", [64, 128], "bfloat16"),
+        ("km qq st lp zs zb ppf", [128, 64], "float32"), ("cep pm", [128, 8, 8], "float32"), ("pp", [128, 8, 9], "int32"),
+        ("cod", [128, 72], "float32"), ("so", [128, 48], "float32"), ("yi", [128, 3], "int32"), ("ybf y5 y8", [128, 1], "float32"),
+        ("l5i l8i", [128, 4], "int32"), ("l5 l8", [128, 4], "uint16"), ("soff cdl", [128, 64], "uint16"),
+        ("eq cs m25", [128, 200], "float32"), ("m8a m8b", [128, 32], "float32"),
+        ("dui dum cei ce", [128, 8, 5], "float32"), ("m5a m5b sm tq cl clp", [128, 40], "float32"), ("rr w5", [128, 41], "float32"),
+        ("cc pri", [128, 8, 5], "int32"), ("dd ad", [128, 40], "int32"),
+        ("p5", [128, 8], "int32"), ("bsi cxh sk1 ncc", [128, 8], "float32"), ("hz", [128, 2], "float32"),
+        ("lbi", [128, 4], "int32"), ("lb lf0 lf1", [128, 4], "uint16"), ("lst0 lst1 fl dec", [128, 8], "uint16"),
+        ("sch", [128, 128, S + 1], "int32"), ("eall aa hit bb", [128, NDUM], "float32"),
+        ("ypt", [128, 1024], "float32"), ("eu0 eu1", [128, 64], "uint16"),
+        ("fh0 fh1", [128, 320], "bfloat16"), ("rg0 rg1", [128, 1024], "bfloat16"),
+        ("ab0 ab1", [128, 1024], "bfloat16")):
     for _m in _n.split():
         SCRATCH[_m] = ("sbuf", _s, _d)
-for _m in "kp0 kp1 pd0 pd1 pnew pmis".split():
+for _m in "kp0 kp1 pd0 pd1 pd2 pd3 pmis".split():
     SCRATCH[_m] = ("psum", [128, 512], "float32")
-SEMAPHORES = ("cv cs ct cg lpk0 lpk1 lrt ljc lsr lfx rw1 rw2 rf1 rf2 lsend oyf oyp0 oyp1 oyp2 oyp3").split()
-LNAMES = ("FWD", "FWD8", "REV", "ROUT", "PRR", "TRL", "TRS")
-LISTS = ((8, -47, 0, "q6"), (8, -47, -8, "q6"), (-1, 12, 5, "q6"), (-8, 49, 40, "q6"), (-8, 49, 32, "q6"),
-         (6, -47, 0, "q8"), (6, -49, 5, "q8"))
+SCRATCH["pft"] = ("psum", [128, 1024], "bfloat16")
+SEMAPHORES = ("cv cs ct cg lpk0 lpk1 lrt0 lrt1 ljc ljw lsr lfx rw1 rw2 rf10 rf11 rf20 rf21 lsend oyf0 oyf1 "
+              "oyp0 oyp1 oyp2 oyp3").split()
+GATHERS = (("s", 0, 4), ("v", 4, 8), ("v", 8, 12), ("v", 12, 16))
+BANKS = ((0, 4), (4, 8), (8, 12), (12, 16))
+PERIOD = 2.0
+PLACE = {"scan": 0.0, "row": 0.04, "court": 0.03, "lf": 0.44, "lst": 0.61, "fh": 0.48, "eu": 0.78, "turn": 0.79, "ft": 1.19,
+         "pay": 0.93, "g0": 1.96, "g1": 1.32, "g2": 1.04, "g3": 2.41,
+         "n0": 1.1, "i0": 1.7, "n1": 1.25, "i1": 1.74, "n2": 1.73, "i2": 2.27, "n3": 1.98, "i3": 2.43,
+         "a0": 2.08, "a1": 2.35, "a2": 2.61, "a3": 3.4, "m0": 2.42, "m1": 2.71, "m2": 3.01, "m3": 3.08}
+CYC, GATH, SCAT, PE, LAG = 0.83e-3, 1.5, 3.8, 0.45e-3, 0.17
+ORDER = []
+
+
+def plan(batch):
+    w, rd, pred = {}, {}, []
+    for i, it in enumerate(batch):
+        p = {w[r] for r in it[2] if r in w}
+        for x in it[3]:
+            p |= ({w[x]} if x in w else set()) | rd.get(x, set())
+        for r in it[2]:
+            rd.setdefault(r, set()).add(i)
+        for x in it[3]:
+            w[x] = i
+            rd[x] = set()
+        pred.append(p - {i})
+    n = len(batch)
+    busy, late = [it[6] for it in batch], [it[7] for it in batch]
+    succ = [[] for _ in batch]
+    left = [len(p) for p in pred]
+    for i in range(n):
+        for p in pred[i]:
+            succ[p].append((i, late[p] + LAG))
+    last = {}
+    for i in sorted((i for i in range(n) if batch[i][8] is not None), key=lambda i: (batch[i][8], i)):
+        q = batch[i][0]
+        if q in last:
+            succ[last[q]].append((i, busy[last[q]]))
+            left[i] += 1
+        last[q] = i
+    topo, cnt = [i for i in range(n) if not left[i]], list(left)
+    for i in topo:
+        for j, _ in succ[i]:
+            cnt[j] -= 1
+            if not cnt[j]:
+                topo.append(j)
+    assert len(topo) == n
+    prio = [0.0] * n
+    for i in reversed(topo):
+        prio[i] = max([late[i]] + [d + prio[j] for j, d in succ[i]])
+    ready = {i: 0.0 for i in range(n) if not left[i]}
+    free, order, seen = {}, [], [0.0] * n
+
+    def start(i):
+        return max(free.get(batch[i][0], 0.0), ready[i])
+    while ready:
+        i = min(ready, key=lambda i: (round(start(i), 3), -prio[i], i))
+        q, t = batch[i][0], start(i)
+        for j in sorted((j for j in ready if batch[j][0] == q and t < start(j) < t + busy[i]), key=lambda j: (-prio[j], j)):
+            if max(start(j) + prio[j], start(j) + busy[j] + prio[i]) < max(t + prio[i], t + busy[i] + prio[j]) - 1e-6:
+                i = j
+                break
+        t = start(i)
+        del ready[i]
+        free[q] = t + busy[i]
+        order.append(i)
+        for j, d in succ[i]:
+            left[j] -= 1
+            seen[j] = max(seen[j], t + d)
+            if left[j] == 0:
+                ready[j] = seen[j]
+    return order
 
 
 def make_flow(g, T):
     queues = {"v": g.vector, "s": g.scalar, "t": g.tensor, "g": g, "y": g.sync}
     know = {q: {} for q in queues}
     total, clocks, writer, readers = {}, {}, {}, {}
-    batch, collect = [], [False]
+    batch = []
 
     def need(q, toks):
         worst = {}
@@ -52,86 +122,43 @@ def make_flow(g, T):
                 for k, n in clocks[(sem, val)].items():
                     know[q][k] = max(know[q].get(k, 0), n)
 
-    def deps(reads, writes):
-        toks = [writer[r] for r in reads if r in writer]
-        for w in writes:
-            if w in writer:
-                toks.append(writer[w])
-            toks += readers.get(w, [])
-        return toks
+    def op(q, calls, reads, writes, dur, sem=None, inc=1, late=None, at=None):
+        batch.append((q, calls, reads, writes, sem, inc, dur, dur if late is None else late, at))
 
-    def done(tok, reads, writes):
+    def issue(q, calls, reads, writes, sem, inc):
+        if q[0] == "x":
+            total[sem] = inc
+            clocks[(sem, inc)] = {sem: inc}
+            tok = (sem, inc)
+        else:
+            toks = [writer[r] for r in reads if r in writer]
+            for w in writes:
+                toks += ([writer[w]] if w in writer else []) + readers.get(w, [])
+            need(q, toks)
+            name = sem or "c" + q
+            for c in (calls if isinstance(calls, list) else [calls]):
+                if name == "lsend":
+                    c(queues[q])
+                else:
+                    c(queues[q]).then_inc(T.sem[name], inc)
+                total[name] = total.get(name, 0) + inc
+                clocks[(name, total[name])] = {**know[q], name: total[name]}
+            tok = (name, total[name])
         for r in reads:
             readers.setdefault(r, []).append(tok)
         for w in writes:
             writer[w] = tok
             readers[w] = []
 
-    def schedule():
-        lag = 0.12
-        w, rd, pred = {}, {}, []
-        for i, it in enumerate(batch):
-            p = {w[r] for r in it[2] if r in w}
-            for x in it[3]:
-                p |= ({w[x]} if x in w else set()) | rd.get(x, set())
-            for r in it[2]:
-                rd.setdefault(r, set()).add(i)
-            for x in it[3]:
-                w[x] = i
-                rd[x] = set()
-            pred.append(p - {i})
-        prio = [it[6] for it in batch]
-        for i in range(len(batch) - 1, -1, -1):
-            for p in pred[i]:
-                prio[p] = max(prio[p], batch[p][6] + lag + prio[i])
-        free, endt, left = {}, {}, list(range(len(batch)))
-        while left:
-            best = None
-            for i in left:
-                if all(p in endt for p in pred[i]):
-                    st = max([free.get(batch[i][0], 0.0)] + [endt[p] + lag for p in pred[i]])
-                    k = (round(st, 3), -prio[i], i)
-                    best = k if best is None or k < best else best
-            i = best[2]
-            left.remove(i)
-            endt[i] = best[0] + batch[i][6]
-            free[batch[i][0]] = endt[i]
-            issue(*batch[i][:6])
-        batch.clear()
-
-    def op(q, calls, reads, writes, sem=None, inc=1, dur=0.06):
-        if collect[0]:
-            batch.append((q, calls, reads, writes, sem, inc, dur))
-        else:
-            issue(q, calls, reads, writes, sem, inc)
-
-    def issue(q, calls, reads, writes, sem, inc):
-        remote = q == "r"
-        q = "g" if remote else q
-        need(q, deps(reads, writes))
-        name = sem or "c" + q
-        for c in (calls if isinstance(calls, list) else [calls]):
-            if remote:
-                c(queues[q])
-            else:
-                c(queues[q]).then_inc(T.sem[name], inc)
-            total[name] = total.get(name, 0) + inc
-            clocks[(name, total[name])] = {**know[q], name: total[name]}
-        done((name, total[name]), reads, writes)
-
-    def send(call, reads, lsem, n):
-        op("r", call, reads, [], lsem, n, 1.0)
-
-    def lands(names, sem, n):
-        total[sem] = n
-        clocks[(sem, n)] = {sem: n}
-        done((sem, n), [], list(names))
-
     def finish():
+        if not ORDER:
+            ORDER.extend(plan(batch))
+        for i in ORDER:
+            issue(*batch[i][:6])
         for sem, n in sorted(total.items()):
             if know["g"].get(sem, 0) < n:
                 g.wait_ge(T.sem[sem], n)
-    return op, send, lands, finish, collect, schedule
+    return op, finish
 
 
 def rank_program(g, core, T, topo):
@@ -139,306 +166,296 @@ def rank_program(g, core, T, topo):
     if rank is None:
         return
     N = len(T.cores)
-    op, send, lands, finish, collect, schedule = make_flow(g, T)
-
-    def V(fn, r, w, dur=0.06):
-        op("v", fn, r, w, dur=dur)
-
-    def G(fn, r, w):
-        op("g", fn, r, w)
-
-    def Sc(fn, r, w, dur=0.12):
-        op("s", fn, r, w, dur=dur)
-
-    op("y", lambda e: e.dma_start(T.jci[:], T.jc[:]), [], ["jci"], "ljc", 16)
-    op("s", lambda e: e.dma_start(T.sri[:], T.sr[:]), [], ["sri"], "lsr", 16)
-    op("y", lambda e: e.dma_start(T.pkt[:, 0:512], T.pk[:, 0:512]), [], ["pkt0"], "lpk0", 16)
-    op("s", lambda e: e.dma_start(T.fin0[:], T.fx[:]), [], ["fin0"], "lfx", 16)
-    op("y", lambda e: e.dma_start(T.pkt[:, 512:1024], T.pk[:, 512:1024]), [], ["pkt1"], "lpk1", 16)
-    op("s", lambda e: e.dma_start(T.rtt[:], T.rt[:]), [], ["rtt"], "lrt", 16)
-    for t in (1, 2):
-        lands(("fw%d" % t, "fws%d" % t), "rw%d" % t, len(topo.engines(T.cores[(rank - t) % N], core)))
-        lands(("fin%d" % t,), "rf%d" % t, len(topo.engines(T.cores[(rank - 1) % N], core)))
-
+    op, finish = make_flow(g, T)
     flag = {"allow_small_or_imprecise_dtypes": True}
-    G(lambda e: e.iota(T.pi[:], [[1, 1]], 0, 1), [], ["pi"])
-    G(lambda e: e.iota(T.io32[:], [[1, 32]], 0, 0), [], ["io32"])
-    V(lambda e: e.memset(T.onef[:], 1.0), [], ["onef"])
-    V(lambda e: e.memset(T.oneb[:], 1.0), [], ["oneb"])
-    G(lambda e: e.affine_select(T.bon[:], T.onef[:], [[-16, 8], [0, 16]], A.is_ge, 0.0, 0, 1), ["onef"], ["bon"])
-    G(lambda e: e.affine_select(T.bof[:], T.bon[:], [[16, 8], [0, 16]], A.is_ge, 0.0, 15, -1), ["bon"], ["bof"])
-    G(lambda e: e.affine_select(T.bo8[:], T.oneb[0:8, :], [[1, 128]], A.is_ge, 0.0, 0, -16), ["oneb"], ["bo8"])
-    G(lambda e: e.affine_select(T.bo8[:], T.bo8[:], [[-1, 128]], A.is_ge, 0.0, 15, 16), ["bo8"], ["bo8"])
-    G(lambda e: e.affine_select(T.idb[:], T.oneb[:], [[-1, 128]], A.is_equal, 0.0, 0, 1), ["oneb"], ["idb"])
-    G(lambda e: e.iota(T.jji[:], [[16, 4]], 0, 0), [], ["jji"])
-    G(lambda e: e.iota(T.eoi[:], [[16, 8], [128, 6]], 0, 0, **flag), [], ["eoi"])
-    G(lambda e: e.iota(T.dui[:], [[16, 8], [-128, 6]], 2048 + 640, 0, **flag), [], ["dui"])
-    G(lambda e: e.iota(T.fbi[:], [[0, 2], [256, 4]], 5 * 1024, 0, **flag), [], ["fbi"])
-    for h in "01":
-        G(lambda e: e.iota(T["fsp" + h][:], [[0, 1024]], 0, 0, **flag), [], ["fsp%s_%d" % (h, b) for b in range(4)])
-    V(lambda e: e.memset(T.sel[:], 0.0), [], ["sel"])
-    V(lambda e: e.tensor_scalar(T.yli[:], T.pi[:], 15, None, A.bitwise_and), ["pi"], ["yli"])
-    V(lambda e: e.memset(T.fmask[:], 1.0), [], ["fmask"])
-    V(lambda e: e.tensor_copy(T.ylf[:], T.yli[:]), ["yli"], ["ylf"])
-    V(lambda e: e.tensor_scalar(T.q2k[:], T.yli[:], 2048.0, None, A.mult), ["yli"], ["q2k"])
-    V(lambda e: e.tensor_scalar(T.y16[:], T.yli[:], 16.0, None, A.mult), ["yli"], ["y16"])
-    V(lambda e: e.tensor_scalar(T.w1[:], T.io32[:], T.ylf[:, 0:1], None, A.is_equal), ["io32", "ylf"], ["w1"])
-    V(lambda e: e.memset(T.fmask[:, 0::16], 0.0), ["fmask"], ["fmask"])
-    V(lambda e: e.memset(T.tab[:, 2048:], 0.0), [], ["tab"])
-    V(lambda e: e.memset(T.km[:], 0.0), [], ["km"])
-    SELK = ["sel%d" % y for y in range(16)]
-    for y in range(16):
-        Sc(lambda e: e.activation(T.sel[:, y, y::16], T.bof[:, 0::16], AF.Copy, scale=32768.0), ["bof", "sel"], ["sel%d" % y])
-    V(lambda e: e.tensor_scalar(T.jh[:], T.jci[:], 8, None, A.arith_shift_right), ["jci"], ["jh"])
-    V(lambda e: e.tensor_scalar(T.jl[:], T.jci[:], 255, None, A.bitwise_and), ["jci"], ["jl"])
-    V(lambda e: e.memset(T.km[:, 0::16], 1.0e9), ["km"], ["km"])
-    V(lambda e: e.tensor_copy(T.jlb[:], T.jl[:]), ["jl"], ["jlb"])
-    V(lambda e: e.tensor_scalar(T.jhb[:], T.jh[:], 256.0, T.q2k[:, 0:1], A.mult, A.add), ["jh", "q2k"], ["jhb"])
-    V(lambda e: e.tensor_copy(T.srb[:], T.sri[:]), ["sri"], ["srb"])
-    op("t", lambda e: e.matmul(T.pnew[:, 0:128], T.bo8[:], T.srb[:], True, True), ["bo8", "srb"], ["pnew"])
-    for q in range(16):
-        V(lambda e: e.tensor_scalar(T.jx0[:, :, q::16], T.jhb[:], T.w1[:, q:q + 1], None, A.mult), ["jhb", "w1"], ["jx0_%d" % q])
-        Sc(lambda e: e.activation(T.jx1[:, :, q::16], T.jlb[:], AF.Copy, scale=T.w1[:, q:q + 1]), ["jlb", "w1"], ["jx1_%d" % q])
-    V(lambda e: e.tensor_scalar(T.oh[:], T.pnew[:, 0:128], T.ylf[:, 0:1], None, A.is_equal), ["pnew", "ylf"], ["oh"])
-    V(lambda e: e.tensor_tensor(T.ms[:, 0:128], T.oh[:], T.jhb[:], A.mult), ["oh", "jhb"], ["ms0"])
-    V(lambda e: e.tensor_tensor(T.ms[:, 128:256], T.oh[:], T.jlb[:], A.mult), ["oh", "jlb"], ["ms1"])
-    op("t", [lambda e, y=y: e.matmul(T.pd1[:, 0:16], T.sel[:, y, :], T.ms[:, y::16], y == 0, y == 15)
-             for y in range(16)], SELK + ["ms0", "ms1"], ["pd1"])
-    Sc(lambda e: e.activation(T.fw0[:, 256:272], T.pd1[:, 0:16], AF.Copy, scale=1.0 / 32768.0), ["pd1"], ["fws0"])
-    for i, b in enumerate(("jx0", "jx1")):
-        op("t", [lambda e, y=y: e.matmul(T.pd0[:, i * 128:(i + 1) * 128], T.sel[:, y, :], T[b][:, :, y * 16:y * 16 + 16], y == 0, y == 15)
-                 for y in range(16)], SELK + ["%s_%d" % (b, q) for q in range(16)], ["pd0"])
-    V(lambda e: e.memset(T.segm[:], 1.0), [], ["segm"])
-    V(lambda e: e.tensor_scalar(T.jj[:], T.jji[:], T.ylf[:, 0:1], None, A.add), ["jji", "ylf"], ["jj"])
-    V(lambda e: e.tensor_scalar(T.fb[:], T.fbi[:], T.y16[:, 0:1], 1.0 / 1024.0, A.add, A.mult), ["fbi", "y16"], ["fb"])
-    V(lambda e: e.tensor_scalar(T.q6[:], T.jj[:], 1.0 / 6.0, -2.5 / 6.0, A.mult, A.add), ["jj"], ["q6"])
-    V(lambda e: e.tensor_scalar(T.q8[:], T.jj[:], 0.125, -3.5 / 8.0, A.mult, A.add), ["jj"], ["q8"])
-    V(lambda e: e.memset(T.segm[:, 0::6], 0.0), ["segm"], ["segm"])
-    V(lambda e: e.tensor_copy(T.q6f[:], T.q6[:]), ["q6"], ["q6f"])
-    V(lambda e: e.tensor_copy(T.q8f[:], T.q8[:]), ["q8"], ["q8f"])
-    for i, (a, b, c, q) in enumerate(LISTS):
-        Sc(lambda e: e.activation(T.la[:, 4 * i:4 * i + 4], T.jj[:], AF.Copy, scale=float(a), bias=float(c)), ["jj"], ["la%d" % i])
-        Sc(lambda e: e.activation(T.lb[:, 4 * i:4 * i + 4], T[q + "f"][:], AF.Copy, scale=float(b)), [q + "f"], ["lb%d" % i])
-    Sc(lambda e: e.activation(T.fw0[:, 0:256], T.pd0[:, 0:256], AF.Copy, scale=1.0 / 32768.0), ["pd0"], ["fw0"])
-    Sc(lambda e: e.activation(T.idn[:], T.idb[:], AF.Copy, scale=-1.0), ["idb"], ["idn"])
-    for t in (1, 2):
+    HS = (0, 1)
+
+    def V(fn, r, w, n=64, at=None):
+        op("v", fn, r, w, max(64, n) * CYC, at=at)
+
+    def Sc(fn, r, w, n=64, at=None):
+        op("s", fn, r, w, 0.065 + max(64, n) * CYC, at=at)
+
+    def VG(fn, r, w, n, rate=GATH, at=None):
+        op("v", fn, r, w, 0.05 + rate * n * CYC, at=at)
+
+    def SG(fn, r, w, n, at=None):
+        op("s", fn, r, w, 0.065 + GATH * n * CYC, at=at)
+
+    def G(fn, r, w, n):
+        op("g", fn, r, w, 0.17 + 2 * n * CYC)
+
+    def PEn(calls, r, w, n, at=None):
+        op("t", calls, r, w, n * PE, at=at)
+
+    def dma(q, dst, src, r, w, sem, late, at=None):
+        op(q, lambda e: e.dma_start(dst, src), r, w, 0.05, sem, 16, late, at)
+
+    def send(dst_ap, src_ap, r, t, sem, lands):
         dst = T.cores[(rank + t) % N]
         rid, pid = topo.addr(dst, core)
-        send(lambda e: e.remote_dma(T["fw%d" % t][:], T.fw0[:], T.sem["rw%d" % t], T.sem.lsend, pid, rid, topo.mask(core, dst)),
-             ["fw0", "fws0"], "lsend", len(topo.engines(core, dst)))
-    for n in ("eq", "c48", "cl", "cd", "fv"):
-        G(lambda e: e.iota(T[n][:], [[0, T[n].shape[1]]], 0, 0, **flag), [], [n])
-    G(lambda e: e.iota(T.pri[:], [[0, 48]], 0, 0), [], ["pri"])
-    G(lambda e: e.iota(T.hx[:, 0, 40:48], [[0, 8]], 0, 0), [], ["hx5"])
-    for h in "01":
-        G(lambda e: e.iota(T["fr" + h][:, 5120:6144], [[0, 1024]], 0, 0, **flag), [], ["fr%s_5_%d" % (h, b) for b in range(4)])
-    TABK = ["tab"] + ["tab%d%d" % (i, j) for i in range(2) for j in range(2)]
+        op("g", lambda e: e.remote_dma(dst_ap, src_ap, T.sem[sem], T.sem.lsend, pid, rid, topo.mask(core, dst)),
+           r, ["@" + sem], 0.3, "lsend", len(topo.engines(core, dst)), 0.3)
+        op("x" + sem, None, ["@" + sem], lands, 1.5, sem, len(topo.engines(T.cores[(rank - t) % N], core)))
+
+    dma("y", T.jci[:, 0:128], T.jc[:], [], ["jci"], "ljc", 1.2, -9)
+    dma("s", T.jci[:, 128:144], T.jc[:, 0:16], [], ["jcw"], "ljw", 1.2, -9)
+    dma("s", T.sri[:], T.sr[:], [], ["sri"], "lsr", 1.2, -8)
+    dma("y", T.pkt[:, 0:512], T.pk[:, 0:512], [], ["pkt0"], "lpk0", 1.8, -8)
+    dma("s", T.pkt[:, 512:1024], T.pk[:, 512:1024], [], ["pkt1"], "lpk1", 2.5, -7)
+    dma("y", T.fin0[:], T.fx[:], [], ["fin00", "fin01"], "lfx", 2.6, -7)
+    dma("y", T.rtt[:], T.rt[:], [], ["rtt"], "lrt0", 4.5, -6)
+
+    G(lambda e: e.iota(T.pi[:], [[1, 1]], 0, 1), [], ["pi"], 1)
+    G(lambda e: e.iota(T.i144[:], [[1, 144]], 0, 0), [], ["i144"], 144)
+    V(lambda e: e.memset(T.negf[:], -1.0), [], ["negf"], 128)
+    V(lambda e: e.memset(T.oneb[:], 1.0), [], ["oneb"])
+    V(lambda e: e.memset(T.ndi[:], -1.0), [], ["ndi"], 512)
+    G(lambda e: e.affine_select(T.bon[:], T.negf[:], [[-16, 8], [0, 16]], A.is_ge, 0.0, 0, 1), ["negf"], ["bon"], 128)
+    G(lambda e: e.affine_select(T.bon[:], T.bon[:], [[16, 8], [0, 16]], A.is_ge, 0.0, 15, -1), [], ["bon"], 128)
+    G(lambda e: e.affine_select(T.bo8[:], T.oneb[0:8, :], [[1, 8], [0, 16]], A.is_equal, 0.0, 0, -1), ["oneb"], ["bo8"], 128)
+    G(lambda e: e.affine_select(T.idb[:], T.oneb[:], [[-1, 128]], A.is_equal, 0.0, 0, 1), ["oneb"], ["idb"], 128)
+    G(lambda e: e.affine_select(T.ide[:], T.idb[:], [[0, 4], [-1, 2], [0, 16]], A.is_ge, 0.0, 0, 0), ["idb"], ["ide"], 128)
+    V(lambda e: e.tensor_tensor(T.ido[:], T.idb[:], T.ide[:], A.subtract), ["idb", "ide"], ["ido"], 256)
+    ND = ["nd%d" % b for b in range(4)]
+    for b in range(4):
+        G(lambda e, b=b: e.affine_select(T.nd[:, 256 * b:256 * b + 256], T.ndi[:, 256 * b:256 * b + 256], [[-1, 4], [-16, 4], [0, 16]],
+                                         A.is_equal, 0.0, -4 * b, 1), ["ndi"], [ND[b]], 256)
+    G(lambda e: e.iota(T.cst[0:32, :], [[16, 4], [0, 16]], 0, 0, **flag), [], ["cst0"], 64)
+    V(lambda e: e.memset(T.cst[32:64, :], -7680.0), [], ["cst1"])
+    V(lambda e: e.memset(T.c64[:], 64.0), [], ["c64"])
+    V(lambda e: e.tensor_scalar(T.yli[:], T.pi[:], 15, None, A.bitwise_and), ["pi"], ["yli"])
+    V(lambda e: e.tensor_copy(T.ylf[:], T.yli[:]), ["yli"], ["ylf"])
+    V(lambda e: e.tensor_scalar(T.q2k[:], T.yli[:], 2048.0, None, A.mult), ["yli"], ["q2k"])
+    V(lambda e: e.tensor_scalar(T.y64[:], T.yli[:], 64.0, None, A.mult), ["yli"], ["y64"])
+    V(lambda e: e.tensor_scalar(T.g15[:], T.pi[:], T.ylf[:, 0:1], 15.0, A.subtract, A.add), ["pi", "ylf"], ["g15"])
+    V(lambda e: e.tensor_scalar(T.selb[:], T.i144[:], T.g15[:, 0:1], 131072.0, A.is_equal, A.mult), ["i144", "g15"], ["sel"], 144)
+    V(lambda e: e.memset(T.km[:], -1.0e9), [], ["km"])
+    V(lambda e: e.memset(T.km[:, 0::16], 1.0e9), ["km"], ["km"])
+    G(lambda e: e.iota(T.cxh[:], [[0, 2], [1, 4]], 0, 0, **flag), [], ["cxh"], 8)
+    Sc(lambda e: e.activation(T.cxh[:], T.cxh[:], AF.Copy, scale=32768.0), ["cxh"], ["cxh"])
+    G(lambda e: e.iota(T.pp[:, :, 0:4], [[0, 32]], -1000, 0), [], ["ppad"], 32)
+    G(lambda e: e.iota(T.tab[:, 2048:], [[0, NDUM]], 0, 0, **flag), [], ["tabd"], NDUM)
+
+    def sel(y):
+        return T.selb[:, 15 - y:143 - y]
+
+    V(lambda e: e.tensor_scalar(T.i80[:], T.i144[:, 0:80], 79, None, A.bitwise_and), ["i144"], ["i80"], 80)
+    V(lambda e: e.tensor_scalar(T.w1[:], T.i80[:], T.ylf[:, 0:1], None, A.is_equal), ["i80", "ylf"], ["w1"], 80)
+    Sc(lambda e: e.activation(T.w1c[:], T.w1[:], AF.Copy, scale=-1.0, bias=1.0), ["w1"], ["w1c"], 80)
+    G(lambda e: e.iota(T.m25[:], [[0, 200]], 1, 0, **flag), [], ["m25"], 200)
+    for n, width, cases, last in (("m5a", 5, 8, 0), ("m5b", 5, 8, 1), ("m8a", 8, 4, 0), ("m8b", 8, 4, 1)):
+        G(lambda e, n=n, width=width, cases=cases, last=last: e.affine_select(
+            T[n][:], T.m25[:, 0:width * cases], [[0, cases], [1, width]], A.is_gt, 0.0, -last, 0), ["m25"], [n], 40)
+    for i in (4, 5):
+        G(lambda e, i=i: e.iota(T.m25[:, i::25], [[0, 8]], 0, 0, **flag), [], ["m25"], 8)
+    for n, size, value in (("eq", 200, 0), ("cl", 40, 0), ("rr", 41, 0), ("w5", 41, -1000), ("cep", 64, 0), ("pm", 64, 0), ("dum", 40, 0),
+                           ("cod", 72, 0), ("so", 48, 0)):
+        G(lambda e, n=n, size=size, value=value: e.iota(T[n][:], [[0, size]], value, 0, **flag), [], [n + "0"], size)
+    G(lambda e: e.iota(T.ad[:, 0:1], [[0, 1]], 0, 0), [], ["ad"], 1)
+    G(lambda e: e.iota(T.zc[:], [[0, 1]], 1, 0, **flag), [], ["zc"], 1)
+    G(lambda e: e.iota(T.dui[:], [[80, 8], [16, 5]], 2048, 0, **flag), [], ["dui"], 40)
+    G(lambda e: e.iota(T.cei[:], [[0, 2], [-16, 4], [-64, 5]], 319, 0, **flag), [], ["cei"], 40)
+    G(lambda e: e.iota(T.l5i[:], [[20, 2], [4, 2]], 0, 0), [], ["l5i"], 4)
+    G(lambda e: e.iota(T.l8i[:], [[32, 2], [4, 2]], 3, 0), [], ["l8i"], 4)
+    V(lambda e: e.tensor_scalar(T.yi[:, 0:1], T.pi[:], 3, None, A.bitwise_and), ["pi"], ["ya"])
+    V(lambda e: e.tensor_scalar(T.yi[:, 1:2], T.pi[:], 2, 3, A.arith_shift_right, A.bitwise_and), ["pi"], ["yb"])
+    Sc(lambda e: e.activation(T.ybf[:], T.yi[:, 1:2], AF.Copy), ["yb"], ["ybf"])
+    for n, k in (("5", 5.0), ("8", 8.0)):
+        Sc(lambda e, n=n, k=k: e.activation(T["y" + n][:], T.yi[:, 0:1], AF.Identity, bias=T.ybf[:, 0:1], scale=k), ["ya", "ybf"], ["y" + n])
+        V(lambda e, n=n: e.tensor_scalar(T["l" + n][:], T["l%si" % n][:], T["y" + n][:, 0:1], None, A.add), ["l%si" % n, "y" + n], ["l" + n])
+    G(lambda e: e.iota(T.bsi[:], [[0, 2], [-16, 4]], 63, 0, **flag), [], ["bsi"], 8)
+    G(lambda e: e.iota(T.lbi[:], [[10, 4]], 4, 0), [], ["lbi"], 4)
+    Sc(lambda e: e.activation(T.dum[:, :, 1:5], T.dui[:, :, 1:5], AF.Identity, bias=T.ylf[:, 0:1]), ["dui", "ylf", "dum0"], ["dum"])
+    V(lambda e: e.tensor_scalar(T.ce[:], T.cei[:], T.ylf[:, 0:1], 1.0 / 64, A.subtract, A.mult), ["cei", "ylf"], ["ce"])
+    V(lambda e: e.tensor_scalar(T.eq[:, 4::25], T.bsi[:], T.ylf[:, 0:1], 1.0 / 64, A.subtract, A.mult), ["bsi", "ylf", "eq0"], ["eq5"])
+    V(lambda e: e.tensor_scalar(T.hz[:, 0:1], T.ylf[:], 8.0, 5.0, A.is_ge, A.mult), ["ylf"], ["h8"])
+    V(lambda e: e.tensor_scalar(T.yi[:, 2:3], T.pi[:], 7, None, A.bitwise_and), ["pi"], ["y8i"])
+    V(lambda e: e.tensor_scalar(T.hz[:, 1:2], T.yi[:, 2:3], 0.0, 40.0, A.is_equal, A.mult), ["y8i"], ["z40"])
+    V(lambda e: e.tensor_scalar(T.lb[:], T.lbi[:], T.hz[:, 0:1], T.hz[:, 1:2], A.add, A.max), ["lbi", "h8", "z40"], ["lb"])
+
+    V(lambda e: e.tensor_scalar(T.jh[:], T.jci[:], 8, None, A.arith_shift_right), ["jci", "jcw"], ["jh"], 144)
+    V(lambda e: e.tensor_scalar(T.jl[:], T.jci[:], 255, None, A.bitwise_and), ["jci", "jcw"], ["jl"], 144)
+    Sc(lambda e: e.activation(T.jlb[:], T.jl[:], AF.Copy), ["jl"], ["jlb"], 144)
+    V(lambda e: e.tensor_scalar(T.jhb[:], T.jh[:], 256.0, T.q2k[:, 0:1], A.mult, A.add), ["jh", "q2k"], ["jhb"], 144)
+    for i, b in enumerate(("jhb", "jlb")):
+        V(lambda e, i=i, b=b: e.transpose(T.tra[:, i], T[b][:, 0:128]), [b], ["tra%d" % i])
+        V(lambda e, i=i, b=b: e.transpose(T.trb[:, i], T[b][:, 16:144]), [b], ["trb%d" % i])
+    calls = []
+    for i in range(2):
+        o = 64 * i
+        calls += [lambda e, i=i, o=o: e.matmul(T.pd0[:, o:o + 64], T.ide[:], T.tra[:, i, :, 0:16], True, False),
+                  lambda e, i=i, o=o: e.matmul(T.pd0[:, o + 16:o + 64], T.ido[:], T.trb[:, i, 0:3, 16:32], False, False),
+                  lambda e, i=i, o=o: e.matmul(T.pd0[:, o:o + 16], T.ido[:], T.trb[:, i, 3, 16:32], False, True),
+                  lambda e, i=i, o=o: e.matmul(T.pd0[:, 128 + o:192 + o], T.ide[:], T.trb[:, i, :, 0:16], True, False),
+                  lambda e, i=i, o=o: e.matmul(T.pd0[:, 128 + o:192 + o], T.ido[:], T.tra[:, i, :, 16:32], False, True)]
+    PEn(calls, ["ide", "ido", "tra0", "tra1", "trb0", "trb1"], ["pd0"], 640)
+    Sc(lambda e: e.activation(T.fw0[:, 0:16:2, :], T.pd0[:, 0:128], AF.Copy), [], ["pd0", "fw0a"], 128)
+    Sc(lambda e: e.activation(T.fw0[:, 1:16:2, :], T.pd0[:, 128:256], AF.Copy), [], ["pd0", "fw0b"], 128)
+    Sc(lambda e: e.activation(T.srb[:], T.sri[:], AF.Copy), ["sri"], ["srb"], 128)
+    PEn(lambda e: e.matmul(T.pmis[:, 0:128], T.bo8[:], T.srb[:], True, True), ["bo8", "srb"], ["pmis"], 128)
+    V(lambda e: e.tensor_scalar(T.oh[:], T.pmis[:, 0:128], T.ylf[:, 0:1], None, A.is_equal), ["ylf"], ["pmis", "oh"], 128)
+    V(lambda e: e.tensor_tensor(T.ms[:, 0:128], T.oh[:], T.jhb[:, 0:128], A.mult), ["oh", "jhb"], ["ms0"], 256)
+    V(lambda e: e.tensor_tensor(T.ms[:, 128:256], T.oh[:], T.jlb[:, 0:128], A.mult), ["oh", "jlb"], ["ms1"], 256)
+    PEn([lambda e, y=y: e.matmul(T.pd1[:, 0:16], sel(y), T.ms[:, y::16], y == 0, y == 15) for y in range(16)],
+        ["sel", "ms0", "ms1"], ["pd1"], 1024)
+    Sc(lambda e: e.activation(T.fw0[:, 16, :], T.pd1[:, 0:16], AF.Copy, scale=1.0 / 131072.0), [], ["pd1", "fw0s"])
+    for t in (1, 2):
+        send(T["fw%d" % t][:], T.fw0[:], ["fw0a", "fw0b", "fw0s"], t, "rw%d" % t, ["fw%d%s" % (t, x) for x in "abs"])
+    TAB = ["tabd"] + ["tab%d%d" % (i, j) for i in range(2) for j in range(2)]
     for i in range(2):
         a, b = 512 * i, 512 * i + 512
-        V(lambda e: e.tensor_scalar(T.tmpi[:, a:b], T.pkt[:, a:b], 4095, None, A.bitwise_and), ["pkt%d" % i], ["tmpi%d" % i])
-        V(lambda e: e.tensor_scalar(T.pkt[:, a:b], T.pkt[:, a:b], 12, None, A.arith_shift_right), ["pkt%d" % i], ["pkt%d" % i])
-        V(lambda e: e.tensor_copy(T.tab[:, a:b], T.tmpi[:, a:b]), ["tmpi%d" % i], ["tab%d0" % i])
-        V(lambda e: e.tensor_copy(T.tab[:, 1024 + a:1024 + b], T.pkt[:, a:b]), ["pkt%d" % i], ["tab%d1" % i])
+        V(lambda e, a=a, b=b: e.tensor_scalar(T.tmpi[:, a:b], T.pkt[:, a:b], 4095, None, A.bitwise_and), ["pkt%d" % i], ["tmpi%d" % i], 512)
+        V(lambda e, a=a, b=b: e.tensor_scalar(T.pkt[:, a:b], T.pkt[:, a:b], 12, None, A.arith_shift_right), [], ["pkt%d" % i], 512)
+        Sc(lambda e, a=a, b=b: e.activation(T.tab[:, a:b], T.tmpi[:, a:b], AF.Copy), ["tmpi%d" % i], ["tab%d0" % i], 512)
+        Sc(lambda e, a=a, b=b: e.activation(T.tab[:, 1024 + a:1024 + b], T.pkt[:, a:b], AF.Copy), ["pkt%d" % i], ["tab%d1" % i], 512)
 
-    HXA = ["hxa0", "hxa1"]
-    HXB = ["hxb0", "hxb1"]
+    def place(t, s, h):
+        base = 100.0 * t + PERIOD * (2 * s + h)
+        return lambda name: base + PLACE[name]
 
-    def start_keys(t):
-        fw = "fw%d" % t
-        V(lambda e: e.tensor_tensor(T.sk[:], T[fw][:, 256:264], T[fw][:, 264:272], A.add), ["fws%d" % t], ["sk"])
-        V(lambda e: e.tensor_scalar(T.hx[:, 0, 0:8], T.sk[:], 2047, None, A.bitwise_and), ["sk"], HXA)
-        V(lambda e: e.tensor_scalar(T.hx[:, 1, 0:8], T.sk[:], 11, 15, A.arith_shift_right, A.bitwise_and), ["sk"], HXB)
-        for h in "01":
-            lo = 4 * int(h)
-            V(lambda e, h=h, lo=lo: e.tensor_copy(T["lst" + h][:], T.hx[:, 0, lo:lo + 4]), ["hxa" + h], ["lst" + h])
-
-    def start_facts(h, t):
-        fin = "fin%d" % t
-        lo = 64 * int(h)
-        Sc(lambda e: e.activation(T["fsp" + h][:, 0::16], T[fin][:, lo:lo + 64], AF.Copy), [fin], ["fsp%s_%d" % (h, b) for b in range(4)])
-
-    def entries(h):
-        V(lambda e: e.tensor_copy(T["eu" + h][:], T.tab[:].indirect(T["lst" + h][:])), TABK + ["lst" + h], ["eu" + h])
-
-    def spread(h, s):
-        for x, a, b in (("a", 0, 256), ("b", 256, 1024)):
-            V(lambda e: e.tensor_tensor_scan(T["fr" + h][:, 1024 * s + a:1024 * s + b], T.fmask[:, a:b], T["fsp" + h][:, a:b], 0.0, A.mult, A.add),
-              ["fmask"] + ["fsp%s_%d" % (h, i) for i in range(4)], ["fr%s_%d%s" % (h, s, x)])
-
-    def post(h, s):
-        lo = 64 * int(h)
-        c = s * 8 + 4 * int(h)
-        key = T.sch[:, s - 1, lo + 15:lo + 64:16]
-        sch, lst, lf = "sch%d%s" % (s, h), "lst" + h, "lf" + h
-        V(lambda e: e.tensor_tensor_scan(T.sch[:, s - 1, lo:lo + 64], T.km[:], T["kp" + h][:, 0:64], 0.0, A.max, A.min),
-          ["km", "kp" + h], [sch])
-        V(lambda e: e.tensor_scalar(T.hx[:, 1, c:c + 4], key, 11, 15, A.arith_shift_right, A.bitwise_and), [sch], ["hxb" + h])
+    def choice(h, s, t):
+        c, at = slice(4 * h, 4 * h + 4), place(t, s, h)
+        key, sch = T.sch[:, 64 * h + (15 if s else 14):64 * h + 64:16, s], "sch%d%d" % (s, h)
+        row, rn = (T.pp[:, c, s + 4], "pp%d%d" % (s, h)) if s < S else (T.p5[:, c], "p5%d" % h)
+        if s == 0 or s == S:
+            def at(name):
+                return None
+        V(lambda e: e.tensor_scalar(row, key, 11, 63, A.arith_shift_right, A.bitwise_and), [sch], [rn], at=at("row"))
         if s < S:
-            V(lambda e: e.tensor_scalar(T.hx[:, 0, c:c + 4], key, 2047, None, A.bitwise_and), [sch], ["hxa" + h])
-        V(lambda e: e.tensor_scalar(T[lf][:, 0::2], T.hx[:, 1, c:c + 4], T.y16[:, 0:1], None, A.add), ["hxb" + h, "y16"], [lf])
-        if s < S:
-            V(lambda e: e.tensor_copy(T[lst][:], T.hx[:, 0, c:c + 4]), ["hxa" + h], [lst])
-            dst, o, fk = T["fsp" + h], 0, "fsp%s_" % h
+            V(lambda e: e.tensor_scalar(T.cc[:, c, s], key, 2047, None, A.bitwise_and), [sch], ["cc%d%d" % (s, h)], at=at("court"))
+            V(lambda e: e.tensor_copy(T["lst%d" % h][:, 0::2], T.cc[:, c, s]), ["cc%d%d" % (s, h)], ["lst%d" % h], at=at("lst"))
+        if s:
+            V(lambda e: e.tensor_scalar(T["lf%d" % h][:], row, T.y64[:, 0:1], None, A.add), [rn, "y64"], ["lf%d" % h], at=at("lf"))
+            SG(lambda e: e.activation(T["fh%d" % h][:, 64 * s - 64:64 * s], T["ab%d" % h][:].indirect(T["lf%d" % h][:]), AF.Copy),
+               ["lf%d" % h] + ["ab%d_%d" % (h, y) for y in range(16)], ["fh%d_%d" % (h, s)], 64, at=at("fh"))
+
+    def step(h, s, t):
+        eu, rg, ab, kp, ft, fw = "eu%d" % h, "rg%d" % h, "ab%d" % h, "kp%d" % h, "ft%d" % h, "fw%d" % t
+        c, at = slice(4 * h, 4 * h + 4), place(t, s - 1, h)
+        op("v", [lambda e, i=i: e.tensor_copy(T[eu][:, i::4], T.tab[:].indirect(T["lst%d" % h][:, 2 * i:2 * i + 1])) for i in range(4)],
+           TAB + ["lst%d" % h], [eu], 4 * (0.05 + GATH * 16 * CYC), at=at("eu"))
+        src, sn = (T["fin%d" % t][:, 64 * h:64 * h + 64], "fin%d%d" % (t, h)) if s == 1 else (
+            T["fh%d" % h][:, 64 * s - 128:64 * s - 64], "fh%d_%d" % (h, s - 1))
+        PEn(lambda e: e.transpose(T.pft[0:64, 0:128], src, T.idb[:]), [sn, "idb"], ["pft"], 128, at=at("turn"))
+        V(lambda e: e.tensor_copy(T[ft][:], T.pft[0:64, 0:128]), [], ["pft", ft], at=at("ft"))
+        PEn([lambda e: e.matmul(T[kp][:, 0:64], T.c64[:], T.cst[:], True, False),
+             lambda e: e.matmul(T[kp][:, 0:64], T.idb[:], T[fw][:, 4 * h:4 * h + 4, :], False, False),
+             lambda e: e.matmul(T[kp][:, 0:64], T.idb[:], T[fw][:, 8 + 4 * h:12 + 4 * h, :], False, False)],
+            ["c64", "cst0", "cst1", "idb", fw + "a", fw + "b"], [kp], 192, at=at("pay"))
+        for i, (q, y0, y1) in enumerate(GATHERS):
+            col, lst, rk = slice(64 * y0, 64 * y1), T[eu][:, 4 * y0:4 * y1], [rg + "_%d" % y for y in range(y0, y1)]
+            if q == "s":
+                SG(lambda e, col=col, lst=lst: e.activation(T[rg][:, col], T.rtt[:].indirect(lst), AF.Copy), ["rtt", eu], rk,
+                   64 * (y1 - y0), at=at("g%d" % i))
+            else:
+                VG(lambda e, col=col, lst=lst: e.tensor_copy(T[rg][:, col], T.rtt[:].indirect(lst)), ["rtt", eu], rk,
+                   64 * (y1 - y0), at=at("g%d" % i))
+        for b, (y0, y1) in enumerate(BANKS):
+            col, pd, n, keys = slice(64 * y0, 64 * y1), "pd%d" % b, 64 * (y1 - y0), range(y0, y1)
+            rk, ak = [rg + "_%d" % y for y in keys], [ab + "_%d" % y for y in keys]
+            PEn(lambda e, col=col, pd=pd, n=n: e.matmul(T[pd][:, 0:n], T[ft][:], T.nd[:, col], True, False), [ft] + ND, [pd], n,
+                at=at("n%d" % b))
+            PEn(lambda e, col=col, pd=pd, n=n: e.matmul(T[pd][:, 0:n], T.idb[:], T[rg][:, col], False, True), ["idb"] + rk, [pd], n,
+                at=at("i%d" % b))
+            Sc(lambda e, col=col, pd=pd, n=n: e.activation(T[ab][:, col], T[pd][:, 0:n], AF.Abs), [], [pd] + ak, n, at=at("a%d" % b))
+            PEn([lambda e, y=y: e.matmul(T[kp][:, 0:64], sel(y), T[ab][:, 64 * y:64 * y + 64], False, y == BANKS[-1][1] - 1)
+                 for y in keys], ["sel"] + ak, [kp], n, at=at("m%d" % b))
+        V(lambda e: e.tensor_tensor_scan(T.sch[:, 64 * h:64 * h + 64, s], T.km[:], T[kp][:, 0:64], 0.0, A.max, A.min), ["km"], [kp, "sch%d%d" % (s, h)],
+          at=place(t, s, h)("scan"))
+
+    def both(name, steps):
+        return ["%s%d%d" % (name, s, h) for s in steps for h in HS]
+
+    def early(t):
+        PP = both("pp", range(S)) + ["ppad"]
+        for d in range(1, 5):
+            V(lambda e, d=d: e.tensor_tensor(T.eq[:, d - 1::5], T.pp[:, :, 4:9], T.pp[:, :, 4 - d:9 - d], A.is_equal),
+              PP + ["eq0"], ["eq%d" % d], 80)
+        V(lambda e: e.tensor_tensor_scan(T.cs[:], T.m25[:], T.eq[:], 0.0, A.mult, A.max),
+          ["m25"] + ["eq%d" % d for d in range(6)], ["cs"], 200)
+        V(lambda e: e.tensor_tensor(T.tq[:], T.cs[:, 4::5], T.dum[:], A.mult), ["cs", "dum"], ["tq"], 80)
+        V(lambda e: e.tensor_tensor(T.so[:, 0:40], T.tq[:], T.cc[:], A.max), ["tq", "so0"] + both("cc", range(S)), ["so"], 80)
+        VG(lambda e: e.tensor_copy(T.soff[:], T.so[:].indirect(T.l5[:])), ["so", "l5"], ["soff"], 64)
+        for h in HS:
+            SG(lambda e, h=h: e.activation(T.eall[:, 320 * h:320 * h + 320], T.tab[:].indirect(T.soff[:, 32 * h:32 * h + 20]), AF.Copy),
+               TAB + ["soff"], ["eall%d" % h], 320)
+        V(lambda e: e.tensor_tensor_scan(T.sm[:], T.m5a[:], T.cs[:, 4::5], 0.0, A.mult, A.add), ["m5a", "cs"], ["sm"])
+        V(lambda e: e.tensor_scalar(T.fl[:], T.sm[:, 4::5], -64.0, 319.0, A.mult, A.add), ["sm"], ["fl"])
+        Sc(lambda e: e.activation(T.cep[:, :, 0], T.sm[:, 4::5], AF.Copy), ["sm", "cep0"], ["ceps"])
+        Sc(lambda e: e.activation(T.ppf[:], T.pp[:, :, 1:9], AF.Copy), PP, ["ppf"])
+        V(lambda e: e.tensor_tensor(T.cl[:, 1:40], T.cs[:, 9::5], T.cs[:, 4:195:5], A.is_gt), ["cs", "cl0"], ["cl"], 80)
+        V(lambda e: e.tensor_tensor(T.clp[:], T.cl[:], T.pp[:, :, 4:9], A.mult), ["cl"] + PP, ["clp"], 80)
+        V(lambda e: e.tensor_tensor_scan(T.rr[:, 0:40], T.m5b[:], T.clp[:], 0.0, A.mult, A.subtract), ["m5b", "clp", "rr0"], ["rr"])
+        VG(lambda e: e.tensor_tensor(T.qq[:], T.rr[:].indirect(T.lb[:]), T.ppf[:], A.add), ["rr", "lb", "ppf"], ["qq"], 64)
+        Sc(lambda e: e.activation(T.ncc[:], T.cs[:, 24::25], AF.Copy, scale=-1.0, bias=1.0), ["cs"], ["ncc"])
+        V(lambda e: e.tensor_scalar(T.dd[:], T.sch[:, 15::16, 0:5], 17, None, A.arith_shift_right), ["d0"] + both("sch", range(1, S)), ["dd"])
+        V(lambda e: e.tensor_tensor(T.ad[:, 1:40], T.dd[:, 1:40], T.dd[:, 0:39], A.add), ["dd"], ["ad"], 80)
+        V(lambda e: e.tensor_scalar(T.ad[:], T.ad[:], T.zc[:, 0:1], None, A.add), ["zc"], ["ad"])
+        V(lambda e: e.tensor_scalar(T.pri[:], T.ad[:], 1, None, A.bitwise_and), ["ad"], ["pri"])
+        V(lambda e: e.tensor_tensor(T.cep[:, :, 3:7], T.pri[:, :, 1:5], T.ce[:, :, 0:4], A.mult), ["pri", "ce", "cep0"], ["cep"])
+        Sc(lambda e: e.activation(T.pm[:, :, 3:7], T.pp[:, :, 5:9], AF.Copy, bias=-64.0), PP + ["pm0"], ["pma"])
+
+    def late(h, t):
+        c, n, w = slice(4 * h, 4 * h + 4), str(h), slice(320 * h, 320 * h + 320)
+        x = slice(64 * h, 64 * h + 64)
+        fout, fn = T.fout[:, 128 * t + 64 * h:128 * t + 64 * h + 64], "fout%d%d" % (t, h)
+        SG(lambda e: e.activation(fout, T["fh" + n][:].indirect(T.fl[:, c]), AF.Copy),
+           ["fl"] + ["fh%d_%d" % (h, s) for s in range(1, S + 1)], [fn], 64)
+        if t == VI - 1:
+            dma("y", T.yf[:, x], fout, [fn], ["yf" + n], "oyf" + n, 1.5)
         else:
-            dst, o, fk = T["fr" + h], 5120, "fr%s_5_" % h
-        for b in range(4):
-            win = T["dr" + h][:, 256 * b:256 * b + 256] if b < 3 else T["ab" + h][:, 3, :]
-            Sc(lambda e, b=b, win=win: e.activation(dst[:, o + 256 * b:o + 256 * b + 256:16], win.indirect(T[lf][:, 2 * b:2 * b + 1]), AF.Abs),
-               [("dr%sc0", "dr%sc1", "dr%sc2", "ab%s3")[b] % h, lf], [fk + str(b)])
+            send(T["fin%d" % (t + 1)][:, x], fout, [fn], 1, "rf%d%d" % (t + 1, h), ["fin%d%d" % (t + 1, h)])
+        z = slice(32 * h, 32 * h + 32)
+        V(lambda e: e.tensor_tensor(T.w5[:, 20 * h + 4:20 * h + 20:5], T.p5[:, c], T.ncc[:, c], A.mult), ["p5" + n, "ncc", "w50"], ["w5"])
+        Sc(lambda e: e.activation(T.pm[:, c, 7], T.p5[:, c], AF.Copy, bias=-64.0), ["p5" + n, "pm0"], ["pm_" + n])
+        VG(lambda e: e.tensor_tensor(T.st[:, z], T.w5[:].indirect(T.lb[:, 2 * h:2 * h + 2]), T.qq[:, z], A.is_equal),
+           ["w5", "lb", "qq"], ["st" + n], 32)
+        V(lambda e: e.tensor_tensor_scan(T.lp[:, z], T.m8b[:], T.st[:, z], 0.0, A.mult, A.max), ["m8b", "st" + n], ["lp" + n])
+        V(lambda e: e.tensor_tensor(T.zb[:, z], T.st[:, z], T.cep[:, c], A.mult), ["st" + n, "cep", "ceps"], ["zb" + n])
+        V(lambda e: e.tensor_tensor(T.cod[:, z], T.lp[:, z], T.pm[:, c], A.mult), ["lp" + n, "pma", "pm_" + n, "cod0"], ["cod"])
+        V(lambda e: e.tensor_tensor_scan(T.zs[:, z], T.m8a[:], T.zb[:, z], 0.0, A.mult, A.max), ["m8a", "zb" + n], ["zs" + n])
+        VG(lambda e: e.tensor_scalar(T.cdl[:, z], T.cod[:].indirect(T.l8[:, 2 * h:2 * h + 2]), 64.0, None, A.add), ["cod", "l8"], ["cdl" + n], 32)
+        V(lambda e: e.tensor_scalar(T.dec[:, c], T.zs[:, 32 * h + 7:32 * h + 32:8], -64.0, 319.0, A.mult, A.add), ["zs" + n], ["dec" + n])
+        cdl = T.cdl[:, 32 * h:32 * h + 20]
+        SG(lambda e: e.activation(T.edec[:, x], T.eall[:, w].indirect(T.dec[:, c]), AF.Copy), ["eall" + n, "dec" + n], ["edec" + n], 64)
+        SG(lambda e: e.activation(T.hit[:, w], T.w1[:].indirect(cdl), AF.Copy), ["w1", "cdl" + n], ["hit" + n], 320)
+        VG(lambda e: e.tensor_tensor(T.aa[:, w], T.w1c[:].indirect(cdl), T.eall[:, w], A.mult), ["w1c", "cdl" + n, "eall" + n], ["aa" + n], 320)
+        VG(lambda e: e.tensor_tensor(T.edec[:, x], T.aa[:, w].indirect(T.dec[:, c]), T.edec[:, x], A.subtract),
+           ["aa" + n, "dec" + n], ["edec" + n], 64)
+        pn = "kp" + n
+        PEn(lambda e: e.matmul(T[pn][:, 0:64], T.bon[:], T.edec[:, x], True, True), ["bon", "edec" + n], [pn], 256)
+        op("v", [lambda e, o=320 * h + 64 * u: e.tensor_tensor(T.bb[:, o:o + 64], T[pn][:, 0:64], T.hit[:, o:o + 64], A.mult) for u in range(S)],
+           ["hit" + n], [pn, "bb" + n], 5 * 64 * CYC)
+        VG(lambda e: e.tensor_tensor(T.tab[:].indirect(T.soff[:, 32 * h:32 * h + 20]), T.aa[:, w], T.bb[:, w], A.add),
+           ["aa" + n, "bb" + n, "soff"], TAB, 320, SCAT)
 
-    def gather(h, s, i):
-        eu, fr, dr = "eu" + h, "fr" + h, "dr" + h
-        f0 = 1024 * (s - 1)
-        V(lambda e: e.tensor_tensor(T[dr][:, 256 * i:256 * i + 256], T.rtt[:].indirect(T[eu][:, 16 * i:16 * i + 16]),
-                                    T[fr][:, f0 + 256 * i:f0 + 256 * i + 256], A.subtract),
-          ["rtt", eu, "fr%s_%d%s" % (h, s - 1, "abb"[i])], [dr + "c%d" % i], 0.37)
-
-    def begin(h, s, t):
-        eu, fr, dr, ab, rg, pd, kp = (n + h for n in ("eu", "fr", "dr", "ab", "rg", "pd", "kp"))
-        f0 = 1024 * (s - 1)
-        Sc(lambda e: e.activation(T[rg][:], T.rtt[:].indirect(T[eu][:, 48:64]), AF.Copy), ["rtt", eu], [rg])
-        gather(h, s, 0)
-        gather(h, s, 1)
-        op("t", [lambda e: e.matmul(T[pd][:, 0:256], T.idb[:], T[rg][:], True, False),
-                 lambda e: e.matmul(T[pd][:, 0:256], T.idn[:], T[fr][:, f0 + 768:f0 + 1024], False, True)],
-           ["idb", "idn", rg, "fr%s_%db" % (h, s - 1)], [pd])
-        fw = "fw%d" % t
-        lo = 64 * int(h)
-        op("t", [lambda e: e.matmul(T[kp][:, 0:64], T.idb[:], T[fw][:, lo:lo + 64], True, False),
-                 lambda e: e.matmul(T[kp][:, 0:64], T.idb[:], T[fw][:, 128 + lo:128 + lo + 64], False, False)], ["idb", fw], [kp])
-        for b in (0, 1):
-            Sc(lambda e, b=b: e.activation(T[ab][:, b, :], T[dr][:, 256 * b:256 * b + 256], AF.Abs), [dr + "c%d" % b], [ab + str(b)], 0.3)
-
-    def end(h, s):
-        dr, ab, kp, pd = "dr" + h, "ab" + h, "kp" + h, "pd" + h
-        gather(h, s, 2)
-        Sc(lambda e: e.activation(T[ab][:, 3, :], T[pd][:, 0:256], AF.Abs), [pd], [ab + "3"], 0.3)
-        Sc(lambda e: e.activation(T[ab][:, 2, :], T[dr][:, 512:768], AF.Abs), [dr + "c2"], [ab + "2"], 0.3)
-        op("t", [lambda e, y=y: e.matmul(T[kp][:, 0:64], T.sel[:, y, :], T[ab][:, :, y * 16:y * 16 + 16], False, y == 15)
-                 for y in range(16)], SELK + [ab + "0", ab + "1", ab + "2", ab + "3"], [kp], dur=0.75)
-
-    def L(name):
-        i = LNAMES.index(name)
-        return T.lists[:, 4 * i:4 * i + 3]
-
-    def close(t):
-        EQK = ["eq"] + ["eq%d" % d for d in range(1, 6)]
-        for d in range(1, 6):
-            V(lambda e, d=d: e.tensor_tensor(T.eq[:, 48 * (d - 1):40 * d], T.hx[:, 1, 8 * d:48], T.hx[:, 1, 0:48 - 8 * d], A.is_equal),
-              HXB + ["eq"], ["eq%d" % d])
-        V(lambda e: e.tensor_scalar(T.prf[:], T.hx[:, 1, :].indirect(L("ROUT")), 1.0, None, A.add), HXB + ["lists"], ["prf"], 0.11)
-        V(lambda e: e.tensor_tensor(T.m1[:], T.eq[:, 0:80], T.eq[:, 80:160], A.max), EQK, ["m1"])
-        V(lambda e: e.tensor_tensor(T.m1[:, 0:40], T.m1[:, 0:40], T.m1[:, 40:80], A.max), ["m1"], ["m1"])
-        V(lambda e: e.tensor_copy(T.ctf[:], T.hx[:, 0, :].indirect(L("FWD8"))), HXA + ["hx5", "lists"], ["ctf"], 0.11)
-        V(lambda e: e.tensor_tensor(T.c48[:, 8:48], T.m1[:, 0:40], T.eq[:, 160:200], A.max), ["m1", "c48"] + EQK, ["c48"])
-        V(lambda e: e.tensor_scalar(T.kr[:], T.hx[:, 1, :].indirect(L("ROUT")), -31.0, None, A.add), HXB + ["lists"], ["kr"], 0.11)
-        V(lambda e: e.tensor_copy(T.cf[:], T.c48[:].indirect(L("FWD"))), ["c48", "lists"], ["cf"], 0.11)
-        V(lambda e: e.tensor_scalar(T.d6[:, 8:48], T.sch[:, :, 15::16], 15, None, A.arith_shift_right),
-          ["sch%d%s" % (s, h) for s in range(1, 6) for h in "01"], ["d6"])
-        V(lambda e: e.tensor_tensor_scan(T.cc[:], T.segm[:], T.cf[:], 0.0, A.mult, A.max), ["segm", "cf"], ["cc"])
-        V(lambda e: e.tensor_tensor(T.ad[:], T.d6[:, 8:48], T.d6[:, 0:40], A.add), ["d6", "d60"], ["ad"])
-        V(lambda e: e.tensor_tensor(T.cl[:, 1:48], T.cc[:, 1:48], T.cc[:, 0:47], A.is_gt), ["cc", "cl"], ["cl"])
-        V(lambda e: e.tensor_tensor(T.cd[:, 1:48], T.cc[:, 0:47], T.dum[:, 1:48], A.mult), ["cc", "dum", "cd"], ["cd"])
-        V(lambda e: e.tensor_tensor_scan(T.cs[:], T.segm[:], T.cc[:], 0.0, A.mult, A.add), ["segm", "cc"], ["cs"])
-        V(lambda e: e.tensor_tensor(T.cpr[:], T.cl[:].indirect(L("REV")), T.prf[:], A.mult), ["cl", "prf", "lists"], ["cpr"], 0.11)
-        V(lambda e: e.tensor_tensor(T.so[:], T.cd[:], T.ctf[:], A.max), ["cd", "ctf"], ["so"])
-        V(lambda e: e.tensor_tensor(T.fs[:], T.fb[:], T.cs[:, 4::6], A.subtract), ["fb", "cs"], ["fs"])
-        V(lambda e: e.tensor_tensor_scan(T.bv[:], T.segm[:], T.cpr[:], 0.0, A.mult, A.add), ["segm", "cpr"], ["bv"])
-        V(lambda e: e.tensor_copy(T.soff[:], T.so[:].indirect(L("TRS"))), ["so", "lists"], ["soff"], 0.11)
-        V(lambda e: e.tensor_scalar(T.fl[:], T.fs[:], 1024.0, None, A.mult), ["fs"], ["fl"])
-        for h in "01":
-            lo = 64 * int(h)
-            Sc(lambda e, h=h, lo=lo: e.activation(T.fout[:, lo:lo + 64], T["fr" + h][:].indirect(T.fl[:, 4 * int(h):4 * int(h) + 4]), AF.Copy),
-               ["fl"] + ["fr%s_%d%s" % (h, s, x) for s in range(5) for x in "ab"] + ["fr%s_5_%d" % (h, b) for b in range(4)], ["fout" + h])
-        if t < VI - 1:
-            dst = T.cores[(rank + 1) % N]
-            rid, pid = topo.addr(dst, core)
-            send(lambda e: e.remote_dma(T["fin%d" % (t + 1)][:], T.fout[:], T.sem["rf%d" % (t + 1)], T.sem.lsend, pid, rid,
-                                        topo.mask(core, dst)), ["fout0", "fout1"], "lsend", len(topo.engines(core, dst)))
-        else:
-            op("y", lambda e: e.dma_start(T.yf[:], T.fout[:]), ["fout0", "fout1"], ["yf"], "oyf", 16)
-        Sc(lambda e: e.activation(T.eall[:], T.tab[:].indirect(T.soff[:, 0:40]), AF.Copy), TABK + ["soff"], ["eall"], dur=0.86)
-        V(lambda e: e.tensor_scalar(T.cl2[:], T.cl[:].indirect(L("REV")), 2.0, None, A.mult), ["cl", "lists"], ["cl2"], 0.11)
-        V(lambda e: e.tensor_tensor(T.eqv[:], T.bv[:], T.prf[:], A.is_equal), ["bv", "prf"], ["eqv"])
-        V(lambda e: e.tensor_tensor(T.cle[:], T.cl[:].indirect(L("REV")), T.eoc[:], A.mult), ["cl", "eoc", "lists"], ["cle"], 0.11)
-        V(lambda e: e.tensor_tensor_scan(T.ss[:], T.cl2[:], T.eqv[:], 0.0, A.add, A.subtract), ["cl2", "eqv"], ["ss"])
-        if t > 0:
-            V(lambda e: e.tensor_scalar(T.ad[:], T.ad[:], T.zc[:, 0:1], None, A.add), ["ad", "zc"], ["ad"])
-        V(lambda e: e.tensor_tensor(T.cod[:], T.ss[:], T.kr[:], A.mult), ["ss", "kr"], ["cod"])
-        V(lambda e: e.tensor_tensor_scan(T.scb[:], T.segm[:], T.cle[:], 0.0, A.mult, A.add), ["segm", "cle"], ["scb"])
-        V(lambda e: e.tensor_scalar(T.cdl[:], T.cod[:].indirect(L("TRL")), 31.0, None, A.add), ["cod", "lists"], ["cdl"], 0.11)
-        Sc(lambda e: e.activation(T.hit[:], T.w1[:].indirect(T.cdl[:, 0:40]), AF.Copy), ["w1", "cdl"], ["hit"], dur=0.86)
-        V(lambda e: e.tensor_scalar(T.pri[:, 0:40], T.ad[:], 1, None, A.bitwise_and), ["ad", "pri"], ["pri"])
-        V(lambda e: e.tensor_tensor(T.sc2[:], T.scb[:], T.eoc[:], A.subtract), ["scb", "eoc"], ["sc2"])
-        V(lambda e: e.tensor_tensor(T.fv[:, 0:47], T.ss[:, 0:47], T.ss[:, 1:48], A.is_gt), ["ss", "fv"], ["fv"])
-        V(lambda e: e.tensor_tensor(T.sc2[:], T.pri[:].indirect(L("PRR")), T.sc2[:], A.mult), ["pri", "sc2", "lists"], ["sc2"], 0.11)
-        V(lambda e: e.tensor_tensor(T.sc2[:], T.sc2[:], T.eoc[:], A.add), ["sc2", "eoc"], ["sc2"])
-        V(lambda e: e.tensor_tensor(T.sc2[:], T.sc2[:], T.fv[:], A.mult), ["sc2", "fv"], ["sc2"])
-        V(lambda e: e.tensor_tensor_scan(T.tot[:], T.segm[:], T.sc2[:], 0.0, A.mult, A.add), ["segm", "sc2"], ["tot"])
-        V(lambda e: e.tensor_copy(T.dec[:], T.tot[:, 5::6]), ["tot"], ["dec"])
-        Sc(lambda e: e.activation(T.edec[:], T.eall[:].indirect(T.dec[:]), AF.Copy), ["eall", "dec"], ["edec"], dur=0.22)
-        V(lambda e: e.tensor_tensor(T.aa[:], T.w1c[:].indirect(T.cdl[:, 0:40]), T.eall[:], A.mult), ["w1c", "cdl", "eall"], ["aa"], dur=0.85)
-        V(lambda e: e.tensor_tensor(T.edec[:], T.aa[:].indirect(T.dec[:]), T.edec[:], A.subtract), ["aa", "dec", "edec"], ["edec"], dur=0.21)
-        op("t", lambda e: e.matmul(T.pnew[:, 0:128], T.bon[:], T.edec[:], True, True), ["bon", "edec"], ["pnew"], dur=0.4)
-        if t < VI - 1:
-            V(lambda e: e.tensor_reduce(T.zr[:], T.cc[:, 5::6], AxisListType.X, A.add), ["cc"], ["zr"])
-            op("t", lambda e: e.matmul(T.pmis[:, 0:1], T.onef[:], T.zr[:], True, True), ["onef", "zr"], ["pmis"])
-            start_keys(t + 1)
-        for r in range(5):
-            V(lambda e, r=r: e.tensor_tensor(T.bb[:, 128 * r:128 * r + 128], T.pnew[:, 0:128], T.hit[:, 128 * r:128 * r + 128], A.mult),
-              ["pnew", "hit"], ["bb%d" % r], dur=0.11)
-        V(lambda e: e.tensor_tensor(T.tab[:].indirect(T.soff[:, 0:40]), T.aa[:], T.bb[:], A.add),
-          ["aa", "soff"] + TABK + ["bb%d" % r for r in range(5)], ["tab"], dur=2.0)
-
-    start_keys(0)
     for t in range(VI):
-        fin = "fin%d" % t
-        start_facts("0", t)
-        start_facts("1", t)
-        op("t", [lambda e, y=y: e.matmul(T.pmis[:, 8:16], T.sel[:, y, :], T[fin][:, y::16], y == 0, y == 15) for y in range(16)],
-           SELK + [fin], ["pmis"])
-        spread("0", 0)
-        entries("0")
-        begin("0", 1, t)
-        entries("1")
-        end("0", 1)
-        spread("1", 0)
-        begin("1", 1, t)
-        V(lambda e: e.tensor_scalar(T.d6[:, 0:8], T.pmis[:, 8:16], 1.0 / 32768.0, None, A.mult), ["pmis"], ["d60"])
-        if t == 1:
-            V(lambda e: e.tensor_copy(T.zc[:], T.pmis[:, 0:1]), ["pmis"], ["zc"])
-        elif t == 2:
-            V(lambda e: e.tensor_tensor(T.zc[:], T.pmis[:, 0:1], T.zc[:], A.add), ["pmis", "zc"], ["zc"])
-        if t == 0:
-            n = 4 * len(LISTS)
-            V(lambda e: e.tensor_tensor(T.lc[:, 0:n], T.la[:, 0:n], T.lb[:, 0:n], A.add),
-              [x % i for x in ("la%d", "lb%d") for i in range(len(LISTS))], ["lc"])
-            Sc(lambda e: e.activation(T.eoc[:], T.eoi[:], AF.Identity, bias=T.ylf[:, 0:1]), ["eoi", "ylf"], ["eoc"])
-            Sc(lambda e: e.activation(T.dum[:], T.dui[:], AF.Identity, bias=T.ylf[:, 0:1]), ["dui", "ylf"], ["dum"])
-            Sc(lambda e: e.activation(T.w1c[:], T.w1[:], AF.Copy, scale=-1.0, bias=1.0), ["w1"], ["w1c"])
-            Sc(lambda e: e.activation(T.bon[:], T.bof[:], AF.Copy, scale=-1.0), ["bof"], ["bon"])
-            V(lambda e: e.tensor_copy(T.lists[:, 0:n], T.lc[:, 0:n]), ["lc"], ["lists"])
+        fin, fw = "fin%d" % t, "fw%d" % t
+        V(lambda e, fw=fw: e.tensor_tensor(T.sk1[:], T[fw][:, 16, 0:8], T.cxh[:], A.add), [fw + "s", "cxh"], ["sk1"])
+        V(lambda e, fw=fw: e.tensor_tensor(T.sch[:, 14::16, 0], T[fw][:, 16, 8:16], T.sk1[:], A.add), [fw + "s", "sk1"], both("sch", [0]))
+        for h in HS:
+            choice(h, 0, t)
         for s in range(1, S + 1):
-            collect[0] = s == S
-            post("0", s)
-            end("1", s)
-            if s < S:
-                entries("0")
-                spread("0", s)
-                begin("0", s + 1, t)
-            post("1", s)
-            if s < S:
-                end("0", s + 1)
-                entries("1")
-                spread("1", s)
-                begin("1", s + 1, t)
-        close(t)
-        collect[0] = False
-        schedule()
+            for h in HS:
+                step(h, s, t)
+                choice(h, s, t)
+            if s == 1:
+                PEn([lambda e, y=y, fin=fin: e.matmul(T.pmis[:, 8:16], sel(y), T[fin][:, y::16], y == 0, y == 15) for y in range(16)],
+                    ["sel", fin + "0", fin + "1"], ["pmis"], 1024)
+                V(lambda e: e.tensor_copy(T.sch[:, 15::16, 0], T.pmis[:, 8:16]), [], ["pmis", "d0"])
+            if s == S - 1:
+                early(t)
+        for h in HS:
+            late(h, t)
+        if t < VI - 1:
+            V(lambda e: e.tensor_reduce(T.zr[:], T.lp[:, 7::8], AxisListType.X, A.add), ["lp0", "lp1"], ["zr"])
+            PEn(lambda e: e.matmul(T.pmis[:, 0:1], T.negf[:], T.zr[:], True, True), ["negf", "zr"], ["pmis"], 256)
+            V(lambda e: e.tensor_tensor(T.zc[:], T.zc[:], T.pmis[:, 0:1], A.subtract), [], ["pmis", "zc"])
 
     for i in range(4):
         pd, o = "pd%d" % (i % 2), 256 * i
-        Sc(lambda e: e.activation(T[pd][:, 0:256], T.tab[:, 1024 + o:1280 + o], AF.Copy, scale=4096.0), TABK, [pd])
-        V(lambda e: e.tensor_tensor(T.ypt[:, o:o + 256], T[pd][:, 0:256], T.tab[:, o:o + 256], A.add), [pd] + TABK, ["ypt%d" % i])
-        op("y", lambda e: e.dma_start(T.yp[:, o:o + 256], T.ypt[:, o:o + 256]), ["ypt%d" % i], ["yp%d" % i], "oyp%d" % i, 16)
+        Sc(lambda e, pd=pd, o=o: e.activation(T[pd][:, 0:256], T.tab[:, 1024 + o:1280 + o], AF.Copy, scale=4096.0), TAB, [pd], 256)
+        V(lambda e, pd=pd, o=o: e.tensor_tensor(T.ypt[:, o:o + 256], T[pd][:, 0:256], T.tab[:, o:o + 256], A.add), TAB, [pd, "ypt%d" % i], 256)
+        dma("y", T.yp[:, o:o + 256], T.ypt[:, o:o + 256], ["ypt%d" % i], ["yp%d" % i], "oyp%d" % i, 1.5)
     finish()

@@ -6,24 +6,25 @@ VI, S = 3, 5
 NDUM = 640
 SCRATCH = {}
 for _n, _s, _d in (
-        ("pkt tmpi", [128, 1024], "int32"), ("rtt", [128, 3072], "bfloat16"), ("tab", [128, 2048 + NDUM], "float32"),
+        ("pkt tmpi tmpj", [128, 1024], "int32"), ("rtt", [128, 3072], "bfloat16"), ("tab", [128, 2048 + NDUM], "float32"),
         ("jci jh jl i144", [128, 144], "int32"), ("jhb jlb selb", [128, 144], "bfloat16"),
         ("tra trb", [128, 2, 4, 32], "bfloat16"),
         ("sri", [8, 128], "int32"), ("srb bo8", [8, 128], "bfloat16"),
-        ("fout", [128, 128 * VI], "bfloat16"), ("fin0 fin1 fin2 oneb idb ide ido oh", [128, 128], "bfloat16"), ("fw0 fw1 fw2", [128, 17, 16], "bfloat16"),
-        ("pi yli", [128, 1], "int32"), ("ylf y64 q2k g15 zr zc", [128, 1], "float32"),
-        ("i80", [128, 80], "int32"), ("w1 w1c", [128, 80], "float32"),
-        ("negf bon edec", [128, 128], "float32"), ("ms", [128, 256], "bfloat16"),
-        ("nd ndi", [64, 1024], "bfloat16"), ("cst", [64, 64], "bfloat16"), ("c64 ft0 ft1", [64, 128], "bfloat16"),
-        ("km qq st lp zs zb ppf", [128, 64], "float32"), ("cep pm", [128, 8, 8], "float32"), ("pp", [128, 8, 9], "int32"),
+        ("fout", [128, 128 * VI], "bfloat16"), ("fin0 fin1 fin2 oneb idb ide ido", [128, 128], "bfloat16"), ("fw0 fw1 fw2", [128, 17, 16], "bfloat16"),
+        ("pi yli", [128, 1], "int32"), ("ylf y64 q2k g15 zr zm", [128, 1], "float32"),
+        ("i80", [128, 80], "int32"), ("w1", [128, 80], "float32"),
+        ("negf bon edec nid", [128, 128], "float32"), ("ms", [128, 256], "bfloat16"),
+        ("bonh nh", [128, 128], "float16"), ("half", [64, 320], "bfloat16"), ("nd", [64, 1024], "bfloat16"), ("ndi", [64, 256], "bfloat16"), ("cst", [64, 64], "bfloat16"), ("c64 ft0 ft1", [64, 128], "bfloat16"),
+        ("km st lp zs zb ppf", [128, 64], "float32"), ("cep pm", [128, 8, 8], "float32"), ("pp", [128, 8, 10], "int32"),
         ("cod", [128, 72], "float32"), ("so", [128, 48], "float32"), ("yi", [128, 3], "int32"), ("ybf y5 y8", [128, 1], "float32"),
         ("l5i l8i", [128, 4], "int32"), ("l5 l8", [128, 4], "uint16"), ("soff cdl", [128, 64], "uint16"),
         ("eq cs m25", [128, 200], "float32"), ("m8a m8b", [128, 32], "float32"),
-        ("dui dum cei ce", [128, 8, 5], "float32"), ("m5a m5b sm tq cl clp", [128, 40], "float32"), ("rr w5", [128, 41], "float32"),
-        ("cc pri", [128, 8, 5], "int32"), ("dd ad", [128, 40], "int32"),
-        ("p5", [128, 8], "int32"), ("bsi cxh sk1 ncc", [128, 8], "float32"), ("hz", [128, 2], "float32"),
+        ("dui dum cei ce pri", [128, 8, 5], "float32"), ("m5a sm tq shut pw ad", [128, 40], "float32"), ("w5", [128, 41], "float32"),
+        ("cc", [128, 8, 5], "int32"), ("dd", [128, 40], "int32"), ("zc", [128, 2], "int32"),
+        ("bsi cxh sk1", [128, 8], "float32"), ("hz", [128, 2], "float32"),
         ("lbi", [128, 4], "int32"), ("lb lf0 lf1", [128, 4], "uint16"), ("lst0 lst1 fl dec", [128, 8], "uint16"),
-        ("sch", [128, 128, S + 1], "int32"), ("eall aa hit bb", [128, NDUM], "float32"),
+        ("sch", [128, 128, S + 1], "int32"), ("eall hit bb", [128, NDUM], "float32"),
+        ("sk", [128, 2, 8], "int32"), ("lsts", [128, 16], "uint16"),
         ("ypt", [128, 1024], "float32"), ("eu0 eu1", [128, 64], "uint16"),
         ("fh0 fh1", [128, 320], "bfloat16"), ("rg0 rg1", [128, 1024], "bfloat16"),
         ("ab0 ab1", [128, 1024], "bfloat16")):
@@ -34,40 +35,50 @@ for _m in "kp0 kp1 pd0 pd1 pd2 pd3 pmis".split():
 SCRATCH["pft"] = ("psum", [128, 1024], "bfloat16")
 SEMAPHORES = ("cv cs ct cg lpk0 lpk1 lrt0 lrt1 ljc ljw lsr lfx rw1 rw2 rf10 rf11 rf20 rf21 lsend oyf0 oyf1 "
               "oyp0 oyp1 oyp2 oyp3").split()
-GATHERS = (("s", 0, 4), ("v", 4, 8), ("v", 8, 12), ("v", 12, 16))
+GATHERS = (("s", 0, 4), ("v", 4, 8), ("v", 8, 12), ("v", 12, 14), ("v", 14, 16))
+OTHER = {(1, 0): (("s", 0, 4), ("v", 4, 8), ("s", 8, 12), ("v", 12, 16))}
 BANKS = ((0, 4), (4, 8), (8, 12), (12, 16))
 PERIOD = 2.0
-PLACE = {"scan": 0.0, "row": 0.04, "court": 0.03, "lf": 0.44, "lst": 0.61, "fh": 0.48, "eu": 0.78, "turn": 0.79, "ft": 1.19,
-         "pay": 0.93, "g0": 1.96, "g1": 1.32, "g2": 1.04, "g3": 2.41,
-         "n0": 1.1, "i0": 1.7, "n1": 1.25, "i1": 1.74, "n2": 1.73, "i2": 2.27, "n3": 1.98, "i3": 2.43,
-         "a0": 2.08, "a1": 2.35, "a2": 2.61, "a3": 3.4, "m0": 2.42, "m1": 2.71, "m2": 3.01, "m3": 3.08}
-CYC, GATH, SCAT, PE, LAG = 0.83e-3, 1.5, 3.8, 0.45e-3, 0.17
+PLACE = {"scan": 0.0, "row": 0.04, "court": 0.03, "lf": 0.44, "lst": 0.43, "fh": 0.48, "eu": 0.78, "turn": 0.79, "ft": 1.19,
+         "pay": 0.41, "g0": 1.96, "g1": 1.32, "g2": 1.04, "g3": 2.02, "g4": 2.2,
+         "n0": 1.1, "i0": 1.24, "n1": 1.25, "i1": 1.69, "n2": 1.70, "i2": 1.97, "n3": 1.98, "i3": 2.43,
+         "a0": 2.08, "a1": 2.33, "a2": 2.34, "a3": 3.4, "m0": 2.44, "m1": 2.78, "m2": 3.01, "m3": 3.08}
+CYC, GATH, SCAT, PE, LAG = 0.95e-3, 1.56, 3.8, 0.48e-3, 0.2
+DEPTH, SLACK, ROUNDS, FREE = 1, 0.1, 8, False
+PLACED = (2, 3, 4, 5)
+EARLY = ((0,), (1,))
+VIA_TENSOR = (0, 1)
+OUT = (("v", 0, 256), ("s", 256, 576), ("s", 576, 832), ("s", 832, 1024))
 ORDER = []
 
 
 def plan(batch):
-    w, rd, pred = {}, {}, []
+    n = len(batch)
+    busy, late = [it[6] for it in batch], [it[7] for it in batch]
+    w, rd, left = {}, {}, []
+    succ = [[] for _ in batch]
     for i, it in enumerate(batch):
         p = {w[r] for r in it[2] if r in w}
+        group = {w[x[1:]] for x in it[3] if x[0] == "+"}
         for x in it[3]:
-            p |= ({w[x]} if x in w else set()) | rd.get(x, set())
+            if x[0] != "+":
+                p |= ({w[x]} if x in w else set()) | rd.get(x, set())
         for r in it[2]:
             rd.setdefault(r, set()).add(i)
         for x in it[3]:
-            w[x] = i
-            rd[x] = set()
-        pred.append(p - {i})
-    n = len(batch)
-    busy, late = [it[6] for it in batch], [it[7] for it in batch]
-    succ = [[] for _ in batch]
-    left = [len(p) for p in pred]
-    for i in range(n):
-        for p in pred[i]:
-            succ[p].append((i, late[p] + LAG))
-    last = {}
+            w[x.lstrip("+")] = i
+            rd[x.lstrip("+")] = set()
+        for j in p - {i}:
+            succ[j].append((i, late[j] + LAG))
+        for j in group - p:
+            succ[j].append((i, busy[j]))
+        left.append(len((p | group) - {i}))
+    last, kept = {}, set()
     for i in sorted((i for i in range(n) if batch[i][8] is not None), key=lambda i: (batch[i][8], i)):
         q = batch[i][0]
-        if q in last:
+        if q in last and i not in [j for j, d in succ[last[q]]]:
+            if batch[i][8] >= 0:
+                kept.add((last[q], i))
             succ[last[q]].append((i, busy[last[q]]))
             left[i] += 1
         last[q] = i
@@ -82,19 +93,38 @@ def plan(batch):
     for i in reversed(topo):
         prio[i] = max([late[i]] + [d + prio[j] for j, d in succ[i]])
     ready = {i: 0.0 for i in range(n) if not left[i]}
-    free, order, seen = {}, [], [0.0] * n
+    free, order, seen, held = {}, [], [0.0] * n, {}
+    before = [[] for _ in batch]
+    for i in range(n):
+        for j, d in succ[i]:
+            before[j].append((i, d))
 
     def start(i):
-        return max(free.get(batch[i][0], 0.0), ready[i])
+        return max(free.get(batch[i][0], 0.0), ready[i], held.get(i, 0.0))
+
+    def soon(j, depth):
+        if j in ready:
+            return start(j)
+        if depth == 0:
+            return 1e9
+        return max([seen[j]] + [soon(p, depth - 1) + d for p, d in before[j] if not done[p]])
+    done = [False] * n
     while ready:
         i = min(ready, key=lambda i: (round(start(i), 3), -prio[i], i))
         q, t = batch[i][0], start(i)
-        for j in sorted((j for j in ready if batch[j][0] == q and t < start(j) < t + busy[i]), key=lambda j: (-prio[j], j)):
-            if max(start(j) + prio[j], start(j) + busy[j] + prio[i]) < max(t + prio[i], t + busy[i] + prio[j]) - 1e-6:
-                i = j
-                break
-        t = start(i)
+        near, edge = set(ready), set(ready)
+        for _ in range(DEPTH):
+            edge = {j for k in edge for j, d in succ[k]} - near
+            near |= edge
+        for j in near:
+            if batch[j][0] == q and prio[j] > prio[i]:
+                s = soon(j, DEPTH)
+                if t < s < t + busy[i] and max(s + prio[j], s + busy[j] + prio[i]) < max(t + prio[i], t + busy[i] + prio[j]) - SLACK:
+                    held[i] = max(held.get(i, 0.0), s + 1e-3)
+        if held.get(i, 0.0) > t:
+            continue
         del ready[i]
+        done[i] = True
         free[q] = t + busy[i]
         order.append(i)
         for j, d in succ[i]:
@@ -102,7 +132,48 @@ def plan(batch):
             seen[j] = max(seen[j], t + d)
             if left[j] == 0:
                 ready[j] = seen[j]
-    return order
+
+    def lay(order, links, back):
+        at, used = [0.0] * n, {}
+        for i in order:
+            if back:
+                t = max([late[i] - busy[i]] + [at[j] + busy[j] + d - busy[i] for j, d in links[i]])
+            else:
+                t = max([0.0] + [at[j] + d for j, d in links[i]])
+            slots = used.setdefault(batch[i][0], [])
+            k = bisect(slots, t)
+            if k and slots[k - 1][1] > t:
+                t = slots[k - 1][1]
+            while k < len(slots) and slots[k][0] < t + busy[i] - 1e-9:
+                t = slots[k][1]
+                k += 1
+            slots.insert(k, (t, t + busy[i]))
+            at[i] = t
+        return at
+    if FREE:
+        succ = [[(j, d) for j, d in succ[i] if (i, j) not in kept] for i in range(n)]
+        before = [[(j, d) for j, d in before[i] if (j, i) not in kept] for i in range(n)]
+    best = None
+    for _ in range(ROUNDS):
+        at = lay(order, before, False)
+        end = max(at[i] + late[i] for i in range(n))
+        order = sorted(order, key=lambda i: at[i])
+        if best is None or end < best[0] - 1e-6:
+            best = (end, order)
+        at = lay(sorted(order[::-1], key=lambda i: -at[i] - busy[i]), succ, True)
+        order = sorted(order, key=lambda i: -at[i] - busy[i])
+    return best[1] if best else order
+
+
+def bisect(slots, t):
+    lo, hi = 0, len(slots)
+    while lo < hi:
+        mid = (lo + hi) // 2
+        if slots[mid][0] <= t:
+            lo = mid + 1
+        else:
+            hi = mid
+    return lo
 
 
 def make_flow(g, T):
@@ -134,6 +205,7 @@ def make_flow(g, T):
             toks = [writer[r] for r in reads if r in writer]
             for w in writes:
                 toks += ([writer[w]] if w in writer else []) + readers.get(w, [])
+            writes = [w.lstrip("+") for w in writes]
             need(q, toks)
             name = sem or "c" + q
             for c in (calls if isinstance(calls, list) else [calls]):
@@ -209,8 +281,8 @@ def rank_program(g, core, T, topo):
     G(lambda e: e.iota(T.pi[:], [[1, 1]], 0, 1), [], ["pi"], 1)
     G(lambda e: e.iota(T.i144[:], [[1, 144]], 0, 0), [], ["i144"], 144)
     V(lambda e: e.memset(T.negf[:], -1.0), [], ["negf"], 128)
-    V(lambda e: e.memset(T.oneb[:], 1.0), [], ["oneb"])
-    V(lambda e: e.memset(T.ndi[:], -1.0), [], ["ndi"], 512)
+    V(lambda e: e.memset(T.oneb[:], 1.0), [], ["oneb"], at=-9)
+    V(lambda e: e.memset(T.ndi[:], -1.0), [], ["ndi"], 128, at=-8)
     G(lambda e: e.affine_select(T.bon[:], T.negf[:], [[-16, 8], [0, 16]], A.is_ge, 0.0, 0, 1), ["negf"], ["bon"], 128)
     G(lambda e: e.affine_select(T.bon[:], T.bon[:], [[16, 8], [0, 16]], A.is_ge, 0.0, 15, -1), [], ["bon"], 128)
     G(lambda e: e.affine_select(T.bo8[:], T.oneb[0:8, :], [[1, 8], [0, 16]], A.is_equal, 0.0, 0, -1), ["oneb"], ["bo8"], 128)
@@ -219,7 +291,7 @@ def rank_program(g, core, T, topo):
     V(lambda e: e.tensor_tensor(T.ido[:], T.idb[:], T.ide[:], A.subtract), ["idb", "ide"], ["ido"], 256)
     ND = ["nd%d" % b for b in range(4)]
     for b in range(4):
-        G(lambda e, b=b: e.affine_select(T.nd[:, 256 * b:256 * b + 256], T.ndi[:, 256 * b:256 * b + 256], [[-1, 4], [-16, 4], [0, 16]],
+        G(lambda e, b=b: e.affine_select(T.nd[:, 256 * b:256 * b + 256], T.ndi[:], [[-1, 4], [-16, 4], [0, 16]],
                                          A.is_equal, 0.0, -4 * b, 1), ["ndi"], [ND[b]], 256)
     G(lambda e: e.iota(T.cst[0:32, :], [[16, 4], [0, 16]], 0, 0, **flag), [], ["cst0"], 64)
     V(lambda e: e.memset(T.cst[32:64, :], -7680.0), [], ["cst1"])
@@ -242,18 +314,23 @@ def rank_program(g, core, T, topo):
 
     V(lambda e: e.tensor_scalar(T.i80[:], T.i144[:, 0:80], 79, None, A.bitwise_and), ["i144"], ["i80"], 80)
     V(lambda e: e.tensor_scalar(T.w1[:], T.i80[:], T.ylf[:, 0:1], None, A.is_equal), ["i80", "ylf"], ["w1"], 80)
-    Sc(lambda e: e.activation(T.w1c[:], T.w1[:], AF.Copy, scale=-1.0, bias=1.0), ["w1"], ["w1c"], 80)
     G(lambda e: e.iota(T.m25[:], [[0, 200]], 1, 0, **flag), [], ["m25"], 200)
-    for n, width, cases, last in (("m5a", 5, 8, 0), ("m5b", 5, 8, 1), ("m8a", 8, 4, 0), ("m8b", 8, 4, 1)):
+    for n, width, cases, last in (("m5a", 5, 8, 0), ("m8a", 8, 4, 0), ("m8b", 8, 4, 1)):
         G(lambda e, n=n, width=width, cases=cases, last=last: e.affine_select(
             T[n][:], T.m25[:, 0:width * cases], [[0, cases], [1, width]], A.is_gt, 0.0, -last, 0), ["m25"], [n], 40)
     for i in (4, 5):
         G(lambda e, i=i: e.iota(T.m25[:, i::25], [[0, 8]], 0, 0, **flag), [], ["m25"], 8)
-    for n, size, value in (("eq", 200, 0), ("cl", 40, 0), ("rr", 41, 0), ("w5", 41, -1000), ("cep", 64, 0), ("pm", 64, 0), ("dum", 40, 0),
+    for n, size, value in (("eq", 200, 0), ("w5", 41, -1000), ("cep", 64, 0), ("pm", 64, 0), ("dum", 40, 0),
                            ("cod", 72, 0), ("so", 48, 0)):
         G(lambda e, n=n, size=size, value=value: e.iota(T[n][:], [[0, size]], value, 0, **flag), [], [n + "0"], size)
-    G(lambda e: e.iota(T.ad[:, 0:1], [[0, 1]], 0, 0), [], ["ad"], 1)
-    G(lambda e: e.iota(T.zc[:], [[0, 1]], 1, 0, **flag), [], ["zc"], 1)
+    G(lambda e: e.iota(T.ad[:, 0::20], [[0, 2]], 0, 0, **flag), [], ["ad0"], 2)
+    if VIA_TENSOR:
+        G(lambda e: e.iota(T.half[:], [[0, 320]], 3, 0, **flag), [], ["half"], 320)
+        Sc(lambda e: e.activation(T.half[:], T.half[:], AF.Copy, scale=0.125), [], ["half"], 320)
+        Sc(lambda e: e.activation(T.bonh[:], T.bon[:], AF.Copy), ["bon"], ["bonh"], 128)
+        G(lambda e: e.affine_select(T.nid[:], T.negf[:], [[-1, 128]], A.is_equal, 0.0, 0, 1), ["negf"], ["nid"], 128)
+    G(lambda e: e.iota(T.zc[:, 0:1], [[0, 1]], 0, 0), [], ["zc"], 1)
+    G(lambda e: e.iota(T.zm[:], [[0, 1]], -1, 0, **flag), [], ["zm"], 1)
     G(lambda e: e.iota(T.dui[:], [[80, 8], [16, 5]], 2048, 0, **flag), [], ["dui"], 40)
     G(lambda e: e.iota(T.cei[:], [[0, 2], [-16, 4], [-64, 5]], 319, 0, **flag), [], ["cei"], 40)
     G(lambda e: e.iota(T.l5i[:], [[20, 2], [4, 2]], 0, 0), [], ["l5i"], 4)
@@ -274,10 +351,10 @@ def rank_program(g, core, T, topo):
     V(lambda e: e.tensor_scalar(T.hz[:, 1:2], T.yi[:, 2:3], 0.0, 40.0, A.is_equal, A.mult), ["y8i"], ["z40"])
     V(lambda e: e.tensor_scalar(T.lb[:], T.lbi[:], T.hz[:, 0:1], T.hz[:, 1:2], A.add, A.max), ["lbi", "h8", "z40"], ["lb"])
 
-    V(lambda e: e.tensor_scalar(T.jh[:], T.jci[:], 8, None, A.arith_shift_right), ["jci", "jcw"], ["jh"], 144)
-    V(lambda e: e.tensor_scalar(T.jl[:], T.jci[:], 255, None, A.bitwise_and), ["jci", "jcw"], ["jl"], 144)
+    V(lambda e: e.tensor_scalar(T.jh[:], T.jci[:], 8, None, A.arith_shift_right), ["jci", "jcw"], ["jh"], 144, at=-5)
+    V(lambda e: e.tensor_scalar(T.jl[:], T.jci[:], 255, None, A.bitwise_and), ["jci", "jcw"], ["jl"], 144, at=-4.9)
     Sc(lambda e: e.activation(T.jlb[:], T.jl[:], AF.Copy), ["jl"], ["jlb"], 144)
-    V(lambda e: e.tensor_scalar(T.jhb[:], T.jh[:], 256.0, T.q2k[:, 0:1], A.mult, A.add), ["jh", "q2k"], ["jhb"], 144)
+    V(lambda e: e.tensor_scalar(T.jhb[:], T.jh[:], 256.0, T.q2k[:, 0:1], A.mult, A.add), ["jh", "q2k"], ["jhb"], 144, at=-4.8)
     for i, b in enumerate(("jhb", "jlb")):
         V(lambda e, i=i, b=b: e.transpose(T.tra[:, i], T[b][:, 0:128]), [b], ["tra%d" % i])
         V(lambda e, i=i, b=b: e.transpose(T.trb[:, i], T[b][:, 16:144]), [b], ["trb%d" % i])
@@ -294,47 +371,46 @@ def rank_program(g, core, T, topo):
     Sc(lambda e: e.activation(T.fw0[:, 1:16:2, :], T.pd0[:, 128:256], AF.Copy), [], ["pd0", "fw0b"], 128)
     Sc(lambda e: e.activation(T.srb[:], T.sri[:], AF.Copy), ["sri"], ["srb"], 128)
     PEn(lambda e: e.matmul(T.pmis[:, 0:128], T.bo8[:], T.srb[:], True, True), ["bo8", "srb"], ["pmis"], 128)
-    V(lambda e: e.tensor_scalar(T.oh[:], T.pmis[:, 0:128], T.ylf[:, 0:1], None, A.is_equal), ["ylf"], ["pmis", "oh"], 128)
-    V(lambda e: e.tensor_tensor(T.ms[:, 0:128], T.oh[:], T.jhb[:, 0:128], A.mult), ["oh", "jhb"], ["ms0"], 256)
-    V(lambda e: e.tensor_tensor(T.ms[:, 128:256], T.oh[:], T.jlb[:, 0:128], A.mult), ["oh", "jlb"], ["ms1"], 256)
+    V(lambda e: e.tensor_scalar(T.pmis[:, 128:256], T.pmis[:, 0:128], T.ylf[:, 0:1], None, A.is_equal), ["ylf"], ["pmis"], 128, at=-4.6)
+    op("v", [lambda e, i=i, b=b: e.tensor_tensor(T.ms[:, 128 * i:128 * i + 128], T.pmis[:, 128:256], T[b][:, 0:128], A.mult)
+             for i, b in enumerate(("jhb", "jlb"))], ["jhb", "jlb"], ["pmis", "ms"], 256 * CYC, at=-4.4)
     PEn([lambda e, y=y: e.matmul(T.pd1[:, 0:16], sel(y), T.ms[:, y::16], y == 0, y == 15) for y in range(16)],
-        ["sel", "ms0", "ms1"], ["pd1"], 1024)
+        ["sel", "ms"], ["pd1"], 1024)
     Sc(lambda e: e.activation(T.fw0[:, 16, :], T.pd1[:, 0:16], AF.Copy, scale=1.0 / 131072.0), [], ["pd1", "fw0s"])
     for t in (1, 2):
         send(T["fw%d" % t][:], T.fw0[:], ["fw0a", "fw0b", "fw0s"], t, "rw%d" % t, ["fw%d%s" % (t, x) for x in "abs"])
     TAB = ["tabd"] + ["tab%d%d" % (i, j) for i in range(2) for j in range(2)]
     for i in range(2):
         a, b = 512 * i, 512 * i + 512
-        V(lambda e, a=a, b=b: e.tensor_scalar(T.tmpi[:, a:b], T.pkt[:, a:b], 4095, None, A.bitwise_and), ["pkt%d" % i], ["tmpi%d" % i], 512)
-        V(lambda e, a=a, b=b: e.tensor_scalar(T.pkt[:, a:b], T.pkt[:, a:b], 12, None, A.arith_shift_right), [], ["pkt%d" % i], 512)
+        V(lambda e, a=a, b=b: e.tensor_scalar(T.tmpi[:, a:b], T.pkt[:, a:b], 4095, None, A.bitwise_and), ["pkt%d" % i], ["tmpi%d" % i], 512,
+          at=(-4.7, -4.3)[i])
+        V(lambda e, a=a, b=b: e.tensor_scalar(T.tmpj[:, a:b], T.pkt[:, a:b], 12, None, A.arith_shift_right), ["pkt%d" % i], ["tmpj%d" % i], 512,
+          at=(-4.5, -4.2)[i])
         Sc(lambda e, a=a, b=b: e.activation(T.tab[:, a:b], T.tmpi[:, a:b], AF.Copy), ["tmpi%d" % i], ["tab%d0" % i], 512)
-        Sc(lambda e, a=a, b=b: e.activation(T.tab[:, 1024 + a:1024 + b], T.pkt[:, a:b], AF.Copy), ["pkt%d" % i], ["tab%d1" % i], 512)
+        Sc(lambda e, a=a, b=b: e.activation(T.tab[:, 1024 + a:1024 + b], T.tmpj[:, a:b], AF.Copy), ["tmpj%d" % i], ["tab%d1" % i], 512)
 
     def place(t, s, h):
         base = 100.0 * t + PERIOD * (2 * s + h)
-        return lambda name: base + PLACE[name]
+        return lambda name: base + PLACE[name] if s + 1 in PLACED else None
 
     def choice(h, s, t):
         c, at = slice(4 * h, 4 * h + 4), place(t, s, h)
-        key, sch = T.sch[:, 64 * h + (15 if s else 14):64 * h + 64:16, s], "sch%d%d" % (s, h)
-        row, rn = (T.pp[:, c, s + 4], "pp%d%d" % (s, h)) if s < S else (T.p5[:, c], "p5%d" % h)
-        if s == 0 or s == S:
-            def at(name):
-                return None
+        key, sch = T.sch[:, 64 * h + 15:64 * h + 64:16, s], "sch%d%d" % (s, h)
+        row, rn = T.pp[:, c, s + 4], "pp%d%d" % (s, h)
         V(lambda e: e.tensor_scalar(row, key, 11, 63, A.arith_shift_right, A.bitwise_and), [sch], [rn], at=at("row"))
         if s < S:
             V(lambda e: e.tensor_scalar(T.cc[:, c, s], key, 2047, None, A.bitwise_and), [sch], ["cc%d%d" % (s, h)], at=at("court"))
             V(lambda e: e.tensor_copy(T["lst%d" % h][:, 0::2], T.cc[:, c, s]), ["cc%d%d" % (s, h)], ["lst%d" % h], at=at("lst"))
-        if s:
-            V(lambda e: e.tensor_scalar(T["lf%d" % h][:], row, T.y64[:, 0:1], None, A.add), [rn, "y64"], ["lf%d" % h], at=at("lf"))
-            SG(lambda e: e.activation(T["fh%d" % h][:, 64 * s - 64:64 * s], T["ab%d" % h][:].indirect(T["lf%d" % h][:]), AF.Copy),
-               ["lf%d" % h] + ["ab%d_%d" % (h, y) for y in range(16)], ["fh%d_%d" % (h, s)], 64, at=at("fh"))
+        V(lambda e: e.tensor_scalar(T["lf%d" % h][:], row, T.y64[:, 0:1], None, A.add), [rn, "y64"], ["lf%d" % h], at=at("lf"))
+        SG(lambda e: e.activation(T["fh%d" % h][:, 64 * s - 64:64 * s], T["ab%d" % h][:].indirect(T["lf%d" % h][:]), AF.Copy),
+           ["lf%d" % h] + ["ab%d_%d" % (h, y) for y in range(16)], ["fh%d_%d" % (h, s)], 64, at=at("fh"))
 
     def step(h, s, t):
         eu, rg, ab, kp, ft, fw = "eu%d" % h, "rg%d" % h, "ab%d" % h, "kp%d" % h, "ft%d" % h, "fw%d" % t
         c, at = slice(4 * h, 4 * h + 4), place(t, s - 1, h)
-        op("v", [lambda e, i=i: e.tensor_copy(T[eu][:, i::4], T.tab[:].indirect(T["lst%d" % h][:, 2 * i:2 * i + 1])) for i in range(4)],
-           TAB + ["lst%d" % h], [eu], 4 * (0.05 + GATH * 16 * CYC), at=at("eu"))
+        ln, lo = ("lst%d" % h, 0) if s > 1 else ("lsts", 8 * h)
+        op("v", [lambda e, i=i: e.tensor_copy(T[eu][:, i::4], T.tab[:, 0:2048].indirect(T[ln][:, lo + 2 * i:lo + 2 * i + 1])) for i in range(4)],
+           TAB[1:] + [ln], [eu], 4 * (0.05 + GATH * 16 * CYC), at=at("eu"))
         src, sn = (T["fin%d" % t][:, 64 * h:64 * h + 64], "fin%d%d" % (t, h)) if s == 1 else (
             T["fh%d" % h][:, 64 * s - 128:64 * s - 64], "fh%d_%d" % (h, s - 1))
         PEn(lambda e: e.transpose(T.pft[0:64, 0:128], src, T.idb[:]), [sn, "idb"], ["pft"], 128, at=at("turn"))
@@ -343,7 +419,7 @@ def rank_program(g, core, T, topo):
              lambda e: e.matmul(T[kp][:, 0:64], T.idb[:], T[fw][:, 4 * h:4 * h + 4, :], False, False),
              lambda e: e.matmul(T[kp][:, 0:64], T.idb[:], T[fw][:, 8 + 4 * h:12 + 4 * h, :], False, False)],
             ["c64", "cst0", "cst1", "idb", fw + "a", fw + "b"], [kp], 192, at=at("pay"))
-        for i, (q, y0, y1) in enumerate(GATHERS):
+        for i, (q, y0, y1) in enumerate(OTHER.get((s, h), GATHERS)):
             col, lst, rk = slice(64 * y0, 64 * y1), T[eu][:, 4 * y0:4 * y1], [rg + "_%d" % y for y in range(y0, y1)]
             if q == "s":
                 SG(lambda e, col=col, lst=lst: e.activation(T[rg][:, col], T.rtt[:].indirect(lst), AF.Copy), ["rtt", eu], rk,
@@ -354,108 +430,137 @@ def rank_program(g, core, T, topo):
         for b, (y0, y1) in enumerate(BANKS):
             col, pd, n, keys = slice(64 * y0, 64 * y1), "pd%d" % b, 64 * (y1 - y0), range(y0, y1)
             rk, ak = [rg + "_%d" % y for y in keys], [ab + "_%d" % y for y in keys]
-            PEn(lambda e, col=col, pd=pd, n=n: e.matmul(T[pd][:, 0:n], T[ft][:], T.nd[:, col], True, False), [ft] + ND, [pd], n,
+            PEn(lambda e, col=col, pd=pd, n=n: e.matmul(T[pd][:, 0:n], T[ft][:], T.nd[:, col], True, False), [ft] + ND[y0 // 4:(y1 + 3) // 4], [pd], n,
                 at=at("n%d" % b))
-            PEn(lambda e, col=col, pd=pd, n=n: e.matmul(T[pd][:, 0:n], T.idb[:], T[rg][:, col], False, True), ["idb"] + rk, [pd], n,
+            PEn(lambda e, col=col, pd=pd, n=n: e.matmul(T[pd][:, 0:n], T.idb[:], T[rg][:, col], False, True), ["idb"] + rk, ["+" + pd], n,
                 at=at("i%d" % b))
             Sc(lambda e, col=col, pd=pd, n=n: e.activation(T[ab][:, col], T[pd][:, 0:n], AF.Abs), [], [pd] + ak, n, at=at("a%d" % b))
             PEn([lambda e, y=y: e.matmul(T[kp][:, 0:64], sel(y), T[ab][:, 64 * y:64 * y + 64], False, y == BANKS[-1][1] - 1)
-                 for y in keys], ["sel"] + ak, [kp], n, at=at("m%d" % b))
+                 for y in keys], ["sel"] + ak, ["+" + kp], n, at=at("m%d" % b))
         V(lambda e: e.tensor_tensor_scan(T.sch[:, 64 * h:64 * h + 64, s], T.km[:], T[kp][:, 0:64], 0.0, A.max, A.min), ["km"], [kp, "sch%d%d" % (s, h)],
           at=place(t, s, h)("scan"))
 
     def both(name, steps):
         return ["%s%d%d" % (name, s, h) for s in steps for h in HS]
 
-    def early(t):
-        PP = both("pp", range(S)) + ["ppad"]
+    def early(hs, t):
+        a, b = 4 * hs[0], 4 * hs[-1] + 4
+        c, m = slice(a, b), b - a
+
+        def nm(*names):
+            return [x + "_%d" % h for x in names for h in hs]
+
+        def steps(name, r):
+            return ["%s%d%d" % (name, s, h) for s in r for h in hs]
+        PP = steps("pp", range(S)) + ["ppad"]
+        c5, cc = slice(5 * a, 5 * b), T.cs[:, 25 * a + 4:25 * b:5]
         for d in range(1, 5):
-            V(lambda e, d=d: e.tensor_tensor(T.eq[:, d - 1::5], T.pp[:, :, 4:9], T.pp[:, :, 4 - d:9 - d], A.is_equal),
-              PP + ["eq0"], ["eq%d" % d], 80)
-        V(lambda e: e.tensor_tensor_scan(T.cs[:], T.m25[:], T.eq[:], 0.0, A.mult, A.max),
-          ["m25"] + ["eq%d" % d for d in range(6)], ["cs"], 200)
-        V(lambda e: e.tensor_tensor(T.tq[:], T.cs[:, 4::5], T.dum[:], A.mult), ["cs", "dum"], ["tq"], 80)
-        V(lambda e: e.tensor_tensor(T.so[:, 0:40], T.tq[:], T.cc[:], A.max), ["tq", "so0"] + both("cc", range(S)), ["so"], 80)
-        VG(lambda e: e.tensor_copy(T.soff[:], T.so[:].indirect(T.l5[:])), ["so", "l5"], ["soff"], 64)
-        for h in HS:
+            V(lambda e, d=d: e.tensor_tensor(T.eq[:, 25 * a + d - 1:25 * b:5], T.pp[:, c, 4:9], T.pp[:, c, 4 - d:9 - d], A.is_equal),
+              PP + ["eq0"], nm("eq%d" % d), 10 * m)
+        V(lambda e: e.tensor_tensor_scan(T.cs[:, 25 * a:25 * b], T.m25[:, 0:25 * m], T.eq[:, 25 * a:25 * b], 0.0, A.mult, A.max),
+          ["m25", "eq5"] + nm("eq1", "eq2", "eq3", "eq4"), nm("cs"), 25 * m)
+        V(lambda e: e.tensor_tensor(T.tq[:, c5], cc, T.dum[:, c], A.mult), nm("cs") + ["dum"], nm("tq"), 10 * m)
+        V(lambda e: e.tensor_tensor(T.so[:, c5], T.tq[:, c5], T.cc[:, c], A.max), nm("tq") + ["so0"] + steps("cc", range(S)), ["so"], 10 * m)
+        VG(lambda e: e.tensor_copy(T.soff[:, 8 * a:8 * b], T.so[:].indirect(T.l5[:, a // 2:b // 2])), ["so", "l5"], nm("soff"), 8 * m)
+        for h in hs:
             SG(lambda e, h=h: e.activation(T.eall[:, 320 * h:320 * h + 320], T.tab[:].indirect(T.soff[:, 32 * h:32 * h + 20]), AF.Copy),
-               TAB + ["soff"], ["eall%d" % h], 320)
-        V(lambda e: e.tensor_tensor_scan(T.sm[:], T.m5a[:], T.cs[:, 4::5], 0.0, A.mult, A.add), ["m5a", "cs"], ["sm"])
-        V(lambda e: e.tensor_scalar(T.fl[:], T.sm[:, 4::5], -64.0, 319.0, A.mult, A.add), ["sm"], ["fl"])
-        Sc(lambda e: e.activation(T.cep[:, :, 0], T.sm[:, 4::5], AF.Copy), ["sm", "cep0"], ["ceps"])
-        Sc(lambda e: e.activation(T.ppf[:], T.pp[:, :, 1:9], AF.Copy), PP, ["ppf"])
-        V(lambda e: e.tensor_tensor(T.cl[:, 1:40], T.cs[:, 9::5], T.cs[:, 4:195:5], A.is_gt), ["cs", "cl0"], ["cl"], 80)
-        V(lambda e: e.tensor_tensor(T.clp[:], T.cl[:], T.pp[:, :, 4:9], A.mult), ["cl"] + PP, ["clp"], 80)
-        V(lambda e: e.tensor_tensor_scan(T.rr[:, 0:40], T.m5b[:], T.clp[:], 0.0, A.mult, A.subtract), ["m5b", "clp", "rr0"], ["rr"])
-        VG(lambda e: e.tensor_tensor(T.qq[:], T.rr[:].indirect(T.lb[:]), T.ppf[:], A.add), ["rr", "lb", "ppf"], ["qq"], 64)
-        Sc(lambda e: e.activation(T.ncc[:], T.cs[:, 24::25], AF.Copy, scale=-1.0, bias=1.0), ["cs"], ["ncc"])
-        V(lambda e: e.tensor_scalar(T.dd[:], T.sch[:, 15::16, 0:5], 17, None, A.arith_shift_right), ["d0"] + both("sch", range(1, S)), ["dd"])
-        V(lambda e: e.tensor_tensor(T.ad[:, 1:40], T.dd[:, 1:40], T.dd[:, 0:39], A.add), ["dd"], ["ad"], 80)
-        V(lambda e: e.tensor_scalar(T.ad[:], T.ad[:], T.zc[:, 0:1], None, A.add), ["zc"], ["ad"])
-        V(lambda e: e.tensor_scalar(T.pri[:], T.ad[:], 1, None, A.bitwise_and), ["ad"], ["pri"])
-        V(lambda e: e.tensor_tensor(T.cep[:, :, 3:7], T.pri[:, :, 1:5], T.ce[:, :, 0:4], A.mult), ["pri", "ce", "cep0"], ["cep"])
-        Sc(lambda e: e.activation(T.pm[:, :, 3:7], T.pp[:, :, 5:9], AF.Copy, bias=-64.0), PP + ["pm0"], ["pma"])
+               TAB + ["soff_%d" % h], ["eall%d" % h], 320)
+        V(lambda e: e.tensor_tensor_scan(T.sm[:, c5], T.m5a[:, 0:5 * m], cc, 0.0, A.mult, A.add), ["m5a"] + nm("cs"), nm("sm"))
+        V(lambda e: e.tensor_scalar(T.fl[:, c], T.sm[:, 5 * a + 4:5 * b:5], -64.0, 319.0, A.mult, A.add), nm("sm"), nm("fl"))
+        Sc(lambda e: e.activation(T.cep[:, c, 0], T.sm[:, 5 * a + 4:5 * b:5], AF.Copy), nm("sm") + ["cep0"], nm("ceps"))
+        Sc(lambda e: e.activation(T.ppf[:, 8 * a:8 * b], T.pp[:, c, 1:9], AF.Copy), PP, nm("ppf"))
+        Sc(lambda e: e.activation(T.shut[:, c5], T.tq[:, c5], AF.Sign), nm("tq"), nm("shut"))
+        V(lambda e: e.tensor_scalar(T.dd[:, c5], T.sch[:, 16 * a + 15:16 * b:16, 0:5], 17, 1, A.arith_shift_right, A.bitwise_and),
+          ["d0"] + steps("sch", range(1, S)), nm("dd"))
+        V(lambda e: e.tensor_tensor(T.ad[:, 5 * a + 1:5 * b], T.dd[:, 5 * a + 1:5 * b], T.dd[:, 5 * a:5 * b - 1], A.not_equal),
+          nm("dd") + ["ad0"], nm("ad"), 10 * m)
+        Sc(lambda e: e.activation(T.pri[:, c], T.ad[:, c5], AF.Abs, bias=T.zm[:, 0:1]), nm("ad") + ["zm"], nm("pri"))
+        V(lambda e: e.tensor_tensor(T.cep[:, c, 3:7], T.pri[:, c, 1:5], T.ce[:, c, 0:4], A.mult), nm("pri") + ["ce", "cep0"], nm("cep"))
 
     def late(h, t):
         c, n, w = slice(4 * h, 4 * h + 4), str(h), slice(320 * h, 320 * h + 320)
         x = slice(64 * h, 64 * h + 64)
         fout, fn = T.fout[:, 128 * t + 64 * h:128 * t + 64 * h + 64], "fout%d%d" % (t, h)
         SG(lambda e: e.activation(fout, T["fh" + n][:].indirect(T.fl[:, c]), AF.Copy),
-           ["fl"] + ["fh%d_%d" % (h, s) for s in range(1, S + 1)], [fn], 64)
+           ["fl_" + n] + ["fh%d_%d" % (h, s) for s in range(1, S + 1)], [fn], 64)
         if t == VI - 1:
             dma("y", T.yf[:, x], fout, [fn], ["yf" + n], "oyf" + n, 1.5)
         else:
             send(T["fin%d" % (t + 1)][:, x], fout, [fn], 1, "rf%d%d" % (t + 1, h), ["fin%d%d" % (t + 1, h)])
         z = slice(32 * h, 32 * h + 32)
-        V(lambda e: e.tensor_tensor(T.w5[:, 20 * h + 4:20 * h + 20:5], T.p5[:, c], T.ncc[:, c], A.mult), ["p5" + n, "ncc", "w50"], ["w5"])
-        Sc(lambda e: e.activation(T.pm[:, c, 7], T.p5[:, c], AF.Copy, bias=-64.0), ["p5" + n, "pm0"], ["pm_" + n])
-        VG(lambda e: e.tensor_tensor(T.st[:, z], T.w5[:].indirect(T.lb[:, 2 * h:2 * h + 2]), T.qq[:, z], A.is_equal),
-           ["w5", "lb", "qq"], ["st" + n], 32)
+        c5, PP = slice(20 * h, 20 * h + 20), ["pp%d%d" % (s, h) for s in range(1, S + 1)]
+        V(lambda e: e.tensor_tensor(T.pw[:, c5], T.pp[:, c, 5:10], T.tq[:, c5], A.subtract), PP + ["tq_" + n], ["pw" + n])
+        V(lambda e: e.tensor_tensor_scan(T.w5[:, c5], T.shut[:, c5], T.pw[:, c5], 0.0, A.mult, A.max), ["pw" + n, "shut_" + n, "w50"], ["w5"])
+        Sc(lambda e: e.activation(T.pm[:, c, 3:8], T.pp[:, c, 5:10], AF.Copy, bias=-64.0), PP + ["pm0"], ["pm_" + n])
+        VG(lambda e: e.tensor_tensor(T.st[:, z], T.w5[:].indirect(T.lb[:, 2 * h:2 * h + 2]), T.ppf[:, z], A.is_equal),
+           ["w5", "lb", "ppf_" + n], ["st" + n], 32)
         V(lambda e: e.tensor_tensor_scan(T.lp[:, z], T.m8b[:], T.st[:, z], 0.0, A.mult, A.max), ["m8b", "st" + n], ["lp" + n])
-        V(lambda e: e.tensor_tensor(T.zb[:, z], T.st[:, z], T.cep[:, c], A.mult), ["st" + n, "cep", "ceps"], ["zb" + n])
-        V(lambda e: e.tensor_tensor(T.cod[:, z], T.lp[:, z], T.pm[:, c], A.mult), ["lp" + n, "pma", "pm_" + n, "cod0"], ["cod"])
+        V(lambda e: e.tensor_tensor(T.zb[:, z], T.st[:, z], T.cep[:, c], A.mult), ["st" + n, "cep_" + n, "ceps_" + n], ["zb" + n])
+        V(lambda e: e.tensor_tensor(T.cod[:, z], T.lp[:, z], T.pm[:, c], A.mult), ["lp" + n, "pm_" + n, "cod0"], ["cod"])
         V(lambda e: e.tensor_tensor_scan(T.zs[:, z], T.m8a[:], T.zb[:, z], 0.0, A.mult, A.max), ["m8a", "zb" + n], ["zs" + n])
         VG(lambda e: e.tensor_scalar(T.cdl[:, z], T.cod[:].indirect(T.l8[:, 2 * h:2 * h + 2]), 64.0, None, A.add), ["cod", "l8"], ["cdl" + n], 32)
         V(lambda e: e.tensor_scalar(T.dec[:, c], T.zs[:, 32 * h + 7:32 * h + 32:8], -64.0, 319.0, A.mult, A.add), ["zs" + n], ["dec" + n])
         cdl = T.cdl[:, 32 * h:32 * h + 20]
-        SG(lambda e: e.activation(T.edec[:, x], T.eall[:, w].indirect(T.dec[:, c]), AF.Copy), ["eall" + n, "dec" + n], ["edec" + n], 64)
-        SG(lambda e: e.activation(T.hit[:, w], T.w1[:].indirect(cdl), AF.Copy), ["w1", "cdl" + n], ["hit" + n], 320)
-        VG(lambda e: e.tensor_tensor(T.aa[:, w], T.w1c[:].indirect(cdl), T.eall[:, w], A.mult), ["w1c", "cdl" + n, "eall" + n], ["aa" + n], 320)
-        VG(lambda e: e.tensor_tensor(T.edec[:, x], T.aa[:, w].indirect(T.dec[:, c]), T.edec[:, x], A.subtract),
-           ["aa" + n, "dec" + n], ["edec" + n], 64)
         pn = "kp" + n
-        PEn(lambda e: e.matmul(T[pn][:, 0:64], T.bon[:], T.edec[:, x], True, True), ["bon", "edec" + n], [pn], 256)
-        op("v", [lambda e, o=320 * h + 64 * u: e.tensor_tensor(T.bb[:, o:o + 64], T[pn][:, 0:64], T.hit[:, o:o + 64], A.mult) for u in range(S)],
-           ["hit" + n], [pn, "bb" + n], 5 * 64 * CYC)
-        VG(lambda e: e.tensor_tensor(T.tab[:].indirect(T.soff[:, 32 * h:32 * h + 20]), T.aa[:, w], T.bb[:, w], A.add),
-           ["aa" + n, "bb" + n, "soff"], TAB, 320, SCAT)
+        SG(lambda e: e.activation(T.hit[:, w], T.w1[:].indirect(cdl), AF.Copy), ["w1", "cdl" + n], ["hit" + n], 320)
+        if h in VIA_TENSOR:
+            PEn([lambda e: e.matmul(T[pn][:, 0:320], T.nid[:], T.eall[:, w], True, False),
+                 lambda e: e.matmul(T[pn][:, 0:320], T.c64[:], T.half[:], False, False)], ["nid", "eall" + n, "c64", "half"], [pn], 1600)
+            SG(lambda e: e.activation(T.edec[:, x], T.eall[:, w].indirect(T.dec[:, c]), AF.Copy, scale=-1.0, bias=1536.0),
+               ["eall" + n, "dec" + n], ["edec" + n], 64)
+            VG(lambda e: e.tensor_tensor(T.nh[:, x], T.hit[:, w].indirect(T.dec[:, c]), T.edec[:, x], A.mult),
+               ["hit" + n, "dec" + n, "edec" + n], ["nh" + n], 64)
+            PEn([lambda e, u=u: e.matmul(T[pn][:, 64 * u:64 * u + 64], T.bonh[:], T.nh[:, x], False, u == S - 1) for u in range(S)],
+                ["bonh", "nh" + n], ["+" + pn], 320)
+            V(lambda e: e.tensor_tensor(T.bb[:, w], T[pn][:, 0:320], T.hit[:, w], A.mult), ["hit" + n], [pn, "bb" + n], 320)
+            keep, kn = T.eall[:, w], "eall" + n
+        else:
+            SG(lambda e: e.activation(T.edec[:, x], T.eall[:, w].indirect(T.dec[:, c]), AF.Copy), ["eall" + n, "dec" + n], ["edec" + n], 64)
+            VG(lambda e: e.tensor_tensor(T.aa[:, w], T.w1c[:].indirect(cdl), T.eall[:, w], A.mult), ["w1c", "cdl" + n, "eall" + n], ["aa" + n], 320)
+            VG(lambda e: e.tensor_tensor(T.edec[:, x], T.aa[:, w].indirect(T.dec[:, c]), T.edec[:, x], A.subtract),
+               ["aa" + n, "dec" + n], ["edec" + n], 64)
+            PEn(lambda e: e.matmul(T[pn][:, 0:64], T.bon[:], T.edec[:, x], True, True), ["bon", "edec" + n], [pn], 256)
+            op("v", [lambda e, o=320 * h + 64 * u: e.tensor_tensor(T.bb[:, o:o + 64], T[pn][:, 0:64], T.hit[:, o:o + 64], A.mult) for u in range(S)],
+               ["hit" + n], [pn, "bb" + n], 5 * 64 * CYC)
+            keep, kn = T.aa[:, w], "aa" + n
+        VG(lambda e: e.tensor_tensor(T.tab[:].indirect(T.soff[:, 32 * h:32 * h + 20]), keep, T.bb[:, w], A.add),
+           [kn, "bb" + n, "soff_" + n], TAB, 320, SCAT)
 
     for t in range(VI):
         fin, fw = "fin%d" % t, "fw%d" % t
         V(lambda e, fw=fw: e.tensor_tensor(T.sk1[:], T[fw][:, 16, 0:8], T.cxh[:], A.add), [fw + "s", "cxh"], ["sk1"])
-        V(lambda e, fw=fw: e.tensor_tensor(T.sch[:, 14::16, 0], T[fw][:, 16, 8:16], T.sk1[:], A.add), [fw + "s", "sk1"], both("sch", [0]))
-        for h in HS:
-            choice(h, 0, t)
+        V(lambda e, fw=fw: e.tensor_tensor(T.sk[:, 0, :], T[fw][:, 16, 8:16], T.sk1[:], A.add), [fw + "s", "sk1"], ["sk"])
+        V(lambda e: e.tensor_scalar(T.sk[:, 1, :], T.sk[:, 0, :], 2047, None, A.bitwise_and), ["sk"], ["skc"])
+        V(lambda e: e.tensor_copy(T.lsts[:, 0::2], T.sk[:, 1, :]), ["skc"], ["lsts"])
+        V(lambda e: e.tensor_scalar(T.pp[:, :, 4], T.sk[:, 0, :], 11, 63, A.arith_shift_right, A.bitwise_and), ["sk"], both("pp", [0]))
+        V(lambda e: e.tensor_copy(T.cc[:, :, 0], T.sk[:, 1, :]), ["skc"], both("cc", [0]))
         for s in range(1, S + 1):
             for h in HS:
                 step(h, s, t)
                 choice(h, s, t)
+                for hs in EARLY:
+                    if s == S - 1 and hs[-1] == h:
+                        early(hs, t)
             if s == 1:
-                PEn([lambda e, y=y, fin=fin: e.matmul(T.pmis[:, 8:16], sel(y), T[fin][:, y::16], y == 0, y == 15) for y in range(16)],
-                    ["sel", fin + "0", fin + "1"], ["pmis"], 1024)
+                for y in range(16):
+                    PEn(lambda e, y=y, fin=fin: e.matmul(T.pmis[:, 8:16], sel(y), T[fin][:, y::16], y == 0, y == 15),
+                        ["sel", fin + "0", fin + "1"], ["+pmis" if y else "pmis"], 64)
                 V(lambda e: e.tensor_copy(T.sch[:, 15::16, 0], T.pmis[:, 8:16]), [], ["pmis", "d0"])
-            if s == S - 1:
-                early(t)
         for h in HS:
             late(h, t)
         if t < VI - 1:
             V(lambda e: e.tensor_reduce(T.zr[:], T.lp[:, 7::8], AxisListType.X, A.add), ["lp0", "lp1"], ["zr"])
             PEn(lambda e: e.matmul(T.pmis[:, 0:1], T.negf[:], T.zr[:], True, True), ["negf", "zr"], ["pmis"], 256)
-            V(lambda e: e.tensor_tensor(T.zc[:], T.zc[:], T.pmis[:, 0:1], A.subtract), [], ["pmis", "zc"])
+            V(lambda e: e.tensor_tensor(T.zc[:, 0:1], T.zc[:, 0:1], T.pmis[:, 0:1], A.subtract), [], ["pmis", "zc"])
+            V(lambda e: e.tensor_scalar(T.zc[:, 1:2], T.zc[:, 0:1], 1, None, A.bitwise_and), ["zc"], ["zodd"])
+            Sc(lambda e: e.activation(T.zm[:], T.zc[:, 1:2], AF.Copy, bias=-1.0), ["zodd"], ["zm"])
 
-    for i in range(4):
-        pd, o = "pd%d" % (i % 2), 256 * i
-        Sc(lambda e, pd=pd, o=o: e.activation(T[pd][:, 0:256], T.tab[:, 1024 + o:1280 + o], AF.Copy, scale=4096.0), TAB, [pd], 256)
-        V(lambda e, pd=pd, o=o: e.tensor_tensor(T.ypt[:, o:o + 256], T[pd][:, 0:256], T.tab[:, o:o + 256], A.add), TAB, [pd, "ypt%d" % i], 256)
-        dma("y", T.yp[:, o:o + 256], T.ypt[:, o:o + 256], ["ypt%d" % i], ["yp%d" % i], "oyp%d" % i, 1.5)
+    for i, (q, a, b) in enumerate(OUT):
+        pd, n = T["pd%d" % i][:, 0:b - a], "pd%d" % i
+        if q == "s":
+            Sc(lambda e, pd=pd, a=a, b=b: e.activation(pd, T.tab[:, 1024 + a:1024 + b], AF.Copy, scale=4096.0), TAB, [n], b - a)
+        else:
+            V(lambda e, pd=pd, a=a, b=b: e.tensor_scalar(pd, T.tab[:, 1024 + a:1024 + b], 4096.0, None, A.mult), TAB, [n], b - a)
+        V(lambda e, pd=pd, a=a, b=b: e.tensor_tensor(T.ypt[:, a:b], pd, T.tab[:, a:b], A.add), TAB, [n, "ypt%d" % i], b - a)
+        dma("y", T.yp[:, a:b], T.ypt[:, a:b], ["ypt%d" % i], ["yp%d" % i], "oyp%d" % i, 1.0 + (b - a) * 1.3e-3)
     finish()

@@ -7,24 +7,25 @@ NDUM = 640
 SCRATCH = {}
 for _n, _s, _d in (
         ("pkt tmpi tmpj", [128, 1024], "int32"), ("rtt", [128, 3072], "bfloat16"), ("tab", [128, 2048 + NDUM], "float32"),
-        ("jci jh jl i144", [128, 144], "int32"), ("jhb jlb selb", [128, 144], "bfloat16"),
-        ("tra trb", [128, 2, 4, 32], "bfloat16"),
+        ("jci i144", [128, 144], "int32"), ("selb", [128, 144], "bfloat16"), ("jf", [128, 144], "float16"),
+        ("tra trb", [128, 4, 32], "float16"),
         ("sri", [8, 128], "int32"), ("srb bo8", [8, 128], "bfloat16"),
-        ("fout", [128, 128 * VI], "bfloat16"), ("fin0 fin1 fin2 oneb idb ide ido", [128, 128], "bfloat16"), ("fw0 fw1 fw2", [128, 17, 16], "bfloat16"),
-        ("pi yli", [128, 1], "int32"), ("ylf y64 q2k g15 zr zm", [128, 1], "float32"),
+        ("fout", [128, 128 * VI], "bfloat16"), ("fin0 fin1 fin2 oneb idb ide ido", [128, 128], "bfloat16"),
+        ("fw0 fw1 fw2", [128, 9, 16], "float16"),
+        ("pi yli", [128, 1], "int32"), ("ylf y64 g15 zr zm", [128, 1], "float32"),
         ("i80", [128, 80], "int32"), ("w1", [128, 80], "float32"),
-        ("negf bon edec nid", [128, 128], "float32"), ("ms", [128, 256], "bfloat16"),
+        ("negf bon edec nid", [128, 128], "float32"), ("ms", [128, 256], "float16"),
         ("bonh nh", [128, 128], "float16"), ("half", [64, 320], "bfloat16"), ("nd", [64, 1024], "bfloat16"), ("ndi", [64, 256], "bfloat16"), ("cst", [64, 64], "bfloat16"), ("c64 ft0 ft1", [64, 128], "bfloat16"),
-        ("km st lp zs zb ppf", [128, 64], "float32"), ("cep pm", [128, 8, 8], "float32"), ("pp", [128, 8, 10], "int32"),
+        ("km st lp zs zb ppf", [128, 64], "float32"), ("cep", [128, 8, 8], "float32"), ("pp", [128, 8, 10], "int32"),
         ("cod", [128, 72], "float32"), ("so", [128, 48], "float32"), ("yi", [128, 3], "int32"), ("ybf y5 y8", [128, 1], "float32"),
         ("l5i l8i", [128, 4], "int32"), ("l5 l8", [128, 4], "uint16"), ("soff cdl", [128, 64], "uint16"),
         ("eq cs m25", [128, 200], "float32"), ("m8a m8b", [128, 32], "float32"),
-        ("dui dum cei ce pri", [128, 8, 5], "float32"), ("m5a sm tq shut pw ad", [128, 40], "float32"), ("w5", [128, 41], "float32"),
+        ("dui dum cei ce pri", [128, 8, 5], "float32"), ("m5a sm tq pw ad", [128, 40], "float32"), ("w5", [128, 41], "float32"),
         ("cc", [128, 8, 5], "int32"), ("dd", [128, 40], "int32"), ("zc", [128, 2], "int32"),
-        ("bsi cxh sk1", [128, 8], "float32"), ("hz", [128, 2], "float32"),
+        ("bsi cxh sk", [128, 8], "float32"), ("hz", [128, 2], "float32"),
         ("lbi", [128, 4], "int32"), ("lb lf0 lf1", [128, 4], "uint16"), ("lst0 lst1 fl dec", [128, 8], "uint16"),
         ("sch", [128, 128, S + 1], "int32"), ("eall hit bb", [128, NDUM], "float32"),
-        ("sk", [128, 2, 8], "int32"), ("lsts", [128, 16], "uint16"),
+        ("lsts", [128, 16], "uint16"),
         ("ypt", [128, 1024], "float32"), ("eu0 eu1", [128, 64], "uint16"),
         ("fh0 fh1", [128, 320], "bfloat16"), ("rg0 rg1", [128, 1024], "bfloat16"),
         ("ab0 ab1", [128, 1024], "bfloat16")):
@@ -35,20 +36,22 @@ for _m in "kp0 kp1 pd0 pd1 pd2 pd3 pmis".split():
 SCRATCH["pft"] = ("psum", [128, 1024], "bfloat16")
 SEMAPHORES = ("cv cs ct cg lpk0 lpk1 lrt0 lrt1 ljc ljw lsr lfx rw1 rw2 rf10 rf11 rf20 rf21 lsend oyf0 oyf1 "
               "oyp0 oyp1 oyp2 oyp3").split()
-GATHERS = (("s", 0, 4), ("v", 4, 8), ("v", 8, 12), ("v", 12, 14), ("v", 14, 16))
+GATHERS = (("s", 0, 5), ("v", 5, 9), ("v", 9, 12), ("v", 12, 14), ("v", 14, 16))
 OTHER = {(1, 0): (("s", 0, 4), ("v", 4, 8), ("s", 8, 12), ("v", 12, 16))}
-BANKS = ((0, 4), (4, 8), (8, 12), (12, 16))
+BANKS = ((5, 9), (0, 5), (9, 12), (12, 16))
 PERIOD = 2.0
-PLACE = {"scan": 0.0, "row": 0.04, "court": 0.03, "lf": 0.44, "lst": 0.43, "fh": 0.48, "eu": 0.78, "turn": 0.79, "ft": 1.19,
-         "pay": 0.41, "g0": 1.96, "g1": 1.32, "g2": 1.04, "g3": 2.02, "g4": 2.2,
-         "n0": 1.1, "i0": 1.24, "n1": 1.25, "i1": 1.69, "n2": 1.70, "i2": 1.97, "n3": 1.98, "i3": 2.43,
-         "a0": 2.08, "a1": 2.33, "a2": 2.34, "a3": 3.4, "m0": 2.44, "m1": 2.78, "m2": 3.01, "m3": 3.08}
-CYC, GATH, SCAT, PE, LAG = 0.95e-3, 1.56, 3.8, 0.48e-3, 0.2
-DEPTH, SLACK, ROUNDS, FREE = 1, 0.1, 8, False
+PLACE = {"scan": 0.0, "row": 0.04, "court": 0.05, "lf": 0.43, "lst": 0.425, "fh": 0.45, "eu": 0.78, "turn": 0.52, "ft": 1.1,
+         "pay": 0.51, "g0": 1.3, "g1": 1.0, "g2": 1.3, "g3": 2.02, "g4": 2.41,
+         "n0": 1.2, "i0": 1.25, "n1": 1.3, "i1": 1.75, "n2": 1.5, "i2": 2.01, "n3": 1.99, "i3": 2.45,
+         "a0": 1.7, "a1": 2.1, "a2": 2.6, "a3": 2.9, "m0": 2.44, "m1": 2.5, "m2": 2.95, "m3": 3.1}
+CYC, GATH, SCAT, PE, LAG = 1.0e-3, 1.56, 3.8, 0.5e-3, 0.2
+DEPTH, SLACK, ROUNDS, FREE = 1, 0.2, 8, True
 PLACED = (2, 3, 4, 5)
 EARLY = ((0,), (1,))
+PARITY = ((0, 1),)
 VIA_TENSOR = (0, 1)
 OUT = (("v", 0, 256), ("s", 256, 576), ("s", 576, 832), ("s", 832, 1024))
+PIECES = (((0, 10), (10, 20)), ((0, 20),))
 ORDER = []
 
 
@@ -268,7 +271,7 @@ def rank_program(g, core, T, topo):
         rid, pid = topo.addr(dst, core)
         op("g", lambda e: e.remote_dma(dst_ap, src_ap, T.sem[sem], T.sem.lsend, pid, rid, topo.mask(core, dst)),
            r, ["@" + sem], 0.3, "lsend", len(topo.engines(core, dst)), 0.3)
-        op("x" + sem, None, ["@" + sem], lands, 1.5, sem, len(topo.engines(T.cores[(rank - t) % N], core)))
+        op("x" + sem, None, ["@" + sem], lands, 3.0, sem, len(topo.engines(T.cores[(rank - t) % N], core)))
 
     dma("y", T.jci[:, 0:128], T.jc[:], [], ["jci"], "ljc", 1.2, -9)
     dma("s", T.jci[:, 128:144], T.jc[:, 0:16], [], ["jcw"], "ljw", 1.2, -9)
@@ -288,24 +291,22 @@ def rank_program(g, core, T, topo):
     G(lambda e: e.affine_select(T.bo8[:], T.oneb[0:8, :], [[1, 8], [0, 16]], A.is_equal, 0.0, 0, -1), ["oneb"], ["bo8"], 128)
     G(lambda e: e.affine_select(T.idb[:], T.oneb[:], [[-1, 128]], A.is_equal, 0.0, 0, 1), ["oneb"], ["idb"], 128)
     G(lambda e: e.affine_select(T.ide[:], T.idb[:], [[0, 4], [-1, 2], [0, 16]], A.is_ge, 0.0, 0, 0), ["idb"], ["ide"], 128)
-    V(lambda e: e.tensor_tensor(T.ido[:], T.idb[:], T.ide[:], A.subtract), ["idb", "ide"], ["ido"], 256)
+    G(lambda e: e.affine_select(T.ido[:], T.idb[:], [[0, 4], [1, 2], [0, 16]], A.is_ge, 0.0, -1, 0), ["idb"], ["ido"], 128)
     ND = ["nd%d" % b for b in range(4)]
     for b in range(4):
         G(lambda e, b=b: e.affine_select(T.nd[:, 256 * b:256 * b + 256], T.ndi[:], [[-1, 4], [-16, 4], [0, 16]],
                                          A.is_equal, 0.0, -4 * b, 1), ["ndi"], [ND[b]], 256)
-    G(lambda e: e.iota(T.cst[0:32, :], [[16, 4], [0, 16]], 0, 0, **flag), [], ["cst0"], 64)
+    G(lambda e: e.iota(T.cst[0:32, :], [[1, 64]], 0, 0, **flag), [], ["cst0"], 64)
     V(lambda e: e.memset(T.cst[32:64, :], -7680.0), [], ["cst1"])
     V(lambda e: e.memset(T.c64[:], 64.0), [], ["c64"])
     V(lambda e: e.tensor_scalar(T.yli[:], T.pi[:], 15, None, A.bitwise_and), ["pi"], ["yli"])
     V(lambda e: e.tensor_copy(T.ylf[:], T.yli[:]), ["yli"], ["ylf"])
-    V(lambda e: e.tensor_scalar(T.q2k[:], T.yli[:], 2048.0, None, A.mult), ["yli"], ["q2k"])
     V(lambda e: e.tensor_scalar(T.y64[:], T.yli[:], 64.0, None, A.mult), ["yli"], ["y64"])
     V(lambda e: e.tensor_scalar(T.g15[:], T.pi[:], T.ylf[:, 0:1], 15.0, A.subtract, A.add), ["pi", "ylf"], ["g15"])
     V(lambda e: e.tensor_scalar(T.selb[:], T.i144[:], T.g15[:, 0:1], 131072.0, A.is_equal, A.mult), ["i144", "g15"], ["sel"], 144)
     V(lambda e: e.memset(T.km[:], -1.0e9), [], ["km"])
     V(lambda e: e.memset(T.km[:, 0::16], 1.0e9), ["km"], ["km"])
-    G(lambda e: e.iota(T.cxh[:], [[0, 2], [1, 4]], 0, 0, **flag), [], ["cxh"], 8)
-    Sc(lambda e: e.activation(T.cxh[:], T.cxh[:], AF.Copy, scale=32768.0), ["cxh"], ["cxh"])
+    G(lambda e: e.iota(T.cxh[:], [[0, 2], [16, 4]], 0, 0, **flag), [], ["cxh"], 8)
     G(lambda e: e.iota(T.pp[:, :, 0:4], [[0, 32]], -1000, 0), [], ["ppad"], 32)
     G(lambda e: e.iota(T.tab[:, 2048:], [[0, NDUM]], 0, 0, **flag), [], ["tabd"], NDUM)
 
@@ -315,12 +316,14 @@ def rank_program(g, core, T, topo):
     V(lambda e: e.tensor_scalar(T.i80[:], T.i144[:, 0:80], 79, None, A.bitwise_and), ["i144"], ["i80"], 80)
     V(lambda e: e.tensor_scalar(T.w1[:], T.i80[:], T.ylf[:, 0:1], None, A.is_equal), ["i80", "ylf"], ["w1"], 80)
     G(lambda e: e.iota(T.m25[:], [[0, 200]], 1, 0, **flag), [], ["m25"], 200)
-    for n, width, cases, last in (("m5a", 5, 8, 0), ("m8a", 8, 4, 0), ("m8b", 8, 4, 1)):
+    for n, width, cases, last in (("m5a", 5, 8, 0), ("m8a", 8, 4, 0)):
         G(lambda e, n=n, width=width, cases=cases, last=last: e.affine_select(
             T[n][:], T.m25[:, 0:width * cases], [[0, cases], [1, width]], A.is_gt, 0.0, -last, 0), ["m25"], [n], 40)
     for i in (4, 5):
-        G(lambda e, i=i: e.iota(T.m25[:, i::25], [[0, 8]], 0, 0, **flag), [], ["m25"], 8)
-    for n, size, value in (("eq", 200, 0), ("w5", 41, -1000), ("cep", 64, 0), ("pm", 64, 0), ("dum", 40, 0),
+        G(lambda e, i=i: e.iota(T.m25[:, i::25], [[0, 8]], -1000, 0, **flag), [], ["m25"], 8)
+    G(lambda e: e.iota(T.m8b[:], [[0, 32]], 0, 0, **flag), [], ["m8b"], 32)
+    G(lambda e: e.iota(T.m8b[:, 1::8], [[0, 4]], 64, 0, **flag), [], ["m8b"], 4)
+    for n, size, value in (("eq", 200, 0), ("w5", 41, -1000), ("cep", 64, 0), ("dum", 40, 0),
                            ("cod", 72, 0), ("so", 48, 0)):
         G(lambda e, n=n, size=size, value=value: e.iota(T[n][:], [[0, size]], value, 0, **flag), [], [n + "0"], size)
     G(lambda e: e.iota(T.ad[:, 0::20], [[0, 2]], 0, 0, **flag), [], ["ad0"], 2)
@@ -341,42 +344,35 @@ def rank_program(g, core, T, topo):
     for n, k in (("5", 5.0), ("8", 8.0)):
         Sc(lambda e, n=n, k=k: e.activation(T["y" + n][:], T.yi[:, 0:1], AF.Identity, bias=T.ybf[:, 0:1], scale=k), ["ya", "ybf"], ["y" + n])
         V(lambda e, n=n: e.tensor_scalar(T["l" + n][:], T["l%si" % n][:], T["y" + n][:, 0:1], None, A.add), ["l%si" % n, "y" + n], ["l" + n])
-    G(lambda e: e.iota(T.bsi[:], [[0, 2], [-16, 4]], 63, 0, **flag), [], ["bsi"], 8)
+    G(lambda e: e.iota(T.bsi[:], [[0, 2], [-16, 4]], -1, 0, **flag), [], ["bsi"], 8)
     G(lambda e: e.iota(T.lbi[:], [[10, 4]], 4, 0), [], ["lbi"], 4)
     Sc(lambda e: e.activation(T.dum[:, :, 1:5], T.dui[:, :, 1:5], AF.Identity, bias=T.ylf[:, 0:1]), ["dui", "ylf", "dum0"], ["dum"])
-    V(lambda e: e.tensor_scalar(T.ce[:], T.cei[:], T.ylf[:, 0:1], 1.0 / 64, A.subtract, A.mult), ["cei", "ylf"], ["ce"])
+    V(lambda e: e.tensor_scalar(T.ce[:], T.cei[:], T.ylf[:, 0:1], 1.0 / 512, A.subtract, A.mult), ["cei", "ylf"], ["ce"])
     V(lambda e: e.tensor_scalar(T.eq[:, 4::25], T.bsi[:], T.ylf[:, 0:1], 1.0 / 64, A.subtract, A.mult), ["bsi", "ylf", "eq0"], ["eq5"])
     V(lambda e: e.tensor_scalar(T.hz[:, 0:1], T.ylf[:], 8.0, 5.0, A.is_ge, A.mult), ["ylf"], ["h8"])
     V(lambda e: e.tensor_scalar(T.yi[:, 2:3], T.pi[:], 7, None, A.bitwise_and), ["pi"], ["y8i"])
     V(lambda e: e.tensor_scalar(T.hz[:, 1:2], T.yi[:, 2:3], 0.0, 40.0, A.is_equal, A.mult), ["y8i"], ["z40"])
     V(lambda e: e.tensor_scalar(T.lb[:], T.lbi[:], T.hz[:, 0:1], T.hz[:, 1:2], A.add, A.max), ["lbi", "h8", "z40"], ["lb"])
 
-    V(lambda e: e.tensor_scalar(T.jh[:], T.jci[:], 8, None, A.arith_shift_right), ["jci", "jcw"], ["jh"], 144, at=-5)
-    V(lambda e: e.tensor_scalar(T.jl[:], T.jci[:], 255, None, A.bitwise_and), ["jci", "jcw"], ["jl"], 144, at=-4.9)
-    Sc(lambda e: e.activation(T.jlb[:], T.jl[:], AF.Copy), ["jl"], ["jlb"], 144)
-    V(lambda e: e.tensor_scalar(T.jhb[:], T.jh[:], 256.0, T.q2k[:, 0:1], A.mult, A.add), ["jh", "q2k"], ["jhb"], 144, at=-4.8)
-    for i, b in enumerate(("jhb", "jlb")):
-        V(lambda e, i=i, b=b: e.transpose(T.tra[:, i], T[b][:, 0:128]), [b], ["tra%d" % i])
-        V(lambda e, i=i, b=b: e.transpose(T.trb[:, i], T[b][:, 16:144]), [b], ["trb%d" % i])
-    calls = []
-    for i in range(2):
-        o = 64 * i
-        calls += [lambda e, i=i, o=o: e.matmul(T.pd0[:, o:o + 64], T.ide[:], T.tra[:, i, :, 0:16], True, False),
-                  lambda e, i=i, o=o: e.matmul(T.pd0[:, o + 16:o + 64], T.ido[:], T.trb[:, i, 0:3, 16:32], False, False),
-                  lambda e, i=i, o=o: e.matmul(T.pd0[:, o:o + 16], T.ido[:], T.trb[:, i, 3, 16:32], False, True),
-                  lambda e, i=i, o=o: e.matmul(T.pd0[:, 128 + o:192 + o], T.ide[:], T.trb[:, i, :, 0:16], True, False),
-                  lambda e, i=i, o=o: e.matmul(T.pd0[:, 128 + o:192 + o], T.ido[:], T.tra[:, i, :, 16:32], False, True)]
-    PEn(calls, ["ide", "ido", "tra0", "tra1", "trb0", "trb1"], ["pd0"], 640)
-    Sc(lambda e: e.activation(T.fw0[:, 0:16:2, :], T.pd0[:, 0:128], AF.Copy), [], ["pd0", "fw0a"], 128)
-    Sc(lambda e: e.activation(T.fw0[:, 1:16:2, :], T.pd0[:, 128:256], AF.Copy), [], ["pd0", "fw0b"], 128)
+    V(lambda e: e.tensor_copy(T.jf[:], T.jci[:]), ["jci", "jcw"], ["jf"], 144, at=-5)
+    V(lambda e: e.transpose(T.tra[:], T.jf[:, 0:128]), ["jf"], ["tra"])
+    V(lambda e: e.transpose(T.trb[:], T.jf[:, 16:144]), ["jf"], ["trb"])
+    PEn([lambda e: e.matmul(T.pd0[:, 0:64], T.ide[:], T.tra[:, :, 0:16], True, False),
+         lambda e: e.matmul(T.pd0[:, 16:64], T.ido[:], T.trb[:, 0:3, 16:32], False, False),
+         lambda e: e.matmul(T.pd0[:, 0:16], T.ido[:], T.trb[:, 3, 16:32], False, True),
+         lambda e: e.matmul(T.pd0[:, 64:128], T.ide[:], T.trb[:, :, 0:16], True, False),
+         lambda e: e.matmul(T.pd0[:, 64:128], T.ido[:], T.tra[:, :, 16:32], False, True)], ["ide", "ido", "tra", "trb"], ["pd0"], 320)
+    Sc(lambda e: e.activation(T.fw0[:, 0:8:2, :], T.pd0[:, 0:64], AF.Copy), [], ["pd0", "fw0a"])
+    Sc(lambda e: e.activation(T.fw0[:, 1:8:2, :], T.pd0[:, 64:128], AF.Copy), [], ["pd0", "fw0b"])
     Sc(lambda e: e.activation(T.srb[:], T.sri[:], AF.Copy), ["sri"], ["srb"], 128)
-    PEn(lambda e: e.matmul(T.pmis[:, 0:128], T.bo8[:], T.srb[:], True, True), ["bo8", "srb"], ["pmis"], 128)
-    V(lambda e: e.tensor_scalar(T.pmis[:, 128:256], T.pmis[:, 0:128], T.ylf[:, 0:1], None, A.is_equal), ["ylf"], ["pmis"], 128, at=-4.6)
-    op("v", [lambda e, i=i, b=b: e.tensor_tensor(T.ms[:, 128 * i:128 * i + 128], T.pmis[:, 128:256], T[b][:, 0:128], A.mult)
-             for i, b in enumerate(("jhb", "jlb"))], ["jhb", "jlb"], ["pmis", "ms"], 256 * CYC, at=-4.4)
+    for bank in ("pmis", "pd2"):
+        PEn(lambda e, bank=bank: e.matmul(T[bank][:, 0:128], T.bo8[:], T.srb[:], True, True), ["bo8", "srb"], [bank], 128)
+    Sc(lambda e: e.activation(T.ms[:, 128:256], T.pd2[:, 0:128], AF.Copy, scale=1.0 / 16), [], ["pd2", "ms1"], 128)
+    V(lambda e: e.tensor_scalar(T.pmis[:, 128:256], T.pmis[:, 0:128], T.ylf[:, 0:1], None, A.is_equal), ["ylf"], ["pmis"], 128, at=-4.65)
+    V(lambda e: e.tensor_tensor(T.ms[:, 0:128], T.pmis[:, 128:256], T.jf[:, 0:128], A.mult), ["jf"], ["pmis", "ms0"], 128, at=-4.55)
     PEn([lambda e, y=y: e.matmul(T.pd1[:, 0:16], sel(y), T.ms[:, y::16], y == 0, y == 15) for y in range(16)],
-        ["sel", "ms"], ["pd1"], 1024)
-    Sc(lambda e: e.activation(T.fw0[:, 16, :], T.pd1[:, 0:16], AF.Copy, scale=1.0 / 131072.0), [], ["pd1", "fw0s"])
+        ["sel", "ms0", "ms1"], ["pd1"], 1024)
+    Sc(lambda e: e.activation(T.fw0[:, 8, :], T.pd1[:, 0:16], AF.Copy, scale=1.0 / 131072.0), [], ["pd1", "fw0s"])
     for t in (1, 2):
         send(T["fw%d" % t][:], T.fw0[:], ["fw0a", "fw0b", "fw0s"], t, "rw%d" % t, ["fw%d%s" % (t, x) for x in "abs"])
     TAB = ["tabd"] + ["tab%d%d" % (i, j) for i in range(2) for j in range(2)]
@@ -387,7 +383,10 @@ def rank_program(g, core, T, topo):
         V(lambda e, a=a, b=b: e.tensor_scalar(T.tmpj[:, a:b], T.pkt[:, a:b], 12, None, A.arith_shift_right), ["pkt%d" % i], ["tmpj%d" % i], 512,
           at=(-4.5, -4.2)[i])
         Sc(lambda e, a=a, b=b: e.activation(T.tab[:, a:b], T.tmpi[:, a:b], AF.Copy), ["tmpi%d" % i], ["tab%d0" % i], 512)
-        Sc(lambda e, a=a, b=b: e.activation(T.tab[:, 1024 + a:1024 + b], T.tmpj[:, a:b], AF.Copy), ["tmpj%d" % i], ["tab%d1" % i], 512)
+        if i == 0:
+            Sc(lambda e, a=a, b=b: e.activation(T.tab[:, 1024 + a:1024 + b], T.tmpj[:, a:b], AF.Copy), ["tmpj0"], ["tab01"], 512)
+        else:
+            V(lambda e, a=a, b=b: e.tensor_copy(T.tab[:, 1024 + a:1024 + b], T.tmpj[:, a:b]), ["tmpj1"], ["tab11"], 512)
 
     def place(t, s, h):
         base = 100.0 * t + PERIOD * (2 * s + h)
@@ -416,9 +415,8 @@ def rank_program(g, core, T, topo):
         PEn(lambda e: e.transpose(T.pft[0:64, 0:128], src, T.idb[:]), [sn, "idb"], ["pft"], 128, at=at("turn"))
         V(lambda e: e.tensor_copy(T[ft][:], T.pft[0:64, 0:128]), [], ["pft", ft], at=at("ft"))
         PEn([lambda e: e.matmul(T[kp][:, 0:64], T.c64[:], T.cst[:], True, False),
-             lambda e: e.matmul(T[kp][:, 0:64], T.idb[:], T[fw][:, 4 * h:4 * h + 4, :], False, False),
-             lambda e: e.matmul(T[kp][:, 0:64], T.idb[:], T[fw][:, 8 + 4 * h:12 + 4 * h, :], False, False)],
-            ["c64", "cst0", "cst1", "idb", fw + "a", fw + "b"], [kp], 192, at=at("pay"))
+             lambda e: e.matmul(T[kp][:, 0:64], T.idb[:], T[fw][:, 4 * h:4 * h + 4, :], False, False)],
+            ["c64", "cst0", "cst1", "idb", fw + "a", fw + "b"], [kp], 128, at=at("pay"))
         for i, (q, y0, y1) in enumerate(OTHER.get((s, h), GATHERS)):
             col, lst, rk = slice(64 * y0, 64 * y1), T[eu][:, 4 * y0:4 * y1], [rg + "_%d" % y for y in range(y0, y1)]
             if q == "s":
@@ -457,7 +455,7 @@ def rank_program(g, core, T, topo):
         for d in range(1, 5):
             V(lambda e, d=d: e.tensor_tensor(T.eq[:, 25 * a + d - 1:25 * b:5], T.pp[:, c, 4:9], T.pp[:, c, 4 - d:9 - d], A.is_equal),
               PP + ["eq0"], nm("eq%d" % d), 10 * m)
-        V(lambda e: e.tensor_tensor_scan(T.cs[:, 25 * a:25 * b], T.m25[:, 0:25 * m], T.eq[:, 25 * a:25 * b], 0.0, A.mult, A.max),
+        V(lambda e: e.tensor_tensor_scan(T.cs[:, 25 * a:25 * b], T.m25[:, 0:25 * m], T.eq[:, 25 * a:25 * b], 0.0, A.min, A.max),
           ["m25", "eq5"] + nm("eq1", "eq2", "eq3", "eq4"), nm("cs"), 25 * m)
         V(lambda e: e.tensor_tensor(T.tq[:, c5], cc, T.dum[:, c], A.mult), nm("cs") + ["dum"], nm("tq"), 10 * m)
         V(lambda e: e.tensor_tensor(T.so[:, c5], T.tq[:, c5], T.cc[:, c], A.max), nm("tq") + ["so0"] + steps("cc", range(S)), ["so"], 10 * m)
@@ -466,10 +464,19 @@ def rank_program(g, core, T, topo):
             SG(lambda e, h=h: e.activation(T.eall[:, 320 * h:320 * h + 320], T.tab[:].indirect(T.soff[:, 32 * h:32 * h + 20]), AF.Copy),
                TAB + ["soff_%d" % h], ["eall%d" % h], 320)
         V(lambda e: e.tensor_tensor_scan(T.sm[:, c5], T.m5a[:, 0:5 * m], cc, 0.0, A.mult, A.add), ["m5a"] + nm("cs"), nm("sm"))
-        V(lambda e: e.tensor_scalar(T.fl[:, c], T.sm[:, 5 * a + 4:5 * b:5], -64.0, 319.0, A.mult, A.add), nm("sm"), nm("fl"))
-        Sc(lambda e: e.activation(T.cep[:, c, 0], T.sm[:, 5 * a + 4:5 * b:5], AF.Copy), nm("sm") + ["cep0"], nm("ceps"))
+        V(lambda e: e.tensor_scalar(T.fl[:, c], T.sm[:, 5 * a + 4:5 * b:5], -64.0, 255.0, A.mult, A.add), nm("sm"), nm("fl"))
+        Sc(lambda e: e.activation(T.cep[:, c, 0], T.sm[:, 5 * a + 4:5 * b:5], AF.Copy, scale=0.125, bias=0.125), nm("sm") + ["cep0"], nm("ceps"))
         Sc(lambda e: e.activation(T.ppf[:, 8 * a:8 * b], T.pp[:, c, 1:9], AF.Copy), PP, nm("ppf"))
-        Sc(lambda e: e.activation(T.shut[:, c5], T.tq[:, c5], AF.Sign), nm("tq"), nm("shut"))
+
+    def parity(hs):
+        a, b = 4 * hs[0], 4 * hs[-1] + 4
+        c, m, c5 = slice(a, b), b - a, slice(5 * a, 5 * b)
+
+        def nm(*names):
+            return [x + "_%d" % h for x in names for h in hs]
+
+        def steps(name, r):
+            return ["%s%d%d" % (name, s, h) for s in r for h in hs]
         V(lambda e: e.tensor_scalar(T.dd[:, c5], T.sch[:, 16 * a + 15:16 * b:16, 0:5], 17, 1, A.arith_shift_right, A.bitwise_and),
           ["d0"] + steps("sch", range(1, S)), nm("dd"))
         V(lambda e: e.tensor_tensor(T.ad[:, 5 * a + 1:5 * b], T.dd[:, 5 * a + 1:5 * b], T.dd[:, 5 * a:5 * b - 1], A.not_equal),
@@ -488,18 +495,18 @@ def rank_program(g, core, T, topo):
         else:
             send(T["fin%d" % (t + 1)][:, x], fout, [fn], 1, "rf%d%d" % (t + 1, h), ["fin%d%d" % (t + 1, h)])
         z = slice(32 * h, 32 * h + 32)
-        c5, PP = slice(20 * h, 20 * h + 20), ["pp%d%d" % (s, h) for s in range(1, S + 1)]
+        c5, PP = slice(20 * h, 20 * h + 20), ["pp%d%d" % (s, h) for s in range(S + 1)] + ["ppad"]
         V(lambda e: e.tensor_tensor(T.pw[:, c5], T.pp[:, c, 5:10], T.tq[:, c5], A.subtract), PP + ["tq_" + n], ["pw" + n])
-        V(lambda e: e.tensor_tensor_scan(T.w5[:, c5], T.shut[:, c5], T.pw[:, c5], 0.0, A.mult, A.max), ["pw" + n, "shut_" + n, "w50"], ["w5"])
-        Sc(lambda e: e.activation(T.pm[:, c, 3:8], T.pp[:, c, 5:10], AF.Copy, bias=-64.0), PP + ["pm0"], ["pm_" + n])
-        VG(lambda e: e.tensor_tensor(T.st[:, z], T.w5[:].indirect(T.lb[:, 2 * h:2 * h + 2]), T.ppf[:, z], A.is_equal),
+        V(lambda e: e.tensor_tensor_scan(T.w5[:, c5], T.cs[:, 100 * h + 4:100 * h + 100:5], T.pw[:, c5], 0.0, A.mult, A.max),
+          ["pw" + n, "cs_" + n, "w50"], ["w5"])
+        VG(lambda e: e.tensor_tensor(T.st[:, z], T.w5[:].indirect(T.lb[:, 2 * h:2 * h + 2]), T.ppf[:, z], A.not_equal),
            ["w5", "lb", "ppf_" + n], ["st" + n], 32)
-        V(lambda e: e.tensor_tensor_scan(T.lp[:, z], T.m8b[:], T.st[:, z], 0.0, A.mult, A.max), ["m8b", "st" + n], ["lp" + n])
-        V(lambda e: e.tensor_tensor(T.zb[:, z], T.st[:, z], T.cep[:, c], A.mult), ["st" + n, "cep_" + n, "ceps_" + n], ["zb" + n])
-        V(lambda e: e.tensor_tensor(T.cod[:, z], T.lp[:, z], T.pm[:, c], A.mult), ["lp" + n, "pm_" + n, "cod0"], ["cod"])
+        V(lambda e: e.tensor_tensor_scan(T.lp[:, z], T.m8b[:], T.st[:, z], 0.0, A.max, A.mult), ["m8b", "st" + n], ["lp" + n])
+        V(lambda e: e.tensor_tensor(T.zb[:, z], T.cep[:, c], T.st[:, z], A.subtract), ["st" + n, "cep_" + n, "ceps_" + n], ["zb" + n])
+        V(lambda e: e.tensor_tensor(T.cod[:, z], T.lp[:, z], T.pp[:, c, 2:10], A.max), ["lp" + n, "cod0"] + PP, ["cod"])
         V(lambda e: e.tensor_tensor_scan(T.zs[:, z], T.m8a[:], T.zb[:, z], 0.0, A.mult, A.max), ["m8a", "zb" + n], ["zs" + n])
-        VG(lambda e: e.tensor_scalar(T.cdl[:, z], T.cod[:].indirect(T.l8[:, 2 * h:2 * h + 2]), 64.0, None, A.add), ["cod", "l8"], ["cdl" + n], 32)
-        V(lambda e: e.tensor_scalar(T.dec[:, c], T.zs[:, 32 * h + 7:32 * h + 32:8], -64.0, 319.0, A.mult, A.add), ["zs" + n], ["dec" + n])
+        VG(lambda e: e.tensor_copy(T.cdl[:, z], T.cod[:].indirect(T.l8[:, 2 * h:2 * h + 2])), ["cod", "l8"], ["cdl" + n], 32)
+        V(lambda e: e.tensor_scalar(T.dec[:, c], T.zs[:, 32 * h + 7:32 * h + 32:8], -512.0, 319.0, A.mult, A.add), ["zs" + n], ["dec" + n])
         cdl = T.cdl[:, 32 * h:32 * h + 20]
         pn = "kp" + n
         SG(lambda e: e.activation(T.hit[:, w], T.w1[:].indirect(cdl), AF.Copy), ["w1", "cdl" + n], ["hit" + n], 320)
@@ -513,27 +520,17 @@ def rank_program(g, core, T, topo):
             PEn([lambda e, u=u: e.matmul(T[pn][:, 64 * u:64 * u + 64], T.bonh[:], T.nh[:, x], False, u == S - 1) for u in range(S)],
                 ["bonh", "nh" + n], ["+" + pn], 320)
             V(lambda e: e.tensor_tensor(T.bb[:, w], T[pn][:, 0:320], T.hit[:, w], A.mult), ["hit" + n], [pn, "bb" + n], 320)
-            keep, kn = T.eall[:, w], "eall" + n
-        else:
-            SG(lambda e: e.activation(T.edec[:, x], T.eall[:, w].indirect(T.dec[:, c]), AF.Copy), ["eall" + n, "dec" + n], ["edec" + n], 64)
-            VG(lambda e: e.tensor_tensor(T.aa[:, w], T.w1c[:].indirect(cdl), T.eall[:, w], A.mult), ["w1c", "cdl" + n, "eall" + n], ["aa" + n], 320)
-            VG(lambda e: e.tensor_tensor(T.edec[:, x], T.aa[:, w].indirect(T.dec[:, c]), T.edec[:, x], A.subtract),
-               ["aa" + n, "dec" + n], ["edec" + n], 64)
-            PEn(lambda e: e.matmul(T[pn][:, 0:64], T.bon[:], T.edec[:, x], True, True), ["bon", "edec" + n], [pn], 256)
-            op("v", [lambda e, o=320 * h + 64 * u: e.tensor_tensor(T.bb[:, o:o + 64], T[pn][:, 0:64], T.hit[:, o:o + 64], A.mult) for u in range(S)],
-               ["hit" + n], [pn, "bb" + n], 5 * 64 * CYC)
-            keep, kn = T.aa[:, w], "aa" + n
-        VG(lambda e: e.tensor_tensor(T.tab[:].indirect(T.soff[:, 32 * h:32 * h + 20]), keep, T.bb[:, w], A.add),
-           [kn, "bb" + n, "soff_" + n], TAB, 320, SCAT)
+        for a, b in PIECES[h]:
+            cols = slice(320 * h + 16 * a, 320 * h + 16 * b)
+            VG(lambda e, a=a, b=b, cols=cols: e.tensor_tensor(T.tab[:].indirect(T.soff[:, 32 * h + a:32 * h + b]), T.eall[:, cols], T.bb[:, cols], A.add),
+               ["eall" + n, "bb" + n, "soff_" + n], TAB, 16 * (b - a), SCAT)
 
     for t in range(VI):
         fin, fw = "fin%d" % t, "fw%d" % t
-        V(lambda e, fw=fw: e.tensor_tensor(T.sk1[:], T[fw][:, 16, 0:8], T.cxh[:], A.add), [fw + "s", "cxh"], ["sk1"])
-        V(lambda e, fw=fw: e.tensor_tensor(T.sk[:, 0, :], T[fw][:, 16, 8:16], T.sk1[:], A.add), [fw + "s", "sk1"], ["sk"])
-        V(lambda e: e.tensor_scalar(T.sk[:, 1, :], T.sk[:, 0, :], 2047, None, A.bitwise_and), ["sk"], ["skc"])
-        V(lambda e: e.tensor_copy(T.lsts[:, 0::2], T.sk[:, 1, :]), ["skc"], ["lsts"])
-        V(lambda e: e.tensor_scalar(T.pp[:, :, 4], T.sk[:, 0, :], 11, 63, A.arith_shift_right, A.bitwise_and), ["sk"], both("pp", [0]))
-        V(lambda e: e.tensor_copy(T.cc[:, :, 0], T.sk[:, 1, :]), ["skc"], both("cc", [0]))
+        V(lambda e, fw=fw: e.tensor_copy(T.sk[:], T[fw][:, 8, 0:8]), [fw + "s"], ["sk"])
+        V(lambda e: e.tensor_copy(T.lsts[:, 0::2], T.sk[:]), ["sk"], ["lsts"])
+        V(lambda e, fw=fw: e.tensor_tensor(T.pp[:, :, 4], T[fw][:, 8, 8:16], T.cxh[:], A.add), [fw + "s", "cxh"], both("pp", [0]))
+        V(lambda e: e.tensor_copy(T.cc[:, :, 0], T.sk[:]), ["sk"], both("cc", [0]))
         for s in range(1, S + 1):
             for h in HS:
                 step(h, s, t)
@@ -541,6 +538,9 @@ def rank_program(g, core, T, topo):
                 for hs in EARLY:
                     if s == S - 1 and hs[-1] == h:
                         early(hs, t)
+                for hs in PARITY:
+                    if s == S - 1 and hs[-1] == h:
+                        parity(hs)
             if s == 1:
                 for y in range(16):
                     PEn(lambda e, y=y, fin=fin: e.matmul(T.pmis[:, 8:16], sel(y), T[fin][:, y::16], y == 0, y == 15),
@@ -552,7 +552,7 @@ def rank_program(g, core, T, topo):
             V(lambda e: e.tensor_reduce(T.zr[:], T.lp[:, 7::8], AxisListType.X, A.add), ["lp0", "lp1"], ["zr"])
             PEn(lambda e: e.matmul(T.pmis[:, 0:1], T.negf[:], T.zr[:], True, True), ["negf", "zr"], ["pmis"], 256)
             V(lambda e: e.tensor_tensor(T.zc[:, 0:1], T.zc[:, 0:1], T.pmis[:, 0:1], A.subtract), [], ["pmis", "zc"])
-            V(lambda e: e.tensor_scalar(T.zc[:, 1:2], T.zc[:, 0:1], 1, None, A.bitwise_and), ["zc"], ["zodd"])
+            V(lambda e: e.tensor_scalar(T.zc[:, 1:2], T.zc[:, 0:1], 6, 1, A.arith_shift_right, A.bitwise_and), ["zc"], ["zodd"])
             Sc(lambda e: e.activation(T.zm[:], T.zc[:, 1:2], AF.Copy, bias=-1.0), ["zodd"], ["zm"])
 
     for i, (q, a, b) in enumerate(OUT):

from concourse.mybir import AluOpType, AxisListType, ActivationFunctionType

A = AluOpType
AF = ActivationFunctionType
VI, S = 3, 5
NDUM = 640
SCRATCH = {}
for _n, _s, _d in (
        ("pkt tmpi tmpj", [128, 1024], "int32"), ("rtt", [128, 3072], "bfloat16"), ("tab", [128, 2048 + NDUM], "float32"),
        ("jci i144", [128, 144], "int32"), ("selb", [128, 144], "bfloat16"), ("jf", [128, 144], "float16"),
        ("tra trb", [128, 4, 32], "float16"),
        ("sri", [8, 128], "int32"), ("srb bo8", [8, 128], "bfloat16"),
        ("fout", [128, 128 * VI], "bfloat16"), ("fin0 fin1 fin2 oneb idb ide ido", [128, 128], "bfloat16"),
        ("fw0 fw1 fw2", [128, 9, 16], "float16"),
        ("pi yli", [128, 1], "int32"), ("ylf y64 g15 zr zm", [128, 1], "float32"),
        ("i80", [128, 80], "int32"), ("w1", [128, 80], "float32"),
        ("negf bon edec nid", [128, 128], "float32"), ("ms", [128, 256], "float16"),
        ("bonh nh", [128, 128], "float16"), ("half", [64, 320], "bfloat16"), ("nd", [64, 1024], "bfloat16"), ("ndi", [64, 256], "bfloat16"), ("cst", [64, 64], "bfloat16"), ("c64 ft0 ft1", [64, 128], "bfloat16"),
        ("km st lp zs zb ppf", [128, 64], "float32"), ("cep", [128, 8, 8], "float32"), ("pp", [128, 8, 10], "int32"),
        ("cod", [128, 72], "float32"), ("so", [128, 48], "float32"), ("yi", [128, 3], "int32"), ("ybf y5 y8", [128, 1], "float32"),
        ("l5i l8i", [128, 4], "int32"), ("l5 l8", [128, 4], "uint16"), ("soff cdl", [128, 64], "uint16"),
        ("eq cs m25", [128, 200], "float32"), ("m8a m8b", [128, 32], "float32"),
        ("dui dum cei ce pri", [128, 8, 5], "float32"), ("m5a sm tq pw ad", [128, 40], "float32"), ("w5", [128, 41], "float32"),
        ("cc", [128, 8, 5], "int32"), ("dd", [128, 40], "int32"), ("zc", [128, 2], "int32"),
        ("bsi cxh sk", [128, 8], "float32"), ("hz", [128, 2], "float32"),
        ("lbi", [128, 4], "int32"), ("lb lf0 lf1", [128, 4], "uint16"), ("lst0 lst1 fl dec", [128, 8], "uint16"),
        ("sch", [128, 128, S + 1], "int32"), ("eall hit bb", [128, NDUM], "float32"),
        ("lsts", [128, 16], "uint16"),
        ("ypt", [128, 1024], "float32"), ("eu0 eu1", [128, 64], "uint16"),
        ("fh0 fh1", [128, 320], "bfloat16"), ("rg0 rg1", [128, 1024], "bfloat16"),
        ("ab0 ab1", [128, 1024], "bfloat16")):
    for _m in _n.split():
        SCRATCH[_m] = ("sbuf", _s, _d)
for _m in "kp0 kp1 pd0 pd1 pd2 pd3 pmis".split():
    SCRATCH[_m] = ("psum", [128, 512], "float32")
SCRATCH["pft"] = ("psum", [128, 1024], "bfloat16")
SEMAPHORES = ("cv cs ct cg lpk0 lpk1 lrt0 lrt1 ljc ljw lsr lfx rw1 rw2 rf10 rf11 rf20 rf21 lsend oyf0 oyf1 "
              "oyp0 oyp1 oyp2 oyp3").split()
GATHERS = (("s", 0, 5), ("v", 5, 9), ("v", 9, 12), ("v", 12, 14), ("v", 14, 16))
OTHER = {(1, 0): (("s", 0, 4), ("v", 4, 8), ("s", 8, 12), ("v", 12, 16))}
BANKS = ((5, 9), (0, 5), (9, 12), (12, 16))
PERIOD = 2.0
PLACE = {"scan": 0.0, "row": 0.04, "court": 0.05, "lf": 0.43, "lst": 0.425, "fh": 0.45, "eu": 0.78, "turn": 0.52, "ft": 1.1,
         "pay": 0.51, "g0": 1.3, "g1": 1.0, "g2": 1.3, "g3": 2.02, "g4": 2.41,
         "n0": 1.2, "i0": 1.25, "n1": 1.3, "i1": 1.75, "n2": 1.5, "i2": 2.01, "n3": 1.99, "i3": 2.45,
         "a0": 1.7, "a1": 2.1, "a2": 2.6, "a3": 2.9, "m0": 2.44, "m1": 2.5, "m2": 2.95, "m3": 3.1}
CYC, GATH, SCAT, PE, LAG = 1.0e-3, 1.56, 3.8, 0.5e-3, 0.2
DEPTH, SLACK, ROUNDS, FREE = 1, 0.2, 8, True
PLACED = (2, 3, 4, 5)
EARLY = ((0,), (1,))
PARITY = ((0, 1),)
VIA_TENSOR = (0, 1)
OUT = (("v", 0, 256), ("s", 256, 576), ("s", 576, 832), ("s", 832, 1024))
PIECES = (((0, 10), (10, 20)), ((0, 20),))
ORDER = []


def plan(batch):
    n = len(batch)
    busy, late = [it[6] for it in batch], [it[7] for it in batch]
    w, rd, left = {}, {}, []
    succ = [[] for _ in batch]
    for i, it in enumerate(batch):
        p = {w[r] for r in it[2] if r in w}
        group = {w[x[1:]] for x in it[3] if x[0] == "+"}
        for x in it[3]:
            if x[0] != "+":
                p |= ({w[x]} if x in w else set()) | rd.get(x, set())
        for r in it[2]:
            rd.setdefault(r, set()).add(i)
        for x in it[3]:
            w[x.lstrip("+")] = i
            rd[x.lstrip("+")] = set()
        for j in p - {i}:
            succ[j].append((i, late[j] + LAG))
        for j in group - p:
            succ[j].append((i, busy[j]))
        left.append(len((p | group) - {i}))
    last, kept = {}, set()
    for i in sorted((i for i in range(n) if batch[i][8] is not None), key=lambda i: (batch[i][8], i)):
        q = batch[i][0]
        if q in last and i not in [j for j, d in succ[last[q]]]:
            if batch[i][8] >= 0:
                kept.add((last[q], i))
            succ[last[q]].append((i, busy[last[q]]))
            left[i] += 1
        last[q] = i
    topo, cnt = [i for i in range(n) if not left[i]], list(left)
    for i in topo:
        for j, _ in succ[i]:
            cnt[j] -= 1
            if not cnt[j]:
                topo.append(j)
    assert len(topo) == n
    prio = [0.0] * n
    for i in reversed(topo):
        prio[i] = max([late[i]] + [d + prio[j] for j, d in succ[i]])
    ready = {i: 0.0 for i in range(n) if not left[i]}
    free, order, seen, held = {}, [], [0.0] * n, {}
    before = [[] for _ in batch]
    for i in range(n):
        for j, d in succ[i]:
            before[j].append((i, d))

    def start(i):
        return max(free.get(batch[i][0], 0.0), ready[i], held.get(i, 0.0))

    def soon(j, depth):
        if j in ready:
            return start(j)
        if depth == 0:
            return 1e9
        return max([seen[j]] + [soon(p, depth - 1) + d for p, d in before[j] if not done[p]])
    done = [False] * n
    while ready:
        i = min(ready, key=lambda i: (round(start(i), 3), -prio[i], i))
        q, t = batch[i][0], start(i)
        near, edge = set(ready), set(ready)
        for _ in range(DEPTH):
            edge = {j for k in edge for j, d in succ[k]} - near
            near |= edge
        for j in near:
            if batch[j][0] == q and prio[j] > prio[i]:
                s = soon(j, DEPTH)
                if t < s < t + busy[i] and max(s + prio[j], s + busy[j] + prio[i]) < max(t + prio[i], t + busy[i] + prio[j]) - SLACK:
                    held[i] = max(held.get(i, 0.0), s + 1e-3)
        if held.get(i, 0.0) > t:
            continue
        del ready[i]
        done[i] = True
        free[q] = t + busy[i]
        order.append(i)
        for j, d in succ[i]:
            left[j] -= 1
            seen[j] = max(seen[j], t + d)
            if left[j] == 0:
                ready[j] = seen[j]

    def lay(order, links, back):
        at, used = [0.0] * n, {}
        for i in order:
            if back:
                t = max([late[i] - busy[i]] + [at[j] + busy[j] + d - busy[i] for j, d in links[i]])
            else:
                t = max([0.0] + [at[j] + d for j, d in links[i]])
            slots = used.setdefault(batch[i][0], [])
            k = bisect(slots, t)
            if k and slots[k - 1][1] > t:
                t = slots[k - 1][1]
            while k < len(slots) and slots[k][0] < t + busy[i] - 1e-9:
                t = slots[k][1]
                k += 1
            slots.insert(k, (t, t + busy[i]))
            at[i] = t
        return at
    if FREE:
        succ = [[(j, d) for j, d in succ[i] if (i, j) not in kept] for i in range(n)]
        before = [[(j, d) for j, d in before[i] if (j, i) not in kept] for i in range(n)]
    best = None
    for _ in range(ROUNDS):
        at = lay(order, before, False)
        end = max(at[i] + late[i] for i in range(n))
        order = sorted(order, key=lambda i: at[i])
        if best is None or end < best[0] - 1e-6:
            best = (end, order)
        at = lay(sorted(order[::-1], key=lambda i: -at[i] - busy[i]), succ, True)
        order = sorted(order, key=lambda i: -at[i] - busy[i])
    return best[1] if best else order


def bisect(slots, t):
    lo, hi = 0, len(slots)
    while lo < hi:
        mid = (lo + hi) // 2
        if slots[mid][0] <= t:
            lo = mid + 1
        else:
            hi = mid
    return lo


def make_flow(g, T):
    queues = {"v": g.vector, "s": g.scalar, "t": g.tensor, "g": g, "y": g.sync}
    know = {q: {} for q in queues}
    total, clocks, writer, readers = {}, {}, {}, {}
    batch = []

    def need(q, toks):
        worst = {}
        for sem, val in toks:
            if know[q].get(sem, 0) < val:
                worst[sem] = max(worst.get(sem, 0), val)
        for sem, val in sorted(worst.items()):
            if know[q].get(sem, 0) < val:
                queues[q].wait_ge(T.sem[sem], val)
                for k, n in clocks[(sem, val)].items():
                    know[q][k] = max(know[q].get(k, 0), n)

    def op(q, calls, reads, writes, dur, sem=None, inc=1, late=None, at=None):
        batch.append((q, calls, reads, writes, sem, inc, dur, dur if late is None else late, at))

    def issue(q, calls, reads, writes, sem, inc):
        if q[0] == "x":
            total[sem] = inc
            clocks[(sem, inc)] = {sem: inc}
            tok = (sem, inc)
        else:
            toks = [writer[r] for r in reads if r in writer]
            for w in writes:
                toks += ([writer[w]] if w in writer else []) + readers.get(w, [])
            writes = [w.lstrip("+") for w in writes]
            need(q, toks)
            name = sem or "c" + q
            for c in (calls if isinstance(calls, list) else [calls]):
                if name == "lsend":
                    c(queues[q])
                else:
                    c(queues[q]).then_inc(T.sem[name], inc)
                total[name] = total.get(name, 0) + inc
                clocks[(name, total[name])] = {**know[q], name: total[name]}
            tok = (name, total[name])
        for r in reads:
            readers.setdefault(r, []).append(tok)
        for w in writes:
            writer[w] = tok
            readers[w] = []

    def finish():
        if not ORDER:
            ORDER.extend(plan(batch))
        for i in ORDER:
            issue(*batch[i][:6])
        for sem, n in sorted(total.items()):
            if know["g"].get(sem, 0) < n:
                g.wait_ge(T.sem[sem], n)
    return op, finish


def rank_program(g, core, T, topo):
    rank = T.rank_of(core)
    if rank is None:
        return
    N = len(T.cores)
    op, finish = make_flow(g, T)
    flag = {"allow_small_or_imprecise_dtypes": True}
    HS = (0, 1)

    def V(fn, r, w, n=64, at=None):
        op("v", fn, r, w, max(64, n) * CYC, at=at)

    def Sc(fn, r, w, n=64, at=None):
        op("s", fn, r, w, 0.065 + max(64, n) * CYC, at=at)

    def VG(fn, r, w, n, rate=GATH, at=None):
        op("v", fn, r, w, 0.05 + rate * n * CYC, at=at)

    def SG(fn, r, w, n, at=None):
        op("s", fn, r, w, 0.065 + GATH * n * CYC, at=at)

    def G(fn, r, w, n):
        op("g", fn, r, w, 0.17 + 2 * n * CYC)

    def PEn(calls, r, w, n, at=None):
        op("t", calls, r, w, n * PE, at=at)

    def dma(q, dst, src, r, w, sem, late, at=None):
        op(q, lambda e: e.dma_start(dst, src), r, w, 0.05, sem, 16, late, at)

    def send(dst_ap, src_ap, r, t, sem, lands):
        dst = T.cores[(rank + t) % N]
        rid, pid = topo.addr(dst, core)
        op("g", lambda e: e.remote_dma(dst_ap, src_ap, T.sem[sem], T.sem.lsend, pid, rid, topo.mask(core, dst)),
           r, ["@" + sem], 0.3, "lsend", len(topo.engines(core, dst)), 0.3)
        op("x" + sem, None, ["@" + sem], lands, 3.0, sem, len(topo.engines(T.cores[(rank - t) % N], core)))

    dma("y", T.jci[:, 0:128], T.jc[:], [], ["jci"], "ljc", 1.2, -9)
    dma("s", T.jci[:, 128:144], T.jc[:, 0:16], [], ["jcw"], "ljw", 1.2, -9)
    dma("s", T.sri[:], T.sr[:], [], ["sri"], "lsr", 1.2, -8)
    dma("y", T.pkt[:, 0:512], T.pk[:, 0:512], [], ["pkt0"], "lpk0", 1.8, -8)
    dma("s", T.pkt[:, 512:1024], T.pk[:, 512:1024], [], ["pkt1"], "lpk1", 2.5, -7)
    dma("y", T.fin0[:], T.fx[:], [], ["fin00", "fin01"], "lfx", 2.6, -7)
    dma("y", T.rtt[:], T.rt[:], [], ["rtt"], "lrt0", 4.5, -6)

    G(lambda e: e.iota(T.pi[:], [[1, 1]], 0, 1), [], ["pi"], 1)
    G(lambda e: e.iota(T.i144[:], [[1, 144]], 0, 0), [], ["i144"], 144)
    V(lambda e: e.memset(T.negf[:], -1.0), [], ["negf"], 128)
    V(lambda e: e.memset(T.oneb[:], 1.0), [], ["oneb"], at=-9)
    V(lambda e: e.memset(T.ndi[:], -1.0), [], ["ndi"], 128, at=-8)
    G(lambda e: e.affine_select(T.bon[:], T.negf[:], [[-16, 8], [0, 16]], A.is_ge, 0.0, 0, 1), ["negf"], ["bon"], 128)
    G(lambda e: e.affine_select(T.bon[:], T.bon[:], [[16, 8], [0, 16]], A.is_ge, 0.0, 15, -1), [], ["bon"], 128)
    G(lambda e: e.affine_select(T.bo8[:], T.oneb[0:8, :], [[1, 8], [0, 16]], A.is_equal, 0.0, 0, -1), ["oneb"], ["bo8"], 128)
    G(lambda e: e.affine_select(T.idb[:], T.oneb[:], [[-1, 128]], A.is_equal, 0.0, 0, 1), ["oneb"], ["idb"], 128)
    G(lambda e: e.affine_select(T.ide[:], T.idb[:], [[0, 4], [-1, 2], [0, 16]], A.is_ge, 0.0, 0, 0), ["idb"], ["ide"], 128)
    G(lambda e: e.affine_select(T.ido[:], T.idb[:], [[0, 4], [1, 2], [0, 16]], A.is_ge, 0.0, -1, 0), ["idb"], ["ido"], 128)
    ND = ["nd%d" % b for b in range(4)]
    for b in range(4):
        G(lambda e, b=b: e.affine_select(T.nd[:, 256 * b:256 * b + 256], T.ndi[:], [[-1, 4], [-16, 4], [0, 16]],
                                         A.is_equal, 0.0, -4 * b, 1), ["ndi"], [ND[b]], 256)
    G(lambda e: e.iota(T.cst[0:32, :], [[1, 64]], 0, 0, **flag), [], ["cst0"], 64)
    V(lambda e: e.memset(T.cst[32:64, :], -7680.0), [], ["cst1"])
    V(lambda e: e.memset(T.c64[:], 64.0), [], ["c64"])
    V(lambda e: e.tensor_scalar(T.yli[:], T.pi[:], 15, None, A.bitwise_and), ["pi"], ["yli"])
    V(lambda e: e.tensor_copy(T.ylf[:], T.yli[:]), ["yli"], ["ylf"])
    V(lambda e: e.tensor_scalar(T.y64[:], T.yli[:], 64.0, None, A.mult), ["yli"], ["y64"])
    V(lambda e: e.tensor_scalar(T.g15[:], T.pi[:], T.ylf[:, 0:1], 15.0, A.subtract, A.add), ["pi", "ylf"], ["g15"])
    V(lambda e: e.tensor_scalar(T.selb[:], T.i144[:], T.g15[:, 0:1], 131072.0, A.is_equal, A.mult), ["i144", "g15"], ["sel"], 144)
    V(lambda e: e.memset(T.km[:], -1.0e9), [], ["km"])
    V(lambda e: e.memset(T.km[:, 0::16], 1.0e9), ["km"], ["km"])
    G(lambda e: e.iota(T.cxh[:], [[0, 2], [16, 4]], 0, 0, **flag), [], ["cxh"], 8)
    G(lambda e: e.iota(T.pp[:, :, 0:4], [[0, 32]], -1000, 0), [], ["ppad"], 32)
    G(lambda e: e.iota(T.tab[:, 2048:], [[0, NDUM]], 0, 0, **flag), [], ["tabd"], NDUM)

    def sel(y):
        return T.selb[:, 15 - y:143 - y]

    V(lambda e: e.tensor_scalar(T.i80[:], T.i144[:, 0:80], 79, None, A.bitwise_and), ["i144"], ["i80"], 80)
    V(lambda e: e.tensor_scalar(T.w1[:], T.i80[:], T.ylf[:, 0:1], None, A.is_equal), ["i80", "ylf"], ["w1"], 80)
    G(lambda e: e.iota(T.m25[:], [[0, 200]], 1, 0, **flag), [], ["m25"], 200)
    for n, width, cases, last in (("m5a", 5, 8, 0), ("m8a", 8, 4, 0)):
        G(lambda e, n=n, width=width, cases=cases, last=last: e.affine_select(
            T[n][:], T.m25[:, 0:width * cases], [[0, cases], [1, width]], A.is_gt, 0.0, -last, 0), ["m25"], [n], 40)
    for i in (4, 5):
        G(lambda e, i=i: e.iota(T.m25[:, i::25], [[0, 8]], -1000, 0, **flag), [], ["m25"], 8)
    G(lambda e: e.iota(T.m8b[:], [[0, 32]], 0, 0, **flag), [], ["m8b"], 32)
    G(lambda e: e.iota(T.m8b[:, 1::8], [[0, 4]], 64, 0, **flag), [], ["m8b"], 4)
    for n, size, value in (("eq", 200, 0), ("w5", 41, -1000), ("cep", 64, 0), ("dum", 40, 0),
                           ("cod", 72, 0), ("so", 48, 0)):
        G(lambda e, n=n, size=size, value=value: e.iota(T[n][:], [[0, size]], value, 0, **flag), [], [n + "0"], size)
    G(lambda e: e.iota(T.ad[:, 0::20], [[0, 2]], 0, 0, **flag), [], ["ad0"], 2)
    if VIA_TENSOR:
        G(lambda e: e.iota(T.half[:], [[0, 320]], 3, 0, **flag), [], ["half"], 320)
        Sc(lambda e: e.activation(T.half[:], T.half[:], AF.Copy, scale=0.125), [], ["half"], 320)
        Sc(lambda e: e.activation(T.bonh[:], T.bon[:], AF.Copy), ["bon"], ["bonh"], 128)
        G(lambda e: e.affine_select(T.nid[:], T.negf[:], [[-1, 128]], A.is_equal, 0.0, 0, 1), ["negf"], ["nid"], 128)
    G(lambda e: e.iota(T.zc[:, 0:1], [[0, 1]], 0, 0), [], ["zc"], 1)
    G(lambda e: e.iota(T.zm[:], [[0, 1]], -1, 0, **flag), [], ["zm"], 1)
    G(lambda e: e.iota(T.dui[:], [[80, 8], [16, 5]], 2048, 0, **flag), [], ["dui"], 40)
    G(lambda e: e.iota(T.cei[:], [[0, 2], [-16, 4], [-64, 5]], 319, 0, **flag), [], ["cei"], 40)
    G(lambda e: e.iota(T.l5i[:], [[20, 2], [4, 2]], 0, 0), [], ["l5i"], 4)
    G(lambda e: e.iota(T.l8i[:], [[32, 2], [4, 2]], 3, 0), [], ["l8i"], 4)
    V(lambda e: e.tensor_scalar(T.yi[:, 0:1], T.pi[:], 3, None, A.bitwise_and), ["pi"], ["ya"])
    V(lambda e: e.tensor_scalar(T.yi[:, 1:2], T.pi[:], 2, 3, A.arith_shift_right, A.bitwise_and), ["pi"], ["yb"])
    Sc(lambda e: e.activation(T.ybf[:], T.yi[:, 1:2], AF.Copy), ["yb"], ["ybf"])
    for n, k in (("5", 5.0), ("8", 8.0)):
        Sc(lambda e, n=n, k=k: e.activation(T["y" + n][:], T.yi[:, 0:1], AF.Identity, bias=T.ybf[:, 0:1], scale=k), ["ya", "ybf"], ["y" + n])
        V(lambda e, n=n: e.tensor_scalar(T["l" + n][:], T["l%si" % n][:], T["y" + n][:, 0:1], None, A.add), ["l%si" % n, "y" + n], ["l" + n])
    G(lambda e: e.iota(T.bsi[:], [[0, 2], [-16, 4]], -1, 0, **flag), [], ["bsi"], 8)
    G(lambda e: e.iota(T.lbi[:], [[10, 4]], 4, 0), [], ["lbi"], 4)
    Sc(lambda e: e.activation(T.dum[:, :, 1:5], T.dui[:, :, 1:5], AF.Identity, bias=T.ylf[:, 0:1]), ["dui", "ylf", "dum0"], ["dum"])
    V(lambda e: e.tensor_scalar(T.ce[:], T.cei[:], T.ylf[:, 0:1], 1.0 / 512, A.subtract, A.mult), ["cei", "ylf"], ["ce"])
    V(lambda e: e.tensor_scalar(T.eq[:, 4::25], T.bsi[:], T.ylf[:, 0:1], 1.0 / 64, A.subtract, A.mult), ["bsi", "ylf", "eq0"], ["eq5"])
    V(lambda e: e.tensor_scalar(T.hz[:, 0:1], T.ylf[:], 8.0, 5.0, A.is_ge, A.mult), ["ylf"], ["h8"])
    V(lambda e: e.tensor_scalar(T.yi[:, 2:3], T.pi[:], 7, None, A.bitwise_and), ["pi"], ["y8i"])
    V(lambda e: e.tensor_scalar(T.hz[:, 1:2], T.yi[:, 2:3], 0.0, 40.0, A.is_equal, A.mult), ["y8i"], ["z40"])
    V(lambda e: e.tensor_scalar(T.lb[:], T.lbi[:], T.hz[:, 0:1], T.hz[:, 1:2], A.add, A.max), ["lbi", "h8", "z40"], ["lb"])

    V(lambda e: e.tensor_copy(T.jf[:], T.jci[:]), ["jci", "jcw"], ["jf"], 144, at=-5)
    V(lambda e: e.transpose(T.tra[:], T.jf[:, 0:128]), ["jf"], ["tra"])
    V(lambda e: e.transpose(T.trb[:], T.jf[:, 16:144]), ["jf"], ["trb"])
    PEn([lambda e: e.matmul(T.pd0[:, 0:64], T.ide[:], T.tra[:, :, 0:16], True, False),
         lambda e: e.matmul(T.pd0[:, 16:64], T.ido[:], T.trb[:, 0:3, 16:32], False, False),
         lambda e: e.matmul(T.pd0[:, 0:16], T.ido[:], T.trb[:, 3, 16:32], False, True),
         lambda e: e.matmul(T.pd0[:, 64:128], T.ide[:], T.trb[:, :, 0:16], True, False),
         lambda e: e.matmul(T.pd0[:, 64:128], T.ido[:], T.tra[:, :, 16:32], False, True)], ["ide", "ido", "tra", "trb"], ["pd0"], 320)
    Sc(lambda e: e.activation(T.fw0[:, 0:8:2, :], T.pd0[:, 0:64], AF.Copy), [], ["pd0", "fw0a"])
    Sc(lambda e: e.activation(T.fw0[:, 1:8:2, :], T.pd0[:, 64:128], AF.Copy), [], ["pd0", "fw0b"])
    Sc(lambda e: e.activation(T.srb[:], T.sri[:], AF.Copy), ["sri"], ["srb"], 128)
    for bank in ("pmis", "pd2"):
        PEn(lambda e, bank=bank: e.matmul(T[bank][:, 0:128], T.bo8[:], T.srb[:], True, True), ["bo8", "srb"], [bank], 128)
    Sc(lambda e: e.activation(T.ms[:, 128:256], T.pd2[:, 0:128], AF.Copy, scale=1.0 / 16), [], ["pd2", "ms1"], 128)
    V(lambda e: e.tensor_scalar(T.pmis[:, 128:256], T.pmis[:, 0:128], T.ylf[:, 0:1], None, A.is_equal), ["ylf"], ["pmis"], 128, at=-4.65)
    V(lambda e: e.tensor_tensor(T.ms[:, 0:128], T.pmis[:, 128:256], T.jf[:, 0:128], A.mult), ["jf"], ["pmis", "ms0"], 128, at=-4.55)
    PEn([lambda e, y=y: e.matmul(T.pd1[:, 0:16], sel(y), T.ms[:, y::16], y == 0, y == 15) for y in range(16)],
        ["sel", "ms0", "ms1"], ["pd1"], 1024)
    Sc(lambda e: e.activation(T.fw0[:, 8, :], T.pd1[:, 0:16], AF.Copy, scale=1.0 / 131072.0), [], ["pd1", "fw0s"])
    for t in (1, 2):
        send(T["fw%d" % t][:], T.fw0[:], ["fw0a", "fw0b", "fw0s"], t, "rw%d" % t, ["fw%d%s" % (t, x) for x in "abs"])
    TAB = ["tabd"] + ["tab%d%d" % (i, j) for i in range(2) for j in range(2)]
    for i in range(2):
        a, b = 512 * i, 512 * i + 512
        V(lambda e, a=a, b=b: e.tensor_scalar(T.tmpi[:, a:b], T.pkt[:, a:b], 4095, None, A.bitwise_and), ["pkt%d" % i], ["tmpi%d" % i], 512,
          at=(-4.7, -4.3)[i])
        V(lambda e, a=a, b=b: e.tensor_scalar(T.tmpj[:, a:b], T.pkt[:, a:b], 12, None, A.arith_shift_right), ["pkt%d" % i], ["tmpj%d" % i], 512,
          at=(-4.5, -4.2)[i])
        Sc(lambda e, a=a, b=b: e.activation(T.tab[:, a:b], T.tmpi[:, a:b], AF.Copy), ["tmpi%d" % i], ["tab%d0" % i], 512)
        if i == 0:
            Sc(lambda e, a=a, b=b: e.activation(T.tab[:, 1024 + a:1024 + b], T.tmpj[:, a:b], AF.Copy), ["tmpj0"], ["tab01"], 512)
        else:
            V(lambda e, a=a, b=b: e.tensor_copy(T.tab[:, 1024 + a:1024 + b], T.tmpj[:, a:b]), ["tmpj1"], ["tab11"], 512)

    def place(t, s, h):
        base = 100.0 * t + PERIOD * (2 * s + h)
        return lambda name: base + PLACE[name] if s + 1 in PLACED else None

    def choice(h, s, t):
        c, at = slice(4 * h, 4 * h + 4), place(t, s, h)
        key, sch = T.sch[:, 64 * h + 15:64 * h + 64:16, s], "sch%d%d" % (s, h)
        row, rn = T.pp[:, c, s + 4], "pp%d%d" % (s, h)
        V(lambda e: e.tensor_scalar(row, key, 11, 63, A.arith_shift_right, A.bitwise_and), [sch], [rn], at=at("row"))
        if s < S:
            V(lambda e: e.tensor_scalar(T.cc[:, c, s], key, 2047, None, A.bitwise_and), [sch], ["cc%d%d" % (s, h)], at=at("court"))
            V(lambda e: e.tensor_copy(T["lst%d" % h][:, 0::2], T.cc[:, c, s]), ["cc%d%d" % (s, h)], ["lst%d" % h], at=at("lst"))
        V(lambda e: e.tensor_scalar(T["lf%d" % h][:], row, T.y64[:, 0:1], None, A.add), [rn, "y64"], ["lf%d" % h], at=at("lf"))
        SG(lambda e: e.activation(T["fh%d" % h][:, 64 * s - 64:64 * s], T["ab%d" % h][:].indirect(T["lf%d" % h][:]), AF.Copy),
           ["lf%d" % h] + ["ab%d_%d" % (h, y) for y in range(16)], ["fh%d_%d" % (h, s)], 64, at=at("fh"))

    def step(h, s, t):
        eu, rg, ab, kp, ft, fw = "eu%d" % h, "rg%d" % h, "ab%d" % h, "kp%d" % h, "ft%d" % h, "fw%d" % t
        c, at = slice(4 * h, 4 * h + 4), place(t, s - 1, h)
        ln, lo = ("lst%d" % h, 0) if s > 1 else ("lsts", 8 * h)
        op("v", [lambda e, i=i: e.tensor_copy(T[eu][:, i::4], T.tab[:, 0:2048].indirect(T[ln][:, lo + 2 * i:lo + 2 * i + 1])) for i in range(4)],
           TAB[1:] + [ln], [eu], 4 * (0.05 + GATH * 16 * CYC), at=at("eu"))
        src, sn = (T["fin%d" % t][:, 64 * h:64 * h + 64], "fin%d%d" % (t, h)) if s == 1 else (
            T["fh%d" % h][:, 64 * s - 128:64 * s - 64], "fh%d_%d" % (h, s - 1))
        PEn(lambda e: e.transpose(T.pft[0:64, 0:128], src, T.idb[:]), [sn, "idb"], ["pft"], 128, at=at("turn"))
        V(lambda e: e.tensor_copy(T[ft][:], T.pft[0:64, 0:128]), [], ["pft", ft], at=at("ft"))
        PEn([lambda e: e.matmul(T[kp][:, 0:64], T.c64[:], T.cst[:], True, False),
             lambda e: e.matmul(T[kp][:, 0:64], T.idb[:], T[fw][:, 4 * h:4 * h + 4, :], False, False)],
            ["c64", "cst0", "cst1", "idb", fw + "a", fw + "b"], [kp], 128, at=at("pay"))
        for i, (q, y0, y1) in enumerate(OTHER.get((s, h), GATHERS)):
            col, lst, rk = slice(64 * y0, 64 * y1), T[eu][:, 4 * y0:4 * y1], [rg + "_%d" % y for y in range(y0, y1)]
            if q == "s":
                SG(lambda e, col=col, lst=lst: e.activation(T[rg][:, col], T.rtt[:].indirect(lst), AF.Copy), ["rtt", eu], rk,
                   64 * (y1 - y0), at=at("g%d" % i))
            else:
                VG(lambda e, col=col, lst=lst: e.tensor_copy(T[rg][:, col], T.rtt[:].indirect(lst)), ["rtt", eu], rk,
                   64 * (y1 - y0), at=at("g%d" % i))
        for b, (y0, y1) in enumerate(BANKS):
            col, pd, n, keys = slice(64 * y0, 64 * y1), "pd%d" % b, 64 * (y1 - y0), range(y0, y1)
            rk, ak = [rg + "_%d" % y for y in keys], [ab + "_%d" % y for y in keys]
            PEn(lambda e, col=col, pd=pd, n=n: e.matmul(T[pd][:, 0:n], T[ft][:], T.nd[:, col], True, False), [ft] + ND[y0 // 4:(y1 + 3) // 4], [pd], n,
                at=at("n%d" % b))
            PEn(lambda e, col=col, pd=pd, n=n: e.matmul(T[pd][:, 0:n], T.idb[:], T[rg][:, col], False, True), ["idb"] + rk, ["+" + pd], n,
                at=at("i%d" % b))
            Sc(lambda e, col=col, pd=pd, n=n: e.activation(T[ab][:, col], T[pd][:, 0:n], AF.Abs), [], [pd] + ak, n, at=at("a%d" % b))
            PEn([lambda e, y=y: e.matmul(T[kp][:, 0:64], sel(y), T[ab][:, 64 * y:64 * y + 64], False, y == BANKS[-1][1] - 1)
                 for y in keys], ["sel"] + ak, ["+" + kp], n, at=at("m%d" % b))
        V(lambda e: e.tensor_tensor_scan(T.sch[:, 64 * h:64 * h + 64, s], T.km[:], T[kp][:, 0:64], 0.0, A.max, A.min), ["km"], [kp, "sch%d%d" % (s, h)],
          at=place(t, s, h)("scan"))

    def both(name, steps):
        return ["%s%d%d" % (name, s, h) for s in steps for h in HS]

    def early(hs, t):
        a, b = 4 * hs[0], 4 * hs[-1] + 4
        c, m = slice(a, b), b - a

        def nm(*names):
            return [x + "_%d" % h for x in names for h in hs]

        def steps(name, r):
            return ["%s%d%d" % (name, s, h) for s in r for h in hs]
        PP = steps("pp", range(S)) + ["ppad"]
        c5, cc = slice(5 * a, 5 * b), T.cs[:, 25 * a + 4:25 * b:5]
        for d in range(1, 5):
            V(lambda e, d=d: e.tensor_tensor(T.eq[:, 25 * a + d - 1:25 * b:5], T.pp[:, c, 4:9], T.pp[:, c, 4 - d:9 - d], A.is_equal),
              PP + ["eq0"], nm("eq%d" % d), 10 * m)
        V(lambda e: e.tensor_tensor_scan(T.cs[:, 25 * a:25 * b], T.m25[:, 0:25 * m], T.eq[:, 25 * a:25 * b], 0.0, A.min, A.max),
          ["m25", "eq5"] + nm("eq1", "eq2", "eq3", "eq4"), nm("cs"), 25 * m)
        V(lambda e: e.tensor_tensor(T.tq[:, c5], cc, T.dum[:, c], A.mult), nm("cs") + ["dum"], nm("tq"), 10 * m)
        V(lambda e: e.tensor_tensor(T.so[:, c5], T.tq[:, c5], T.cc[:, c], A.max), nm("tq") + ["so0"] + steps("cc", range(S)), ["so"], 10 * m)
        VG(lambda e: e.tensor_copy(T.soff[:, 8 * a:8 * b], T.so[:].indirect(T.l5[:, a // 2:b // 2])), ["so", "l5"], nm("soff"), 8 * m)
        for h in hs:
            SG(lambda e, h=h: e.activation(T.eall[:, 320 * h:320 * h + 320], T.tab[:].indirect(T.soff[:, 32 * h:32 * h + 20]), AF.Copy),
               TAB + ["soff_%d" % h], ["eall%d" % h], 320)
        V(lambda e: e.tensor_tensor_scan(T.sm[:, c5], T.m5a[:, 0:5 * m], cc, 0.0, A.mult, A.add), ["m5a"] + nm("cs"), nm("sm"))
        V(lambda e: e.tensor_scalar(T.fl[:, c], T.sm[:, 5 * a + 4:5 * b:5], -64.0, 255.0, A.mult, A.add), nm("sm"), nm("fl"))
        Sc(lambda e: e.activation(T.cep[:, c, 0], T.sm[:, 5 * a + 4:5 * b:5], AF.Copy, scale=0.125, bias=0.125), nm("sm") + ["cep0"], nm("ceps"))
        Sc(lambda e: e.activation(T.ppf[:, 8 * a:8 * b], T.pp[:, c, 1:9], AF.Copy), PP, nm("ppf"))

    def parity(hs):
        a, b = 4 * hs[0], 4 * hs[-1] + 4
        c, m, c5 = slice(a, b), b - a, slice(5 * a, 5 * b)

        def nm(*names):
            return [x + "_%d" % h for x in names for h in hs]

        def steps(name, r):
            return ["%s%d%d" % (name, s, h) for s in r for h in hs]
        V(lambda e: e.tensor_scalar(T.dd[:, c5], T.sch[:, 16 * a + 15:16 * b:16, 0:5], 17, 1, A.arith_shift_right, A.bitwise_and),
          ["d0"] + steps("sch", range(1, S)), nm("dd"))
        V(lambda e: e.tensor_tensor(T.ad[:, 5 * a + 1:5 * b], T.dd[:, 5 * a + 1:5 * b], T.dd[:, 5 * a:5 * b - 1], A.not_equal),
          nm("dd") + ["ad0"], nm("ad"), 10 * m)
        Sc(lambda e: e.activation(T.pri[:, c], T.ad[:, c5], AF.Abs, bias=T.zm[:, 0:1]), nm("ad") + ["zm"], nm("pri"))
        V(lambda e: e.tensor_tensor(T.cep[:, c, 3:7], T.pri[:, c, 1:5], T.ce[:, c, 0:4], A.mult), nm("pri") + ["ce", "cep0"], nm("cep"))

    def late(h, t):
        c, n, w = slice(4 * h, 4 * h + 4), str(h), slice(320 * h, 320 * h + 320)
        x = slice(64 * h, 64 * h + 64)
        fout, fn = T.fout[:, 128 * t + 64 * h:128 * t + 64 * h + 64], "fout%d%d" % (t, h)
        SG(lambda e: e.activation(fout, T["fh" + n][:].indirect(T.fl[:, c]), AF.Copy),
           ["fl_" + n] + ["fh%d_%d" % (h, s) for s in range(1, S + 1)], [fn], 64)
        if t == VI - 1:
            dma("y", T.yf[:, x], fout, [fn], ["yf" + n], "oyf" + n, 1.5)
        else:
            send(T["fin%d" % (t + 1)][:, x], fout, [fn], 1, "rf%d%d" % (t + 1, h), ["fin%d%d" % (t + 1, h)])
        z = slice(32 * h, 32 * h + 32)
        c5, PP = slice(20 * h, 20 * h + 20), ["pp%d%d" % (s, h) for s in range(S + 1)] + ["ppad"]
        V(lambda e: e.tensor_tensor(T.pw[:, c5], T.pp[:, c, 5:10], T.tq[:, c5], A.subtract), PP + ["tq_" + n], ["pw" + n])
        V(lambda e: e.tensor_tensor_scan(T.w5[:, c5], T.cs[:, 100 * h + 4:100 * h + 100:5], T.pw[:, c5], 0.0, A.mult, A.max),
          ["pw" + n, "cs_" + n, "w50"], ["w5"])
        VG(lambda e: e.tensor_tensor(T.st[:, z], T.w5[:].indirect(T.lb[:, 2 * h:2 * h + 2]), T.ppf[:, z], A.not_equal),
           ["w5", "lb", "ppf_" + n], ["st" + n], 32)
        V(lambda e: e.tensor_tensor_scan(T.lp[:, z], T.m8b[:], T.st[:, z], 0.0, A.max, A.mult), ["m8b", "st" + n], ["lp" + n])
        V(lambda e: e.tensor_tensor(T.zb[:, z], T.cep[:, c], T.st[:, z], A.subtract), ["st" + n, "cep_" + n, "ceps_" + n], ["zb" + n])
        V(lambda e: e.tensor_tensor(T.cod[:, z], T.lp[:, z], T.pp[:, c, 2:10], A.max), ["lp" + n, "cod0"] + PP, ["cod"])
        V(lambda e: e.tensor_tensor_scan(T.zs[:, z], T.m8a[:], T.zb[:, z], 0.0, A.mult, A.max), ["m8a", "zb" + n], ["zs" + n])
        VG(lambda e: e.tensor_copy(T.cdl[:, z], T.cod[:].indirect(T.l8[:, 2 * h:2 * h + 2])), ["cod", "l8"], ["cdl" + n], 32)
        V(lambda e: e.tensor_scalar(T.dec[:, c], T.zs[:, 32 * h + 7:32 * h + 32:8], -512.0, 319.0, A.mult, A.add), ["zs" + n], ["dec" + n])
        cdl = T.cdl[:, 32 * h:32 * h + 20]
        pn = "kp" + n
        SG(lambda e: e.activation(T.hit[:, w], T.w1[:].indirect(cdl), AF.Copy), ["w1", "cdl" + n], ["hit" + n], 320)
        if h in VIA_TENSOR:
            PEn([lambda e: e.matmul(T[pn][:, 0:320], T.nid[:], T.eall[:, w], True, False),
                 lambda e: e.matmul(T[pn][:, 0:320], T.c64[:], T.half[:], False, False)], ["nid", "eall" + n, "c64", "half"], [pn], 1600)
            SG(lambda e: e.activation(T.edec[:, x], T.eall[:, w].indirect(T.dec[:, c]), AF.Copy, scale=-1.0, bias=1536.0),
               ["eall" + n, "dec" + n], ["edec" + n], 64)
            VG(lambda e: e.tensor_tensor(T.nh[:, x], T.hit[:, w].indirect(T.dec[:, c]), T.edec[:, x], A.mult),
               ["hit" + n, "dec" + n, "edec" + n], ["nh" + n], 64)
            PEn([lambda e, u=u: e.matmul(T[pn][:, 64 * u:64 * u + 64], T.bonh[:], T.nh[:, x], False, u == S - 1) for u in range(S)],
                ["bonh", "nh" + n], ["+" + pn], 320)
            V(lambda e: e.tensor_tensor(T.bb[:, w], T[pn][:, 0:320], T.hit[:, w], A.mult), ["hit" + n], [pn, "bb" + n], 320)
        for a, b in PIECES[h]:
            cols = slice(320 * h + 16 * a, 320 * h + 16 * b)
            VG(lambda e, a=a, b=b, cols=cols: e.tensor_tensor(T.tab[:].indirect(T.soff[:, 32 * h + a:32 * h + b]), T.eall[:, cols], T.bb[:, cols], A.add),
               ["eall" + n, "bb" + n, "soff_" + n], TAB, 16 * (b - a), SCAT)

    for t in range(VI):
        fin, fw = "fin%d" % t, "fw%d" % t
        V(lambda e, fw=fw: e.tensor_copy(T.sk[:], T[fw][:, 8, 0:8]), [fw + "s"], ["sk"])
        V(lambda e: e.tensor_copy(T.lsts[:, 0::2], T.sk[:]), ["sk"], ["lsts"])
        V(lambda e, fw=fw: e.tensor_tensor(T.pp[:, :, 4], T[fw][:, 8, 8:16], T.cxh[:], A.add), [fw + "s", "cxh"], both("pp", [0]))
        V(lambda e: e.tensor_copy(T.cc[:, :, 0], T.sk[:]), ["sk"], both("cc", [0]))
        for s in range(1, S + 1):
            for h in HS:
                step(h, s, t)
                choice(h, s, t)
                for hs in EARLY:
                    if s == S - 1 and hs[-1] == h:
                        early(hs, t)
                for hs in PARITY:
                    if s == S - 1 and hs[-1] == h:
                        parity(hs)
            if s == 1:
                for y in range(16):
                    PEn(lambda e, y=y, fin=fin: e.matmul(T.pmis[:, 8:16], sel(y), T[fin][:, y::16], y == 0, y == 15),
                        ["sel", fin + "0", fin + "1"], ["+pmis" if y else "pmis"], 64)
                V(lambda e: e.tensor_copy(T.sch[:, 15::16, 0], T.pmis[:, 8:16]), [], ["pmis", "d0"])
        for h in HS:
            late(h, t)
        if t < VI - 1:
            V(lambda e: e.tensor_reduce(T.zr[:], T.lp[:, 7::8], AxisListType.X, A.add), ["lp0", "lp1"], ["zr"])
            PEn(lambda e: e.matmul(T.pmis[:, 0:1], T.negf[:], T.zr[:], True, True), ["negf", "zr"], ["pmis"], 256)
            V(lambda e: e.tensor_tensor(T.zc[:, 0:1], T.zc[:, 0:1], T.pmis[:, 0:1], A.subtract), [], ["pmis", "zc"])
            V(lambda e: e.tensor_scalar(T.zc[:, 1:2], T.zc[:, 0:1], 6, 1, A.arith_shift_right, A.bitwise_and), ["zc"], ["zodd"])
            Sc(lambda e: e.activation(T.zm[:], T.zc[:, 1:2], AF.Copy, bias=-1.0), ["zodd"], ["zm"])

    for i, (q, a, b) in enumerate(OUT):
        pd, n = T["pd%d" % i][:, 0:b - a], "pd%d" % i
        if q == "s":
            Sc(lambda e, pd=pd, a=a, b=b: e.activation(pd, T.tab[:, 1024 + a:1024 + b], AF.Copy, scale=4096.0), TAB, [n], b - a)
        else:
            V(lambda e, pd=pd, a=a, b=b: e.tensor_scalar(pd, T.tab[:, 1024 + a:1024 + b], 4096.0, None, A.mult), TAB, [n], b - a)
        V(lambda e, pd=pd, a=a, b=b: e.tensor_tensor(T.ypt[:, a:b], pd, T.tab[:, a:b], A.add), TAB, [n, "ypt%d" % i], b - a)
        dma("y", T.yp[:, a:b], T.ypt[:, a:b], ["ypt%d" % i], ["yp%d" % i], "oyp%d" % i, 1.0 + (b - a) * 1.3e-3)
    finish()
